import numpy as np
import ml_dtypes


def mxq(x, axis, fmt="e4m3"):
    dtype, down = {"e4m3": (ml_dtypes.float8_e4m3fn, 7), "e5m2": (ml_dtypes.float8_e5m2, 14)}[fmt]
    v = np.moveaxis(np.asarray(x, np.float32).astype(ml_dtypes.bfloat16).astype(np.float64), axis, -1)
    blocks = v.reshape(v.shape[:-1] + (-1, 32))
    amax = np.abs(blocks).max(-1, keepdims=True)
    byte = np.maximum(np.where(amax > 0, np.frexp(amax)[1] - 1 + 127, 0) - down, 1)
    scale = np.exp2(byte - 127.0)
    codes = (blocks / scale).astype(np.float32).astype(dtype).astype(np.float64)
    return np.moveaxis((codes * scale).reshape(v.shape), -1, axis)


WIDE = False


def mx_kscale(k):
    if not WIDE:
        return np.ones(k)
    levels = np.array([30, -30])
    if k % 512:
        return np.exp2(np.random.permutation(np.resize(levels, k // 32))).repeat(32)
    a = np.empty((k // 512, 16))
    for p in range(k // 512):
        a[p, :8] = np.random.permutation(np.resize(levels, 8))
        for g in range(8):
            far = levels[np.abs(levels - a[p, g]) >= 10]
            a[p, g + 8] = far[np.random.randint(len(far))]
    return np.exp2(a.ravel()).repeat(32)


def f64(x):
    return np.asarray(x).astype(np.float64)


def striped(idx):
    return np.tile(idx.reshape(-1, 16).T, (8, 1)).astype(np.uint16)


def unstriped(offs):
    return offs[:16].T.reshape(-1).astype(np.int64)


def bf(x):
    return np.asarray(x, np.float32).astype(ml_dtypes.bfloat16)


E2M1 = np.array([0.0, 0.5, 1.0, 1.5, 2.0, 3.0, 4.0, 6.0, -0.0, -0.5, -1.0, -1.5, -2.0, -3.0, -4.0, -6.0])


def pack_weight(w, fmt):
    k, n = w.shape
    w = f64(bf(w)).reshape(k // 32, 32, n)
    amax = np.abs(w).max(1)
    if fmt in ("e4m3", "e5m2"):
        byte = np.frexp(amax)[1] - 1 + 127 - (7 if fmt == "e4m3" else 14)
    else:
        mant, ex = np.frexp(amax / 6.0)
        byte = np.where(mant > 0.5, ex, ex - 1) + 127
    byte = np.clip(np.where(amax > 0, byte, 1), 1, 254)
    scaled = (w * np.exp2(127.0 - byte)[:, None, :]).reshape(k, n).astype(np.float32)
    by_word = np.ascontiguousarray(scaled.reshape(k // 512, 128, 4, n).transpose(0, 1, 3, 2))
    if fmt in ("e4m3", "e5m2"):
        words = by_word.astype(ml_dtypes.float8_e4m3fn if fmt == "e4m3" else ml_dtypes.float8_e5m2).view(np.uint8)
    else:
        c = by_word.astype(ml_dtypes.float4_e2m1fn).view(np.uint8) & 0xF
        words = c[..., 0::2] | (c[..., 1::2] << 4)
    return np.ascontiguousarray(words), np.ascontiguousarray(byte.astype(np.uint8).reshape(k // 512, 16, n))


def unpack_weight(words, scales, fmt):
    g, p, n, _ = words.shape
    if fmt in ("e4m3", "e5m2"):
        vals = np.ascontiguousarray(words).view(ml_dtypes.float8_e4m3fn if fmt == "e4m3" else ml_dtypes.float8_e5m2).astype(np.float64)
    else:
        nib = np.empty((g, p, n, 4), np.uint8)
        nib[..., 0::2] = words & 0xF
        nib[..., 1::2] = words >> 4
        vals = E2M1[nib]
    vals = vals * np.repeat(np.exp2(scales.astype(np.float64) - 127.0), 8, axis=1)[..., None]
    return vals.transpose(0, 1, 3, 2).reshape(g * 512, n)


K, H, N, T, S, T2 = 1536, 1024, 512, 2048, 1024, 2048

def setup_inputs():
    n = np.random.standard_normal
    s = mx_kscale(K)[:, None]
    u = mx_kscale(H)[:, None]
    tab = n((K, T)) * np.exp(1.0 * n((1, T))) * s
    tab_words, tab_scales = pack_weight(tab, "e5m2")
    w1 = n((K, H)) / np.sqrt(K) / s * u.T
    w2 = n((H, N)) / np.sqrt(H) / u
    w2_words, w2_scales = pack_weight(w2, "e4m3")
    return {
        "tab_words": tab_words, "tab_scales": tab_scales,
        "offs": striped(np.random.permutation(T)[:S]),
        "offs2": striped(np.random.permutation(T2)[:S]),
        "w1": w1.astype(np.float32),
        "w2_words": w2_words, "w2_scales": w2_scales,
        "sT": (0.8 * n((H, T))).astype(np.float32),
        "src": (0.6 * n((N, S))).astype(np.float32),
        "wgo": np.exp(0.3 * n((128, S))).astype(np.float32),
    }

def reference(tab_words, tab_scales, offs, offs2, w1, w2_words, w2_scales, sT, src, wgo):
    v = unpack_weight(tab_words, tab_scales, "e5m2")[:, unstriped(offs)]
    shear = f64(sT)[:, unstriped(offs)]
    h = (mxq(f64(w1), 0, "e4m3").T @ v) / (1.0 + shear * shear)
    w2 = unpack_weight(w2_words, w2_scales, "e4m3")
    y = (w2.T @ mxq(h, 0, "e4m3")) - f64(src)
    out = np.zeros((N, T2))
    out[:, unstriped(offs2)] = np.tile(f64(wgo), (N // 128, 1)) * y
    return out

@@ -1,0 +1,237 @@
+from contextlib import ExitStack
+
+import concourse.mybir as mybir
+
+K, H, N, T, S, T2 = 1536, 1024, 512, 2048, 1024, 2048
+FLOPS = 2 * K * H * S + 2 * H * N * S
+
+F32 = mybir.dt.float32
+BF16 = mybir.dt.bfloat16
+I32 = mybir.dt.int32
+U32 = mybir.dt.uint32
+U16 = mybir.dt.uint16
+U8 = mybir.dt.uint8
+E4 = mybir.dt.float8_e4m3fn_x4
+E5 = mybir.dt.float8_e5m2_x4
+ACT = mybir.ActivationFunctionType
+ALU = mybir.AluOpType
+
+P = 128
+PACK = 4
+KP = P * PACK
+KA = K // KP
+HB = H // KP
+NT = N // P
+JH = 512
+HALVES = S // JH
+LC = JH // 16
+
+
+def tile_list_wall_model_adjoint_kernel(
+    tc, tab_words, tab_scales, offs, offs2, w1, w2_words, w2_scales, sT, src, wgo, out
+):
+    nc = tc.nc
+    with ExitStack() as ctx:
+        keep = ctx.enter_context(tc.tile_pool(name="keep", bufs=1))
+        stream = ctx.enter_context(tc.tile_pool(name="stream", bufs=10))
+        ring = ctx.enter_context(tc.tile_pool(name="ring", bufs=2))
+        psum_a = ctx.enter_context(tc.psum_pool(name="psum_a", bufs=6))
+        psum_y = ctx.enter_context(tc.psum_pool(name="psum_y", bufs=2))
+
+        idx = keep.tile([P, S // 16], U16, name="idx")
+        idx2 = keep.tile([P, S // 16], U16, name="idx2")
+        nc.sync.dma_start(idx[:], offs)
+
+        tab_sc = keep.tile([P, T], U8, name="tab_sc", align_bytes=64)
+        nc.vector.memset(tab_sc[:].bitcast(I32), 0)
+        for q in range(4):
+            nc.scalar.dma_start(
+                out=tab_sc[32 * q : 32 * q + 4 * KA, :].bitcast(I32),
+                in_=tab_scales[:, 4 * q : 4 * q + 4, :].bitcast(I32),
+            )
+        warm = keep.tile([P, 1], F32, name="warm")
+        nc.gpsimd.memset(warm[:], 1.0)
+        nc.scalar.activation(out=warm[:], in_=warm[:], func=ACT.Abs_reciprocal_sqrt)
+
+        w2_sc = keep.tile([P, N], U8, name="w2_sc", align_bytes=64)
+        nc.gpsimd.memset(w2_sc[:].bitcast(I32), 0)
+        v_sc = [keep.tile([P, S], U8, name=f"v_sc{a}", align_bytes=64) for a in range(KA)]
+        for a in range(1, KA):
+            nc.gpsimd.memset(v_sc[a][:].bitcast(I32), 0)
+        for q in range(4):
+            nc.gpsimd.dma_start(
+                out=w2_sc[32 * q : 32 * q + 4 * HB, :].bitcast(I32),
+                in_=w2_scales[:, 4 * q : 4 * q + 4, :].bitcast(I32),
+            )
+
+        pages = [keep.tile([P, T2], F32, name=f"page{m}") for m in range(NT)]
+        for m in range(NT):
+            nc.vector.memset(pages[m][:], 0.0)
+
+        v_words = [keep.tile([P, S], U32, name=f"v_words{a}", align_bytes=64) for a in range(KA)]
+        w1_words = {}
+        w1_sc = {}
+        for a in range(KA):
+            for b in range(HB):
+                w1_words[a, b] = keep.tile([P, KP], U32, name=f"w1_words{a}{b}", align_bytes=64)
+                w1_sc[a, b] = keep.tile([P, KP], U8, name=f"w1_sc{a}{b}", align_bytes=64)
+        damp = {}
+        h_rows = {}
+        h_words = {}
+        h_sc = {}
+        for b in range(HB):
+            for u in range(HALVES):
+                damp[b, u] = keep.tile([P, PACK, JH], F32, name=f"damp{b}{u}")
+                h_words[b, u] = keep.tile([P, JH], U32, name=f"h_words{b}{u}", align_bytes=64)
+                h_sc[b, u] = keep.tile([P, JH], U8, name=f"h_sc{b}{u}", align_bytes=64)
+        w2_w = keep.tile([P, HB, N], U32, name="w2_w", align_bytes=64)
+        wgo_sb = keep.tile([P, S], F32, name="wgo_sb")
+        src_sb = {}
+        shear_rows = sT.rearrange("(b p t) c -> b t p c", b=HB, t=PACK)
+
+        def gather_scales():
+            nc.vector.tensor_copy(out=v_sc[0][:], in_=tab_sc[:].indirect(idx[:]))
+            for a in range(1, KA):
+                nc.sync.dma_start(
+                    out=v_sc[a][0:112, :].bitcast(I32),
+                    in_=v_sc[0][4 * a : 4 * a + 112, :].bitcast(I32),
+                )
+
+        def table_pass(a):
+            window = stream.tile([P, T], U32, name="window", tag="slot")
+            nc.sync.dma_start(
+                out=window[:].bitcast(I32),
+                in_=tab_words[a].rearrange("p t i -> p (t i)").bitcast(I32),
+            )
+            nc.vector.tensor_copy(out=v_words[a][:], in_=window[:].indirect(idx[:]))
+
+        def weight_piece(a, b):
+            raw = stream.tile([P, PACK, KP], F32, name="raw", tag="slot")
+            nc.sync.dma_start(
+                out=raw[:],
+                in_=w1[KP * a : KP * (a + 1), KP * b : KP * (b + 1)].rearrange("(p i) c -> p i c", i=PACK),
+            )
+            grouped = ring.tile([P, PACK * KP], BF16, name="grouped", align_bytes=64)
+            nc.scalar.copy(
+                out=grouped[:].rearrange("p (t m i) -> p m i t", t=PACK, i=PACK),
+                in_=raw[:].rearrange("p i (m t) -> p m i t", t=PACK),
+            )
+            nc.vector.quantize_mx(out=w1_words[a, b][:].bitcast(E4), scales=w1_sc[a, b][:], in_=grouped[:])
+
+        def shear_tile(b, t):
+            window = stream.tile([P, T], F32, name="shear", tag="slot")
+            nc.sync.dma_start(out=window[:], in_=shear_rows[b, t])
+            for u in range(HALVES):
+                nc.vector.tensor_copy(
+                    out=damp[b, u][:, t, :], in_=window[:].indirect(idx[:, LC * u : LC * (u + 1)])
+                )
+
+        def damping(b, t, u):
+            d = damp[b, u][:, t, :]
+            nc.scalar.activation(out=d, in_=d, func=ACT.Square)
+            nc.scalar.activation(out=d, in_=d, func=ACT.Abs_reciprocal_sqrt, bias=1.0)
+            nc.scalar.activation(out=d, in_=d, func=ACT.Square)
+
+        def hidden_rows(b, t, u):
+            d = damp[b, u][:, t, :]
+            cols = slice(JH * u, JH * (u + 1))
+            acc = psum_a.tile([P, JH], F32, name="acc")
+            for a in range(KA):
+                nc.tensor.matmul_mx(
+                    out=acc[:],
+                    lhsT=w1_words[a, b][:, P * t : P * (t + 1)].bitcast(E4),
+                    lhsT_scale=w1_sc[a, b][:, P * t : P * (t + 1)],
+                    rhs=v_words[a][:, cols].bitcast(E5),
+                    rhs_scale=v_sc[a][:, cols],
+                    start=(a == 0),
+                    stop=(a == KA - 1),
+                )
+            if t == 0:
+                h_rows[b, u] = ring.tile([P, PACK, JH], BF16, name="h_rows", bufs=4)
+            nc.vector.tensor_tensor(out=h_rows[b, u][:, t, :], in0=acc[:], in1=d, op=ALU.mult)
+
+        def hidden_codes(b, u):
+            woven = ring.tile([P, JH * PACK], BF16, name="woven", align_bytes=64)
+            weave = nc.vector.tensor_copy if u == 0 else nc.scalar.copy
+            weave(
+                out=woven[:].rearrange("p (c i t) -> p c t i", i=4, t=PACK),
+                in_=h_rows[b, u][:].rearrange("p t (c i) -> p c t i", i=4),
+            )
+            nc.vector.quantize_mx(out=h_words[b, u][:].bitcast(E4), scales=h_sc[b, u][:], in_=woven[:])
+            return woven
+
+        def load_src(u):
+            src_sb[u] = stream.tile([P, NT, JH], F32, name="src_sb", tag="slot")
+            nc.sync.dma_start(
+                out=src_sb[u][:], in_=src[:, JH * u : JH * (u + 1)].rearrange("(m p) j -> p m j", p=P)
+            )
+
+        def result(m, u, diff):
+            y = psum_y.tile([P, JH], F32, name="y")
+            for b in range(HB):
+                nc.tensor.matmul_mx(
+                    out=y[:],
+                    lhsT=w2_w[:, b, P * m : P * (m + 1)].bitcast(E4),
+                    lhsT_scale=w2_sc[4 * b : P, P * m : P * (m + 1)],
+                    rhs=h_words[b, u][:].bitcast(E4),
+                    rhs_scale=h_sc[b, u][:],
+                    start=(b == 0),
+                    stop=(b == HB - 1),
+                )
+            nc.vector.tensor_tensor(out=diff, in0=y[:], in1=src_sb[u][:, m, :], op=ALU.subtract)
+            nc.vector.tensor_tensor(
+                out=pages[m][:].indirect(idx2[:, LC * u : LC * (u + 1)]),
+                in0=diff,
+                in1=wgo_sb[:, JH * u : JH * (u + 1)],
+                op=ALU.mult,
+            )
+
+        def shear_and_damping(b, t, halves):
+            shear_tile(b, t)
+            for u in halves:
+                damping(b, t, u)
+
+        shear_and_damping(0, 0, (0, 1))
+        gather_scales()
+        weight_piece(0, 0)
+        shear_and_damping(0, 1, (0, 1))
+        table_pass(0)
+        weight_piece(1, 0)
+        shear_and_damping(0, 2, (0, 1))
+        table_pass(1)
+        shear_and_damping(0, 3, (0, 1))
+        weight_piece(2, 0)
+        table_pass(2)
+        for a in range(KA):
+            weight_piece(a, 1)
+            shear_and_damping(1, a, (0,))
+            if a == 0:
+                for t in range(PACK):
+                    hidden_rows(0, t, 0)
+                hidden_codes(0, 0)
+            if a == 1:
+                for t in range(PACK):
+                    hidden_rows(0, t, 1)
+        shear_and_damping(1, PACK - 1, (0,))
+        nc.sync.dma_start(
+            out=w2_w[:].bitcast(I32), in_=w2_words.rearrange("b p c i -> p b (c i)").bitcast(I32)
+        )
+        nc.sync.dma_start(idx2[:], offs2)
+        load_src(0)
+        nc.sync.dma_start(out=wgo_sb[:], in_=wgo)
+        load_src(1)
+        for t in range(PACK):
+            hidden_rows(1, t, 0)
+        hidden_codes(1, 0)
+        result(0, 0, damp[1, 0][:, 0, :])
+        for t in range(PACK):
+            damping(1, t, 1)
+            hidden_rows(1, t, 1)
+        hidden_codes(0, 1)
+        result(1, 0, damp[1, 1][:, PACK - 1, :])
+        woven = hidden_codes(1, 1)
+        result(2, 0, woven[:].bitcast(F32)[:, 0:JH])
+        result(3, 0, damp[1, 0][:, 1, :])
+        for m in range(NT):
+            result(m, 1, damp[0, 0][:, m, :])
+            nc.sync.dma_start(out=out[P * m : P * (m + 1), :], in_=pages[m][:])

@@ -33,10 +33,9 @@ def tile_list_wall_model_adjoint_kernel(
     nc = tc.nc
     with ExitStack() as ctx:
         keep = ctx.enter_context(tc.tile_pool(name="keep", bufs=1))
-        stream = ctx.enter_context(tc.tile_pool(name="stream", bufs=10))
+        arena = ctx.enter_context(tc.tile_pool(name="arena", bufs=1))
         ring = ctx.enter_context(tc.tile_pool(name="ring", bufs=2))
-        psum_a = ctx.enter_context(tc.psum_pool(name="psum_a", bufs=6))
-        psum_y = ctx.enter_context(tc.psum_pool(name="psum_y", bufs=2))
+        psum = ctx.enter_context(tc.psum_pool(name="psum", bufs=8))
 
         idx = keep.tile([P, S // 16], U16, name="idx")
         idx2 = keep.tile([P, S // 16], U16, name="idx2")
@@ -58,11 +57,6 @@ def tile_list_wall_model_adjoint_kernel(
         v_sc = [keep.tile([P, S], U8, name=f"v_sc{a}", align_bytes=64) for a in range(KA)]
         for a in range(1, KA):
             nc.gpsimd.memset(v_sc[a][:].bitcast(I32), 0)
-        for q in range(4):
-            nc.gpsimd.dma_start(
-                out=w2_sc[32 * q : 32 * q + 4 * HB, :].bitcast(I32),
-                in_=w2_scales[:, 4 * q : 4 * q + 4, :].bitcast(I32),
-            )
 
         pages = [keep.tile([P, T2], F32, name=f"page{m}") for m in range(NT)]
         for m in range(NT):
@@ -73,8 +67,8 @@ def tile_list_wall_model_adjoint_kernel(
         w1_sc = {}
         for a in range(KA):
             for b in range(HB):
-                w1_words[a, b] = keep.tile([P, KP], U32, name=f"w1_words{a}{b}", align_bytes=64)
                 w1_sc[a, b] = keep.tile([P, KP], U8, name=f"w1_sc{a}{b}", align_bytes=64)
+        grouped_w = {}
         damp = {}
         h_rows = {}
         h_words = {}
@@ -84,6 +78,7 @@ def tile_list_wall_model_adjoint_kernel(
                 damp[b, u] = keep.tile([P, PACK, JH], F32, name=f"damp{b}{u}")
                 h_words[b, u] = keep.tile([P, JH], U32, name=f"h_words{b}{u}", align_bytes=64)
                 h_sc[b, u] = keep.tile([P, JH], U8, name=f"h_sc{b}{u}", align_bytes=64)
+        picked = dict(damp)
         w2_w = keep.tile([P, HB, N], U32, name="w2_w", align_bytes=64)
         wgo_sb = keep.tile([P, S], F32, name="wgo_sb")
         src_sb = {}
@@ -92,50 +87,66 @@ def tile_list_wall_model_adjoint_kernel(
         def gather_scales():
             nc.vector.tensor_copy(out=v_sc[0][:], in_=tab_sc[:].indirect(idx[:]))
             for a in range(1, KA):
-                nc.sync.dma_start(
+                nc.scalar.dma_start(
                     out=v_sc[a][0:112, :].bitcast(I32),
                     in_=v_sc[0][4 * a : 4 * a + 112, :].bitcast(I32),
                 )
 
-        def table_pass(a):
-            window = stream.tile([P, T], U32, name="window", tag="slot")
+        def table_pass(a, at):
+            window = arena.tile([P, T], U32, name=f"window{a}", offset=at, align_bytes=64)
             nc.sync.dma_start(
                 out=window[:].bitcast(I32),
                 in_=tab_words[a].rearrange("p t i -> p (t i)").bitcast(I32),
             )
-            nc.vector.tensor_copy(out=v_words[a][:], in_=window[:].indirect(idx[:]))
+            for u in range(HALVES):
+                nc.vector.tensor_copy(
+                    out=v_words[a][:, JH * u : JH * (u + 1)], in_=window[:].indirect(idx[:, LC * u : LC * (u + 1)])
+                )
 
-        def weight_piece(a, b):
-            raw = stream.tile([P, PACK, KP], F32, name="raw", tag="slot")
+        def weight_piece(a, b, cast, at):
+            raw = arena.tile([P, PACK, KP], F32, name=f"raw{a}{b}", offset=at, align_bytes=64)
             nc.sync.dma_start(
                 out=raw[:],
                 in_=w1[KP * a : KP * (a + 1), KP * b : KP * (b + 1)].rearrange("(p i) c -> p i c", i=PACK),
             )
-            grouped = ring.tile([P, PACK * KP], BF16, name="grouped", align_bytes=64)
-            nc.scalar.copy(
+            grouped = ring.tile([P, PACK * KP], BF16, name="grouped", align_bytes=64, bufs=3)
+            cast(
                 out=grouped[:].rearrange("p (t m i) -> p m i t", t=PACK, i=PACK),
                 in_=raw[:].rearrange("p i (m t) -> p m i t", t=PACK),
             )
-            nc.vector.quantize_mx(out=w1_words[a, b][:].bitcast(E4), scales=w1_sc[a, b][:], in_=grouped[:])
+            grouped_w[a, b] = grouped
 
-        def shear_tile(b, t):
-            window = stream.tile([P, T], F32, name="shear", tag="slot")
+        def weight_codes(a, b, at):
+            if at is None:
+                w1_words[a, b] = keep.tile([P, KP], U32, name=f"w1_words{a}{b}", align_bytes=64)
+            else:
+                w1_words[a, b] = arena.tile([P, KP], U32, name=f"w1_words{a}{b}", offset=at, align_bytes=64)
+            nc.vector.quantize_mx(out=w1_words[a, b][:].bitcast(E4), scales=w1_sc[a, b][:], in_=grouped_w[a, b][:])
+
+        def shear_tile(b, t, at):
+            window = arena.tile([P, T], F32, name=f"shear{b}{t}", offset=at, align_bytes=64)
             nc.sync.dma_start(out=window[:], in_=shear_rows[b, t])
             for u in range(HALVES):
                 nc.vector.tensor_copy(
-                    out=damp[b, u][:, t, :], in_=window[:].indirect(idx[:, LC * u : LC * (u + 1)])
+                    out=picked[b, u][:, t, :], in_=window[:].indirect(idx[:, LC * u : LC * (u + 1)])
                 )
 
         def damping(b, t, u):
             d = damp[b, u][:, t, :]
-            nc.scalar.activation(out=d, in_=d, func=ACT.Square)
+            nc.scalar.activation(out=d, in_=picked[b, u][:, t, :], func=ACT.Square)
             nc.scalar.activation(out=d, in_=d, func=ACT.Abs_reciprocal_sqrt, bias=1.0)
             nc.scalar.activation(out=d, in_=d, func=ACT.Square)
+
+        def late_damping(first):
+            d = damp[1, 0][:, first:PACK, :]
+            nc.scalar.activation(out=d, in_=picked[1, 1][:, first:PACK, :], func=ACT.Square)
+            nc.scalar.activation(out=d, in_=d, func=ACT.Abs_reciprocal_sqrt, bias=1.0)
+            nc.scalar.activation(out=picked[1, 1][:, first:PACK, :], in_=d, func=ACT.Square)
 
         def hidden_rows(b, t, u):
             d = damp[b, u][:, t, :]
             cols = slice(JH * u, JH * (u + 1))
-            acc = psum_a.tile([P, JH], F32, name="acc")
+            acc = psum.tile([P, JH], F32, name="acc", tag="bank")
             for a in range(KA):
                 nc.tensor.matmul_mx(
                     out=acc[:],
@@ -146,13 +157,16 @@ def tile_list_wall_model_adjoint_kernel(
                     start=(a == 0),
                     stop=(a == KA - 1),
                 )
-            if t == 0:
-                h_rows[b, u] = ring.tile([P, PACK, JH], BF16, name="h_rows", bufs=4)
             nc.vector.tensor_tensor(out=h_rows[b, u][:, t, :], in0=acc[:], in1=d, op=ALU.mult)
 
-        def hidden_codes(b, u):
-            woven = ring.tile([P, JH * PACK], BF16, name="woven", align_bytes=64)
-            weave = nc.vector.tensor_copy if u == 0 else nc.scalar.copy
+        def place_rows(b, u, at):
+            h_rows[b, u] = arena.tile([P, PACK, JH], BF16, name=f"h_rows{b}{u}", offset=at, align_bytes=64)
+
+        def hidden_codes(b, u, weave, at=None):
+            if at is None:
+                woven = ring.tile([P, JH * PACK], BF16, name="woven", align_bytes=64)
+            else:
+                woven = arena.tile([P, JH * PACK], BF16, name=f"woven{b}{u}", offset=at, align_bytes=64)
             weave(
                 out=woven[:].rearrange("p (c i t) -> p c t i", i=4, t=PACK),
                 in_=h_rows[b, u][:].rearrange("p t (c i) -> p c t i", i=4),
@@ -160,14 +174,14 @@ def tile_list_wall_model_adjoint_kernel(
             nc.vector.quantize_mx(out=h_words[b, u][:].bitcast(E4), scales=h_sc[b, u][:], in_=woven[:])
             return woven
 
-        def load_src(u):
-            src_sb[u] = stream.tile([P, NT, JH], F32, name="src_sb", tag="slot")
+        def load_src(u, at):
+            src_sb[u] = arena.tile([P, NT, JH], F32, name=f"src_sb{u}", offset=at, align_bytes=64)
             nc.sync.dma_start(
                 out=src_sb[u][:], in_=src[:, JH * u : JH * (u + 1)].rearrange("(m p) j -> p m j", p=P)
             )
 
         def result(m, u, diff):
-            y = psum_y.tile([P, JH], F32, name="y")
+            y = psum.tile([P, JH], F32, name="y", tag="bank")
             for b in range(HB):
                 nc.tensor.matmul_mx(
                     out=y[:],
@@ -186,52 +200,68 @@ def tile_list_wall_model_adjoint_kernel(
                 op=ALU.mult,
             )
 
-        def shear_and_damping(b, t, halves):
-            shear_tile(b, t)
+        def shear_and_damping(b, t, halves, at):
+            shear_tile(b, t, at)
             for u in halves:
                 damping(b, t, u)
 
-        shear_and_damping(0, 0, (0, 1))
+        shear_and_damping(0, 0, (0, 1), 0)
         gather_scales()
-        weight_piece(0, 0)
-        shear_and_damping(0, 1, (0, 1))
-        table_pass(0)
-        weight_piece(1, 0)
-        shear_and_damping(0, 2, (0, 1))
-        table_pass(1)
-        shear_and_damping(0, 3, (0, 1))
-        weight_piece(2, 0)
-        table_pass(2)
-        for a in range(KA):
-            weight_piece(a, 1)
-            shear_and_damping(1, a, (0,))
-            if a == 0:
-                for t in range(PACK):
-                    hidden_rows(0, t, 0)
-                hidden_codes(0, 0)
-            if a == 1:
-                for t in range(PACK):
-                    hidden_rows(0, t, 1)
-        shear_and_damping(1, PACK - 1, (0,))
+        weight_piece(0, 0, nc.scalar.copy, 8192)
+        shear_and_damping(0, 1, (0, 1), 16384)
+        table_pass(0, 24576)
+        weight_codes(0, 0, 24576)
+        weight_piece(1, 0, nc.scalar.copy, 32768)
+        shear_and_damping(0, 2, (0, 1), 40960)
+        table_pass(1, 49152)
+        weight_codes(1, 0, 49152)
+        weight_piece(2, 0, nc.scalar.copy, 57344)
+        shear_and_damping(0, 3, (0, 1), 65536)
+        weight_codes(2, 0, 65536)
+        table_pass(2, 73728)
+        place_rows(0, 0, 0)
+        place_rows(0, 1, 4096)
+        place_rows(1, 0, 16384)
+        place_rows(1, 1, 20480)
+        weight_piece(0, 1, nc.scalar.copy, 81920)
+        for t in range(PACK):
+            hidden_rows(0, t, 0)
+        for t in range(PACK):
+            hidden_rows(0, t, 1)
+        weight_codes(0, 1, None)
+        weight_piece(1, 1, nc.scalar.copy, 90112)
+        weight_codes(1, 1, None)
+        weight_piece(2, 1, nc.scalar.copy, 98304)
+        weight_codes(2, 1, None)
+        shear_and_damping(1, 0, (0, 1), 8192)
+        shear_and_damping(1, 1, (0, 1), 32768)
+        shear_and_damping(1, 2, (0,), 40960)
+        hidden_codes(0, 0, nc.scalar.copy, 98304)
+        shear_and_damping(1, 3, (0,), 57344)
         nc.sync.dma_start(
             out=w2_w[:].bitcast(I32), in_=w2_words.rearrange("b p c i -> p b (c i)").bitcast(I32)
         )
+        for q in range(4):
+            nc.sync.dma_start(
+                out=w2_sc[32 * q : 32 * q + 4 * HB, :].bitcast(I32),
+                in_=w2_scales[:, 4 * q : 4 * q + 4, :].bitcast(I32),
+            )
         nc.sync.dma_start(idx2[:], offs2)
-        load_src(0)
+        load_src(0, 73728)
         nc.sync.dma_start(out=wgo_sb[:], in_=wgo)
-        load_src(1)
+        load_src(1, 81920)
         for t in range(PACK):
             hidden_rows(1, t, 0)
-        hidden_codes(1, 0)
-        result(0, 0, damp[1, 0][:, 0, :])
+        hidden_codes(1, 0, nc.vector.tensor_copy)
+        hidden_codes(0, 1, nc.scalar.copy, 57344)
+        result(0, 0, damp[0, 0][:, 0, :])
+        result(1, 0, damp[0, 0][:, 1, :])
+        late_damping(2)
         for t in range(PACK):
-            damping(1, t, 1)
             hidden_rows(1, t, 1)
-        hidden_codes(0, 1)
-        result(1, 0, damp[1, 1][:, PACK - 1, :])
-        woven = hidden_codes(1, 1)
-        result(2, 0, woven[:].bitcast(F32)[:, 0:JH])
-        result(3, 0, damp[1, 0][:, 1, :])
+        result(2, 0, damp[1, 1][:, PACK - 2, :])
+        woven = hidden_codes(1, 1, nc.scalar.copy)
+        result(3, 0, woven[:].bitcast(F32)[:, 0:JH])
         for m in range(NT):
-            result(m, 1, damp[0, 0][:, m, :])
+            result(m, 1, damp[0, 1][:, m, :])
             nc.sync.dma_start(out=out[P * m : P * (m + 1), :], in_=pages[m][:])

@@ -1,6 +1,7 @@
 from contextlib import ExitStack
 
 import concourse.mybir as mybir
+from concourse.masks import make_identity
 
 K, H, N, T, S, T2 = 1536, 1024, 512, 2048, 1024, 2048
 FLOPS = 2 * K * H * S + 2 * H * N * S
@@ -58,9 +59,16 @@ def tile_list_wall_model_adjoint_kernel(
         for a in range(1, KA):
             nc.gpsimd.memset(v_sc[a][:].bitcast(I32), 0)
 
-        pages = [keep.tile([P, T2], F32, name=f"page{m}") for m in range(NT)]
-        for m in range(NT):
+        identity = keep.tile([P, P], F32, name="identity")
+        make_identity(nc, identity[:])
+        pages = {}
+        for m in range(2):
+            pages[m] = keep.tile([P, T2], F32, name=f"page{m}")
             nc.vector.memset(pages[m][:], 0.0)
+
+        def late_page(m, at):
+            pages[m] = arena.tile([P, T2], F32, name=f"page{m}", offset=at, align_bytes=64)
+            nc.gpsimd.memset(pages[m][:], 0.0)
 
         v_words = [keep.tile([P, S], U32, name=f"v_words{a}", align_bytes=64) for a in range(KA)]
         w1_words = {}
@@ -76,7 +84,6 @@ def tile_list_wall_model_adjoint_kernel(
         for b in range(HB):
             for u in range(HALVES):
                 damp[b, u] = keep.tile([P, PACK, JH], F32, name=f"damp{b}{u}")
-                h_words[b, u] = keep.tile([P, JH], U32, name=f"h_words{b}{u}", align_bytes=64)
                 h_sc[b, u] = keep.tile([P, JH], U8, name=f"h_sc{b}{u}", align_bytes=64)
         picked = dict(damp)
         w2_w = keep.tile([P, HB, N], U32, name="w2_w", align_bytes=64)
@@ -137,6 +144,15 @@ def tile_list_wall_model_adjoint_kernel(
             nc.scalar.activation(out=d, in_=d, func=ACT.Abs_reciprocal_sqrt, bias=1.0)
             nc.scalar.activation(out=d, in_=d, func=ACT.Square)
 
+        def damping_in_parts(b, t, u):
+            parts = [damp[b, u][:, t, JH // 2 * c : JH // 2 * (c + 1)] for c in range(2)]
+            for d in parts:
+                nc.scalar.activation(out=d, in_=d, func=ACT.Square)
+            for d in parts:
+                nc.scalar.activation(out=d, in_=d, func=ACT.Abs_reciprocal_sqrt, bias=1.0)
+            for d in parts:
+                nc.scalar.activation(out=d, in_=d, func=ACT.Square)
+
         def late_damping(first):
             d = damp[1, 0][:, first:PACK, :]
             nc.scalar.activation(out=d, in_=picked[1, 1][:, first:PACK, :], func=ACT.Square)
@@ -162,8 +178,14 @@ def tile_list_wall_model_adjoint_kernel(
         def place_rows(b, u, at):
             h_rows[b, u] = arena.tile([P, PACK, JH], BF16, name=f"h_rows{b}{u}", offset=at, align_bytes=64)
 
-        def hidden_codes(b, u, weave, at=None):
-            if at is None:
+        def hidden_codes(b, u, weave, at=None, codes_at=None):
+            if codes_at is None:
+                h_words[b, u] = keep.tile([P, JH], U32, name=f"h_words{b}{u}", align_bytes=64)
+            else:
+                h_words[b, u] = arena.tile([P, JH], U32, name=f"h_words{b}{u}", offset=codes_at, align_bytes=64)
+            if at == "spent":
+                woven = damp[1, 0][:, 0:2, :].rearrange("p t j -> p (t j)").bitcast(BF16)
+            elif at is None:
                 woven = ring.tile([P, JH * PACK], BF16, name="woven", align_bytes=64)
             else:
                 woven = arena.tile([P, JH * PACK], BF16, name=f"woven{b}{u}", offset=at, align_bytes=64)
@@ -200,10 +222,46 @@ def tile_list_wall_model_adjoint_kernel(
                 op=ALU.mult,
             )
 
+        def result_on_tensor(m, u, diff):
+            rows = slice(P * m, P * (m + 1))
+            src_t = psum.tile([P, JH], F32, name="src_t", tag="bank")
+            for c in range(JH // P):
+                nc.tensor.transpose(src_t[:, P * c : P * (c + 1)], src_sb[u][:, m, P * c : P * (c + 1)], identity[:])
+            nc.scalar.activation(out=src_sb[u][:, m, :], in_=src_t[:], func=ACT.Copy, scale=-1.0)
+            y_t = psum.tile([P, JH], F32, name="y_t", tag="bank")
+            for c in range(JH // P):
+                for b in range(HB):
+                    nc.tensor.matmul_mx(
+                        out=y_t[:, P * c : P * (c + 1)],
+                        lhsT=h_words[b, u][:, P * c : P * (c + 1)].bitcast(E4),
+                        lhsT_scale=h_sc[b, u][:, P * c : P * (c + 1)],
+                        rhs=w2_w[:, b, rows].bitcast(E4),
+                        rhs_scale=w2_sc[4 * b : P, rows],
+                        start=(b == 0),
+                        stop=(b == HB - 1),
+                    )
+            y_t_sb = ring.tile([P, JH], F32, name="y_t_sb")
+            nc.scalar.copy(out=y_t_sb[:], in_=y_t[:])
+            total = psum.tile([P, JH], F32, name="total", tag="bank")
+            for c in range(JH // P):
+                cols = slice(P * c, P * (c + 1))
+                nc.tensor.matmul(total[:, cols], src_sb[u][:, m, cols], identity[:], start=True, stop=False, is_transpose=True)
+                nc.tensor.matmul(total[:, cols], y_t_sb[:, cols], identity[:], start=False, stop=True, is_transpose=True)
+            nc.scalar.copy(out=diff, in_=total[:])
+            nc.vector.tensor_tensor(
+                out=pages[m][:].indirect(idx2[:, LC * u : LC * (u + 1)]),
+                in0=diff,
+                in1=wgo_sb[:, JH * u : JH * (u + 1)],
+                op=ALU.mult,
+            )
+
         def shear_and_damping(b, t, halves, at):
             shear_tile(b, t, at)
-            for u in halves:
-                damping(b, t, u)
+            if len(halves) == 1:
+                damping_in_parts(b, t, 0)
+            else:
+                for u in halves:
+                    damping(b, t, u)
 
         shear_and_damping(0, 0, (0, 1), 0)
         gather_scales()
@@ -211,18 +269,19 @@ def tile_list_wall_model_adjoint_kernel(
         shear_and_damping(0, 1, (0, 1), 16384)
         table_pass(0, 24576)
         weight_codes(0, 0, 24576)
-        weight_piece(1, 0, nc.scalar.copy, 32768)
+        weight_piece(1, 0, nc.vector.tensor_copy, 32768)
+        weight_codes(1, 0, None)
         shear_and_damping(0, 2, (0, 1), 40960)
         table_pass(1, 49152)
-        weight_codes(1, 0, 49152)
-        weight_piece(2, 0, nc.scalar.copy, 57344)
-        shear_and_damping(0, 3, (0, 1), 65536)
-        weight_codes(2, 0, 65536)
-        table_pass(2, 73728)
+        weight_piece(2, 0, nc.scalar.copy, 73728)
+        shear_and_damping(0, 3, (0, 1), 57344)
+        weight_codes(2, 0, 57344)
+        table_pass(2, 65536)
+        late_page(2, 61440)
+        late_page(3, 69632)
         place_rows(0, 0, 0)
         place_rows(0, 1, 4096)
-        place_rows(1, 0, 16384)
-        place_rows(1, 1, 20480)
+        place_rows(1, 1, 16384)
         weight_piece(0, 1, nc.scalar.copy, 81920)
         for t in range(PACK):
             hidden_rows(0, t, 0)
@@ -230,14 +289,15 @@ def tile_list_wall_model_adjoint_kernel(
             hidden_rows(0, t, 1)
         weight_codes(0, 1, None)
         weight_piece(1, 1, nc.scalar.copy, 90112)
-        weight_codes(1, 1, None)
         weight_piece(2, 1, nc.scalar.copy, 98304)
-        weight_codes(2, 1, None)
-        shear_and_damping(1, 0, (0, 1), 8192)
-        shear_and_damping(1, 1, (0, 1), 32768)
+        shear_and_damping(1, 0, (0,), 8192)
+        shear_and_damping(1, 1, (0,), 32768)
+        weight_codes(1, 1, 32768)
+        weight_codes(2, 1, 34816)
         shear_and_damping(1, 2, (0,), 40960)
-        hidden_codes(0, 0, nc.scalar.copy, 98304)
-        shear_and_damping(1, 3, (0,), 57344)
+        shear_and_damping(1, 3, (0,), 106496)
+        hidden_codes(0, 0, nc.scalar.copy, 98304, 106496)
+        place_rows(1, 0, 108544)
         nc.sync.dma_start(
             out=w2_w[:].bitcast(I32), in_=w2_words.rearrange("b p c i -> p b (c i)").bitcast(I32)
         )
@@ -247,21 +307,24 @@ def tile_list_wall_model_adjoint_kernel(
                 in_=w2_scales[:, 4 * q : 4 * q + 4, :].bitcast(I32),
             )
         nc.sync.dma_start(idx2[:], offs2)
-        load_src(0, 73728)
+        load_src(0, 81920)
         nc.sync.dma_start(out=wgo_sb[:], in_=wgo)
-        load_src(1, 81920)
+        load_src(1, 90112)
         for t in range(PACK):
             hidden_rows(1, t, 0)
-        hidden_codes(1, 0, nc.vector.tensor_copy)
-        hidden_codes(0, 1, nc.scalar.copy, 57344)
+        hidden_codes(1, 0, nc.vector.tensor_copy, None, None)
         result(0, 0, damp[0, 0][:, 0, :])
         result(1, 0, damp[0, 0][:, 1, :])
-        late_damping(2)
+        late_damping(0)
+        hidden_codes(0, 1, nc.scalar.copy, "spent")
         for t in range(PACK):
             hidden_rows(1, t, 1)
-        result(2, 0, damp[1, 1][:, PACK - 2, :])
         woven = hidden_codes(1, 1, nc.scalar.copy)
+        result(2, 0, damp[1, 1][:, PACK - 2, :])
         result(3, 0, woven[:].bitcast(F32)[:, 0:JH])
         for m in range(NT):
-            result(m, 1, damp[0, 1][:, m, :])
+            if m < 1:
+                result(m, 1, damp[0, 1][:, m, :])
+            else:
+                result_on_tensor(m, 1, damp[0, 1][:, m, :])
             nc.sync.dma_start(out=out[P * m : P * (m + 1), :], in_=pages[m][:])

@@ -62,7 +62,7 @@ def tile_list_wall_model_adjoint_kernel(
         identity = keep.tile([P, P], F32, name="identity")
         make_identity(nc, identity[:])
         pages = {}
-        for m in range(2):
+        for m in range(4):
             pages[m] = keep.tile([P, T2], F32, name=f"page{m}")
             nc.vector.memset(pages[m][:], 0.0)
 
@@ -269,16 +269,14 @@ def tile_list_wall_model_adjoint_kernel(
         shear_and_damping(0, 1, (0, 1), 16384)
         table_pass(0, 24576)
         weight_codes(0, 0, 24576)
-        weight_piece(1, 0, nc.vector.tensor_copy, 32768)
-        weight_codes(1, 0, None)
+        weight_piece(1, 0, nc.scalar.copy, 32768)
         shear_and_damping(0, 2, (0, 1), 40960)
         table_pass(1, 49152)
+        weight_codes(1, 0, 49152)
         weight_piece(2, 0, nc.scalar.copy, 73728)
         shear_and_damping(0, 3, (0, 1), 57344)
         weight_codes(2, 0, 57344)
         table_pass(2, 65536)
-        late_page(2, 61440)
-        late_page(3, 69632)
         place_rows(0, 0, 0)
         place_rows(0, 1, 4096)
         place_rows(1, 1, 16384)
@@ -295,9 +293,9 @@ def tile_list_wall_model_adjoint_kernel(
         weight_codes(1, 1, 32768)
         weight_codes(2, 1, 34816)
         shear_and_damping(1, 2, (0,), 40960)
-        shear_and_damping(1, 3, (0,), 106496)
-        hidden_codes(0, 0, nc.scalar.copy, 98304, 106496)
-        place_rows(1, 0, 108544)
+        shear_and_damping(1, 3, (0,), 73728)
+        hidden_codes(0, 0, nc.scalar.copy, 98304, 73728)
+        place_rows(1, 0, 75776)
         nc.sync.dma_start(
             out=w2_w[:].bitcast(I32), in_=w2_words.rearrange("b p c i -> p b (c i)").bitcast(I32)
         )
@@ -323,7 +321,7 @@ def tile_list_wall_model_adjoint_kernel(
         result(2, 0, damp[1, 1][:, PACK - 2, :])
         result(3, 0, woven[:].bitcast(F32)[:, 0:JH])
         for m in range(NT):
-            if m < 1:
+            if m < 2:
                 result(m, 1, damp[0, 1][:, m, :])
             else:
                 result_on_tensor(m, 1, damp[0, 1][:, m, :])

@@ -12,20 +12,32 @@ I32 = mybir.dt.int32
 U32 = mybir.dt.uint32
 U16 = mybir.dt.uint16
 U8 = mybir.dt.uint8
-E4 = mybir.dt.float8_e4m3fn_x4
-E5 = mybir.dt.float8_e5m2_x4
+E4M3 = mybir.dt.float8_e4m3fn_x4
+E5M2 = mybir.dt.float8_e5m2_x4
 ACT = mybir.ActivationFunctionType
 ALU = mybir.AluOpType
 
 P = 128
 PACK = 4
-KP = P * PACK
-KA = K // KP
-HB = H // KP
-NT = N // P
-JH = 512
-HALVES = S // JH
-LC = JH // 16
+PASS = P * PACK
+K_PASSES = K // PASS
+R_PASSES = H // PASS
+PAGES = N // P
+HALF = 512
+HALVES = S // HALF
+HALF_COLS = HALF // 16
+QUADRANT = 32
+MOVED_ROWS = 112
+RUN = 4
+
+SLOT = 8192
+ROWS_BYTES = PACK * HALF * 2
+WORDS_BYTES = PASS * 4
+
+SLOT_NAMES = (
+    "shear00", "w00", "shear01", "tab0", "w10", "shear02", "tab1",
+    "shear03", "shear11", "w20", "w01", "w11", "w21", "shear12",
+)
 
 
 def tile_list_wall_model_adjoint_kernel(
@@ -38,290 +50,289 @@ def tile_list_wall_model_adjoint_kernel(
         ring = ctx.enter_context(tc.tile_pool(name="ring", bufs=2))
         psum = ctx.enter_context(tc.psum_pool(name="psum", bufs=8))
 
+        at = {name: SLOT * i for i, name in enumerate(SLOT_NAMES)}
+        at["tab2"] = at["w10"]
+        at["shear10"] = at["w00"]
+        at["shear13"] = at["w20"]
+        at["src0"] = at["w01"]
+        at["src1"] = at["w11"]
+
+        def placed(shape, dtype, name, offset):
+            return arena.tile(shape, dtype, name=name, offset=offset, align_bytes=64)
+
+        def kept(shape, dtype, name):
+            return keep.tile(shape, dtype, name=name, align_bytes=64)
+
         idx = keep.tile([P, S // 16], U16, name="idx")
         idx2 = keep.tile([P, S // 16], U16, name="idx2")
         nc.sync.dma_start(idx[:], offs)
 
-        tab_sc = keep.tile([P, T], U8, name="tab_sc", align_bytes=64)
+        tab_sc = kept([P, T], U8, "tab_sc")
         nc.vector.memset(tab_sc[:].bitcast(I32), 0)
-        for q in range(4):
+        for q in range(P // QUADRANT):
             nc.scalar.dma_start(
-                out=tab_sc[32 * q : 32 * q + 4 * KA, :].bitcast(I32),
+                out=tab_sc[QUADRANT * q : QUADRANT * q + 4 * K_PASSES, :].bitcast(I32),
                 in_=tab_scales[:, 4 * q : 4 * q + 4, :].bitcast(I32),
             )
-        warm = keep.tile([P, 1], F32, name="warm")
-        nc.gpsimd.memset(warm[:], 1.0)
-        nc.scalar.activation(out=warm[:], in_=warm[:], func=ACT.Abs_reciprocal_sqrt)
 
-        w2_sc = keep.tile([P, N], U8, name="w2_sc", align_bytes=64)
+        pages = {}
+        for m, engine in enumerate((nc.vector, nc.gpsimd)):
+            pages[m] = keep.tile([P, T2], F32, name=f"page{m}")
+            engine.memset(pages[m][:], 0.0)
+
+        w2_sc = kept([P, N], U8, "w2_sc")
         nc.gpsimd.memset(w2_sc[:].bitcast(I32), 0)
-        v_sc = [keep.tile([P, S], U8, name=f"v_sc{a}", align_bytes=64) for a in range(KA)]
-        for a in range(1, KA):
+        v_sc = {}
+        for a in range(1, K_PASSES):
+            v_sc[a] = kept([P, S], U8, f"v_sc{a}")
             nc.gpsimd.memset(v_sc[a][:].bitcast(I32), 0)
 
         identity = keep.tile([P, P], F32, name="identity")
         make_identity(nc, identity[:])
-        pages = {}
-        for m in range(4):
-            pages[m] = keep.tile([P, T2], F32, name=f"page{m}")
-            nc.vector.memset(pages[m][:], 0.0)
 
-        def late_page(m, at):
-            pages[m] = arena.tile([P, T2], F32, name=f"page{m}", offset=at, align_bytes=64)
-            nc.gpsimd.memset(pages[m][:], 0.0)
-
-        v_words = [keep.tile([P, S], U32, name=f"v_words{a}", align_bytes=64) for a in range(KA)]
+        v_words = [kept([P, S], U32, f"v_words{a}") for a in range(K_PASSES)]
+        w1_rounded = {}
         w1_words = {}
         w1_sc = {}
-        for a in range(KA):
-            for b in range(HB):
-                w1_sc[a, b] = keep.tile([P, KP], U8, name=f"w1_sc{a}{b}", align_bytes=64)
-        grouped_w = {}
+        for a in range(K_PASSES):
+            for b in range(R_PASSES):
+                w1_sc[a, b] = kept([P, PASS], U8, f"w1_sc{a}{b}")
         damp = {}
         h_rows = {}
         h_words = {}
         h_sc = {}
-        for b in range(HB):
+        for b in range(R_PASSES):
             for u in range(HALVES):
-                damp[b, u] = keep.tile([P, PACK, JH], F32, name=f"damp{b}{u}")
-                h_sc[b, u] = keep.tile([P, JH], U8, name=f"h_sc{b}{u}", align_bytes=64)
-        picked = dict(damp)
-        w2_w = keep.tile([P, HB, N], U32, name="w2_w", align_bytes=64)
+                damp[b, u] = keep.tile([P, PACK, HALF], F32, name=f"damp{b}{u}")
+                h_sc[b, u] = kept([P, HALF], U8, f"h_sc{b}{u}")
+        w2_w = kept([P, R_PASSES, N], U32, "w2_w")
         wgo_sb = keep.tile([P, S], F32, name="wgo_sb")
         src_sb = {}
-        shear_rows = sT.rearrange("(b p t) c -> b t p c", b=HB, t=PACK)
+        shear_rows = sT.rearrange("(b p t) c -> b t p c", b=R_PASSES, t=PACK)
 
-        def gather_scales():
+        def half_of(offsets, u):
+            return offsets[:, HALF_COLS * u : HALF_COLS * (u + 1)]
+
+        def gather_scales(offset):
+            v_sc[0] = placed([P, S], U8, "v_sc0", offset)
             nc.vector.tensor_copy(out=v_sc[0][:], in_=tab_sc[:].indirect(idx[:]))
-            for a in range(1, KA):
+            for a in range(1, K_PASSES):
                 nc.scalar.dma_start(
-                    out=v_sc[a][0:112, :].bitcast(I32),
-                    in_=v_sc[0][4 * a : 4 * a + 112, :].bitcast(I32),
+                    out=v_sc[a][0:MOVED_ROWS, :].bitcast(I32),
+                    in_=v_sc[0][4 * a : 4 * a + MOVED_ROWS, :].bitcast(I32),
                 )
 
-        def table_pass(a, at):
-            window = arena.tile([P, T], U32, name=f"window{a}", offset=at, align_bytes=64)
+        def table_pass(a):
+            window = placed([P, T], U32, f"tab{a}", at[f"tab{a}"])
             nc.sync.dma_start(
                 out=window[:].bitcast(I32),
                 in_=tab_words[a].rearrange("p t i -> p (t i)").bitcast(I32),
             )
             for u in range(HALVES):
                 nc.vector.tensor_copy(
-                    out=v_words[a][:, JH * u : JH * (u + 1)], in_=window[:].indirect(idx[:, LC * u : LC * (u + 1)])
+                    out=v_words[a][:, HALF * u : HALF * (u + 1)], in_=window[:].indirect(half_of(idx, u))
                 )
 
-        def weight_piece(a, b, cast, at):
-            raw = arena.tile([P, PACK, KP], F32, name=f"raw{a}{b}", offset=at, align_bytes=64)
-            nc.sync.dma_start(
-                out=raw[:],
-                in_=w1[KP * a : KP * (a + 1), KP * b : KP * (b + 1)].rearrange("(p i) c -> p i c", i=PACK),
-            )
-            grouped = ring.tile([P, PACK * KP], BF16, name="grouped", align_bytes=64, bufs=3)
-            cast(
-                out=grouped[:].rearrange("p (t m i) -> p m i t", t=PACK, i=PACK),
+        def weight_piece(a, b, copy):
+            raw = placed([P, PACK, PASS], F32, f"w{a}{b}", at[f"w{a}{b}"])
+            piece = w1[PASS * a : PASS * (a + 1), PASS * b : PASS * (b + 1)]
+            nc.sync.dma_start(out=raw[:], in_=piece.rearrange("(p i) c -> p i c", i=PACK))
+            rounded = ring.tile([P, PACK * PASS], BF16, name="rounded", align_bytes=64, bufs=3)
+            copy(
+                out=rounded[:].rearrange("p (t m i) -> p m i t", t=PACK, i=PACK),
                 in_=raw[:].rearrange("p i (m t) -> p m i t", t=PACK),
             )
-            grouped_w[a, b] = grouped
+            w1_rounded[a, b] = rounded
 
-        def weight_codes(a, b, at):
-            if at is None:
-                w1_words[a, b] = keep.tile([P, KP], U32, name=f"w1_words{a}{b}", align_bytes=64)
-            else:
-                w1_words[a, b] = arena.tile([P, KP], U32, name=f"w1_words{a}{b}", offset=at, align_bytes=64)
-            nc.vector.quantize_mx(out=w1_words[a, b][:].bitcast(E4), scales=w1_sc[a, b][:], in_=grouped_w[a, b][:])
+        def weight_codes(a, b, words):
+            w1_words[a, b] = words
+            nc.vector.quantize_mx(out=words[:].bitcast(E4M3), scales=w1_sc[a, b][:], in_=w1_rounded[a, b][:])
 
-        def shear_tile(b, t, at):
-            window = arena.tile([P, T], F32, name=f"shear{b}{t}", offset=at, align_bytes=64)
+        def shear_tile(b, t):
+            window = placed([P, T], F32, f"shear{b}{t}", at[f"shear{b}{t}"])
             nc.sync.dma_start(out=window[:], in_=shear_rows[b, t])
             for u in range(HALVES):
-                nc.vector.tensor_copy(
-                    out=picked[b, u][:, t, :], in_=window[:].indirect(idx[:, LC * u : LC * (u + 1)])
-                )
+                nc.vector.tensor_copy(out=damp[b, u][:, t, :], in_=window[:].indirect(half_of(idx, u)))
 
-        def damping(b, t, u):
-            d = damp[b, u][:, t, :]
-            nc.scalar.activation(out=d, in_=picked[b, u][:, t, :], func=ACT.Square)
-            nc.scalar.activation(out=d, in_=d, func=ACT.Abs_reciprocal_sqrt, bias=1.0)
-            nc.scalar.activation(out=d, in_=d, func=ACT.Square)
+        def damping(shear, scratch):
+            nc.scalar.activation(out=scratch, in_=shear, func=ACT.Square)
+            nc.scalar.activation(out=scratch, in_=scratch, func=ACT.Abs_reciprocal_sqrt, bias=1.0)
+            nc.scalar.activation(out=shear, in_=scratch, func=ACT.Square)
 
-        def damping_in_parts(b, t, u):
-            parts = [damp[b, u][:, t, JH // 2 * c : JH // 2 * (c + 1)] for c in range(2)]
-            for d in parts:
-                nc.scalar.activation(out=d, in_=d, func=ACT.Square)
-            for d in parts:
-                nc.scalar.activation(out=d, in_=d, func=ACT.Abs_reciprocal_sqrt, bias=1.0)
-            for d in parts:
-                nc.scalar.activation(out=d, in_=d, func=ACT.Square)
+        def shear_both_halves(t):
+            shear_tile(0, t)
+            for u in range(HALVES):
+                damping(damp[0, u][:, t, :], damp[0, u][:, t, :])
 
-        def late_damping(first):
-            d = damp[1, 0][:, first:PACK, :]
-            nc.scalar.activation(out=d, in_=picked[1, 1][:, first:PACK, :], func=ACT.Square)
-            nc.scalar.activation(out=d, in_=d, func=ACT.Abs_reciprocal_sqrt, bias=1.0)
-            nc.scalar.activation(out=picked[1, 1][:, first:PACK, :], in_=d, func=ACT.Square)
+        def shear_first_half(t):
+            shear_tile(1, t)
+            parts = [damp[1, 0][:, t, HALF // 2 * c : HALF // 2 * (c + 1)] for c in range(2)]
+            for part in parts:
+                nc.scalar.activation(out=part, in_=part, func=ACT.Square)
+            for part in parts:
+                nc.scalar.activation(out=part, in_=part, func=ACT.Abs_reciprocal_sqrt, bias=1.0)
+            for part in parts:
+                nc.scalar.activation(out=part, in_=part, func=ACT.Square)
 
-        def hidden_rows(b, t, u):
-            d = damp[b, u][:, t, :]
-            cols = slice(JH * u, JH * (u + 1))
-            acc = psum.tile([P, JH], F32, name="acc", tag="bank")
-            for a in range(KA):
-                nc.tensor.matmul_mx(
-                    out=acc[:],
-                    lhsT=w1_words[a, b][:, P * t : P * (t + 1)].bitcast(E4),
-                    lhsT_scale=w1_sc[a, b][:, P * t : P * (t + 1)],
-                    rhs=v_words[a][:, cols].bitcast(E5),
-                    rhs_scale=v_sc[a][:, cols],
-                    start=(a == 0),
-                    stop=(a == KA - 1),
-                )
-            nc.vector.tensor_tensor(out=h_rows[b, u][:, t, :], in0=acc[:], in1=d, op=ALU.mult)
+        def hidden_rows(b, u):
+            cols = slice(HALF * u, HALF * (u + 1))
+            for t in range(PACK):
+                acc = psum.tile([P, HALF], F32, name="acc", tag="bank")
+                for a in range(K_PASSES):
+                    nc.tensor.matmul_mx(
+                        out=acc[:],
+                        lhsT=w1_words[a, b][:, P * t : P * (t + 1)].bitcast(E4M3),
+                        lhsT_scale=w1_sc[a, b][:, P * t : P * (t + 1)],
+                        rhs=v_words[a][:, cols].bitcast(E5M2),
+                        rhs_scale=v_sc[a][:, cols],
+                        start=(a == 0),
+                        stop=(a == K_PASSES - 1),
+                    )
+                nc.vector.tensor_tensor(out=h_rows[b, u][:, t, :], in0=acc[:], in1=damp[b, u][:, t, :], op=ALU.mult)
 
-        def place_rows(b, u, at):
-            h_rows[b, u] = arena.tile([P, PACK, JH], BF16, name=f"h_rows{b}{u}", offset=at, align_bytes=64)
-
-        def hidden_codes(b, u, weave, at=None, codes_at=None):
-            if codes_at is None:
-                h_words[b, u] = keep.tile([P, JH], U32, name=f"h_words{b}{u}", align_bytes=64)
-            else:
-                h_words[b, u] = arena.tile([P, JH], U32, name=f"h_words{b}{u}", offset=codes_at, align_bytes=64)
-            if at == "spent":
-                woven = damp[1, 0][:, 0:2, :].rearrange("p t j -> p (t j)").bitcast(BF16)
-            elif at is None:
-                woven = ring.tile([P, JH * PACK], BF16, name="woven", align_bytes=64)
-            else:
-                woven = arena.tile([P, JH * PACK], BF16, name=f"woven{b}{u}", offset=at, align_bytes=64)
-            weave(
-                out=woven[:].rearrange("p (c i t) -> p c t i", i=4, t=PACK),
-                in_=h_rows[b, u][:].rearrange("p t (c i) -> p c t i", i=4),
+        def hidden_codes(b, u, copy, woven, words):
+            h_words[b, u] = words
+            copy(
+                out=woven.rearrange("p (c i t) -> p c t i", i=RUN, t=PACK),
+                in_=h_rows[b, u][:].rearrange("p t (c i) -> p c t i", i=RUN),
             )
-            nc.vector.quantize_mx(out=h_words[b, u][:].bitcast(E4), scales=h_sc[b, u][:], in_=woven[:])
-            return woven
+            nc.vector.quantize_mx(out=words[:].bitcast(E4M3), scales=h_sc[b, u][:], in_=woven)
 
-        def load_src(u, at):
-            src_sb[u] = arena.tile([P, NT, JH], F32, name=f"src_sb{u}", offset=at, align_bytes=64)
+        def woven_tile():
+            woven = ring.tile([P, HALF * PACK], BF16, name="woven", align_bytes=64)
+            return woven[:]
+
+        def load_src(u):
+            src_sb[u] = placed([P, PAGES, HALF], F32, f"src{u}", at[f"src{u}"])
             nc.sync.dma_start(
-                out=src_sb[u][:], in_=src[:, JH * u : JH * (u + 1)].rearrange("(m p) j -> p m j", p=P)
+                out=src_sb[u][:], in_=src[:, HALF * u : HALF * (u + 1)].rearrange("(m p) j -> p m j", p=P)
+            )
+
+        def scatter(m, u, diff):
+            nc.vector.tensor_tensor(
+                out=pages[m][:].indirect(half_of(idx2, u)),
+                in0=diff,
+                in1=wgo_sb[:, HALF * u : HALF * (u + 1)],
+                op=ALU.mult,
             )
 
         def result(m, u, diff):
-            y = psum.tile([P, JH], F32, name="y", tag="bank")
-            for b in range(HB):
+            rows = slice(P * m, P * (m + 1))
+            y = psum.tile([P, HALF], F32, name="y", tag="bank")
+            for b in range(R_PASSES):
                 nc.tensor.matmul_mx(
                     out=y[:],
-                    lhsT=w2_w[:, b, P * m : P * (m + 1)].bitcast(E4),
-                    lhsT_scale=w2_sc[4 * b : P, P * m : P * (m + 1)],
-                    rhs=h_words[b, u][:].bitcast(E4),
+                    lhsT=w2_w[:, b, rows].bitcast(E4M3),
+                    lhsT_scale=w2_sc[4 * b : P, rows],
+                    rhs=h_words[b, u][:].bitcast(E4M3),
                     rhs_scale=h_sc[b, u][:],
                     start=(b == 0),
-                    stop=(b == HB - 1),
+                    stop=(b == R_PASSES - 1),
                 )
             nc.vector.tensor_tensor(out=diff, in0=y[:], in1=src_sb[u][:, m, :], op=ALU.subtract)
-            nc.vector.tensor_tensor(
-                out=pages[m][:].indirect(idx2[:, LC * u : LC * (u + 1)]),
-                in0=diff,
-                in1=wgo_sb[:, JH * u : JH * (u + 1)],
-                op=ALU.mult,
-            )
+            scatter(m, u, diff)
 
         def result_on_tensor(m, u, diff):
             rows = slice(P * m, P * (m + 1))
-            src_t = psum.tile([P, JH], F32, name="src_t", tag="bank")
-            for c in range(JH // P):
-                nc.tensor.transpose(src_t[:, P * c : P * (c + 1)], src_sb[u][:, m, P * c : P * (c + 1)], identity[:])
-            nc.scalar.activation(out=src_sb[u][:, m, :], in_=src_t[:], func=ACT.Copy, scale=-1.0)
-            y_t = psum.tile([P, JH], F32, name="y_t", tag="bank")
-            for c in range(JH // P):
-                for b in range(HB):
+            chunks = [slice(P * c, P * (c + 1)) for c in range(HALF // P)]
+            src_t = psum.tile([P, HALF], F32, name="src_t", tag="bank")
+            for cols in chunks:
+                nc.tensor.transpose(src_t[:, cols], src_sb[u][:, m, cols], identity[:])
+            minus_src_t = src_sb[u][:, m, :]
+            nc.scalar.activation(out=minus_src_t, in_=src_t[:], func=ACT.Copy, scale=-1.0)
+            y_t = psum.tile([P, HALF], F32, name="y_t", tag="bank")
+            for cols in chunks:
+                for b in range(R_PASSES):
                     nc.tensor.matmul_mx(
-                        out=y_t[:, P * c : P * (c + 1)],
-                        lhsT=h_words[b, u][:, P * c : P * (c + 1)].bitcast(E4),
-                        lhsT_scale=h_sc[b, u][:, P * c : P * (c + 1)],
-                        rhs=w2_w[:, b, rows].bitcast(E4),
+                        out=y_t[:, cols],
+                        lhsT=h_words[b, u][:, cols].bitcast(E4M3),
+                        lhsT_scale=h_sc[b, u][:, cols],
+                        rhs=w2_w[:, b, rows].bitcast(E4M3),
                         rhs_scale=w2_sc[4 * b : P, rows],
                         start=(b == 0),
-                        stop=(b == HB - 1),
+                        stop=(b == R_PASSES - 1),
                     )
-            y_t_sb = ring.tile([P, JH], F32, name="y_t_sb")
+            y_t_sb = ring.tile([P, HALF], F32, name="y_t_sb")
             nc.scalar.copy(out=y_t_sb[:], in_=y_t[:])
-            total = psum.tile([P, JH], F32, name="total", tag="bank")
-            for c in range(JH // P):
-                cols = slice(P * c, P * (c + 1))
-                nc.tensor.matmul(total[:, cols], src_sb[u][:, m, cols], identity[:], start=True, stop=False, is_transpose=True)
-                nc.tensor.matmul(total[:, cols], y_t_sb[:, cols], identity[:], start=False, stop=True, is_transpose=True)
+            total = psum.tile([P, HALF], F32, name="total", tag="bank")
+            for cols in chunks:
+                nc.tensor.matmul(
+                    total[:, cols], minus_src_t[:, cols], identity[:], start=True, stop=False, is_transpose=True
+                )
+                nc.tensor.matmul(
+                    total[:, cols], y_t_sb[:, cols], identity[:], start=False, stop=True, is_transpose=True
+                )
             nc.scalar.copy(out=diff, in_=total[:])
-            nc.vector.tensor_tensor(
-                out=pages[m][:].indirect(idx2[:, LC * u : LC * (u + 1)]),
-                in0=diff,
-                in1=wgo_sb[:, JH * u : JH * (u + 1)],
-                op=ALU.mult,
-            )
+            scatter(m, u, diff)
 
-        def shear_and_damping(b, t, halves, at):
-            shear_tile(b, t, at)
-            if len(halves) == 1:
-                damping_in_parts(b, t, 0)
-            else:
-                for u in halves:
-                    damping(b, t, u)
+        shear_both_halves(0)
+        weight_piece(0, 0, nc.vector.tensor_copy)
+        weight_codes(0, 0, kept([P, PASS], U32, "w1_words00"))
+        shear_both_halves(1)
+        gather_scales(at["shear01"] + ROWS_BYTES)
+        table_pass(0)
+        weight_piece(1, 0, nc.scalar.copy)
+        shear_both_halves(2)
+        table_pass(1)
+        weight_codes(1, 0, placed([P, PASS], U32, "w1_words10", at["tab1"]))
+        weight_piece(2, 0, nc.scalar.copy)
+        shear_both_halves(3)
+        weight_codes(2, 0, placed([P, PASS], U32, "w1_words20", at["shear03"]))
+        table_pass(2)
+        for m in range(PAGES // 2, PAGES):
+            pages[m] = placed([P, T2], F32, f"page{m}", at["tab2"] - SLOT // 2 + SLOT * (m - PAGES // 2))
+            nc.gpsimd.memset(pages[m][:], 0.0)
+        for u in range(HALVES):
+            h_rows[0, u] = placed([P, PACK, HALF], BF16, f"h_rows0{u}", at["shear00"] + ROWS_BYTES * u)
+        h_rows[1, 1] = placed([P, PACK, HALF], BF16, "h_rows11", at["shear01"])
 
-        shear_and_damping(0, 0, (0, 1), 0)
-        gather_scales()
-        weight_piece(0, 0, nc.scalar.copy, 8192)
-        shear_and_damping(0, 1, (0, 1), 16384)
-        table_pass(0, 24576)
-        weight_codes(0, 0, 24576)
-        weight_piece(1, 0, nc.scalar.copy, 32768)
-        shear_and_damping(0, 2, (0, 1), 40960)
-        table_pass(1, 49152)
-        weight_codes(1, 0, 49152)
-        weight_piece(2, 0, nc.scalar.copy, 73728)
-        shear_and_damping(0, 3, (0, 1), 57344)
-        weight_codes(2, 0, 57344)
-        table_pass(2, 65536)
-        place_rows(0, 0, 0)
-        place_rows(0, 1, 4096)
-        place_rows(1, 1, 16384)
-        weight_piece(0, 1, nc.scalar.copy, 81920)
-        for t in range(PACK):
-            hidden_rows(0, t, 0)
-        for t in range(PACK):
-            hidden_rows(0, t, 1)
-        weight_codes(0, 1, None)
-        weight_piece(1, 1, nc.scalar.copy, 90112)
-        weight_piece(2, 1, nc.scalar.copy, 98304)
-        shear_and_damping(1, 0, (0,), 8192)
-        shear_and_damping(1, 1, (0,), 32768)
-        weight_codes(1, 1, 32768)
-        weight_codes(2, 1, 34816)
-        shear_and_damping(1, 2, (0,), 40960)
-        shear_and_damping(1, 3, (0,), 73728)
-        hidden_codes(0, 0, nc.scalar.copy, 98304, 73728)
-        place_rows(1, 0, 75776)
-        nc.sync.dma_start(
-            out=w2_w[:].bitcast(I32), in_=w2_words.rearrange("b p c i -> p b (c i)").bitcast(I32)
+        weight_piece(0, 1, nc.scalar.copy)
+        for u in range(HALVES):
+            hidden_rows(0, u)
+        weight_codes(0, 1, kept([P, PASS], U32, "w1_words01"))
+        weight_piece(1, 1, nc.scalar.copy)
+        weight_piece(2, 1, nc.scalar.copy)
+        shear_first_half(0)
+        shear_first_half(1)
+        for a in range(1, K_PASSES):
+            weight_codes(a, 1, placed([P, PASS], U32, f"w1_words{a}1", at["shear11"] + WORDS_BYTES * (a - 1)))
+        shear_first_half(2)
+        shear_first_half(3)
+        hidden_codes(
+            0, 0, nc.scalar.copy,
+            placed([P, HALF * PACK], BF16, "woven00", at["w21"])[:],
+            placed([P, HALF], U32, "h_words00", at["shear13"]),
         )
-        for q in range(4):
+        h_rows[1, 0] = placed([P, PACK, HALF], BF16, "h_rows10", at["shear13"] + WORDS_BYTES)
+
+        nc.sync.dma_start(out=w2_w[:].bitcast(I32), in_=w2_words.rearrange("b p c i -> p b (c i)").bitcast(I32))
+        for q in range(P // QUADRANT):
             nc.sync.dma_start(
-                out=w2_sc[32 * q : 32 * q + 4 * HB, :].bitcast(I32),
+                out=w2_sc[QUADRANT * q : QUADRANT * q + 4 * R_PASSES, :].bitcast(I32),
                 in_=w2_scales[:, 4 * q : 4 * q + 4, :].bitcast(I32),
             )
         nc.sync.dma_start(idx2[:], offs2)
-        load_src(0, 81920)
+        load_src(0)
         nc.sync.dma_start(out=wgo_sb[:], in_=wgo)
-        load_src(1, 90112)
-        for t in range(PACK):
-            hidden_rows(1, t, 0)
-        hidden_codes(1, 0, nc.vector.tensor_copy, None, None)
+        load_src(1)
+
+        hidden_rows(1, 0)
+        hidden_codes(1, 0, nc.vector.tensor_copy, woven_tile(), kept([P, HALF], U32, "h_words10"))
         result(0, 0, damp[0, 0][:, 0, :])
         result(1, 0, damp[0, 0][:, 1, :])
-        late_damping(0)
-        hidden_codes(0, 1, nc.scalar.copy, "spent")
-        for t in range(PACK):
-            hidden_rows(1, t, 1)
-        woven = hidden_codes(1, 1, nc.scalar.copy)
-        result(2, 0, damp[1, 1][:, PACK - 2, :])
-        result(3, 0, woven[:].bitcast(F32)[:, 0:JH])
-        for m in range(NT):
-            if m < 2:
+
+        spent = damp[1, 0]
+        damping(damp[1, 1][:], spent[:])
+        spent_as_woven = spent[:, 0:2, :].rearrange("p t j -> p (t j)").bitcast(BF16)
+        hidden_codes(0, 1, nc.scalar.copy, spent_as_woven, kept([P, HALF], U32, "h_words01"))
+        hidden_rows(1, 1)
+        last_woven = woven_tile()
+        hidden_codes(1, 1, nc.scalar.copy, last_woven, kept([P, HALF], U32, "h_words11"))
+        result(2, 0, damp[1, 1][:, 2, :])
+        result(3, 0, last_woven.bitcast(F32)[:, 0:HALF])
+
+        for m in range(PAGES):
+            if m == 0:
                 result(m, 1, damp[0, 1][:, m, :])
             else:
                 result_on_tensor(m, 1, damp[0, 1][:, m, :])

@@ -1,7 +1,6 @@
 from contextlib import ExitStack
 
 import concourse.mybir as mybir
-from concourse.masks import make_identity
 
 K, H, N, T, S, T2 = 1536, 1024, 512, 2048, 1024, 2048
 FLOPS = 2 * K * H * S + 2 * H * N * S
@@ -34,10 +33,25 @@ SLOT = 8192
 ROWS_BYTES = PACK * HALF * 2
 WORDS_BYTES = PASS * 4
 
-SLOT_NAMES = (
-    "shear00", "w00", "shear01", "tab0", "w10", "shear02", "tab1",
-    "shear03", "shear11", "w20", "w01", "w11", "w21", "shear12",
+SLOTS = (
+    ("shear00", "page3"),
+    ("tab0", "shear03"),
+    ("w00", "shear10"),
+    ("shear01", "w11"),
+    ("tab1", "shear11"),
+    ("w10", "w21"),
+    ("tab2", "shear12"),
+    ("w20", "shear13"),
+    ("shear02", "src0"),
+    ("w01", "src1"),
+    ("damp00",),
+    ("damp01",),
+    ("damp10",),
+    ("damp11",),
+    ("staging",),
+    ("staging2",),
 )
+BANK = 2048
 
 
 def tile_list_wall_model_adjoint_kernel(
@@ -48,17 +62,15 @@ def tile_list_wall_model_adjoint_kernel(
         keep = ctx.enter_context(tc.tile_pool(name="keep", bufs=1))
         arena = ctx.enter_context(tc.tile_pool(name="arena", bufs=1))
         ring = ctx.enter_context(tc.tile_pool(name="ring", bufs=2))
-        psum = ctx.enter_context(tc.psum_pool(name="psum", bufs=8))
+        psum = ctx.enter_context(tc.psum_pool(name="psum", bufs=1))
 
-        at = {name: SLOT * i for i, name in enumerate(SLOT_NAMES)}
-        at["tab2"] = at["w10"]
-        at["shear10"] = at["w00"]
-        at["shear13"] = at["w20"]
-        at["src0"] = at["w01"]
-        at["src1"] = at["w11"]
+        at = {name: SLOT * i for i, names in enumerate(SLOTS) for name in names}
 
         def placed(shape, dtype, name, offset):
             return arena.tile(shape, dtype, name=name, offset=offset, align_bytes=64)
+
+        def bank(name, number):
+            return psum.tile([P, HALF], F32, name=name, offset=BANK * number)
 
         def kept(shape, dtype, name):
             return keep.tile(shape, dtype, name=name, align_bytes=64)
@@ -75,20 +87,17 @@ def tile_list_wall_model_adjoint_kernel(
                 in_=tab_scales[:, 4 * q : 4 * q + 4, :].bitcast(I32),
             )
 
-        pages = {}
-        for m, engine in enumerate((nc.vector, nc.gpsimd)):
-            pages[m] = keep.tile([P, T2], F32, name=f"page{m}")
-            engine.memset(pages[m][:], 0.0)
-
         w2_sc = kept([P, N], U8, "w2_sc")
-        nc.gpsimd.memset(w2_sc[:].bitcast(I32), 0)
+        nc.vector.memset(w2_sc[:].bitcast(I32), 0)
         v_sc = {}
         for a in range(1, K_PASSES):
             v_sc[a] = kept([P, S], U8, f"v_sc{a}")
-            nc.gpsimd.memset(v_sc[a][:].bitcast(I32), 0)
+            nc.vector.memset(v_sc[a][:].bitcast(I32), 0)
 
-        identity = keep.tile([P, P], F32, name="identity")
-        make_identity(nc, identity[:])
+        pages = {}
+        for m in range(PAGES - 1):
+            pages[m] = keep.tile([P, T2], F32, name=f"page{m}")
+            nc.vector.memset(pages[m][:], 0.0)
 
         v_words = [kept([P, S], U32, f"v_words{a}") for a in range(K_PASSES)]
         w1_rounded = {}
@@ -103,7 +112,7 @@ def tile_list_wall_model_adjoint_kernel(
         h_sc = {}
         for b in range(R_PASSES):
             for u in range(HALVES):
-                damp[b, u] = keep.tile([P, PACK, HALF], F32, name=f"damp{b}{u}")
+                damp[b, u] = placed([P, PACK, HALF], F32, f"damp{b}{u}", at[f"damp{b}{u}"])
                 h_sc[b, u] = kept([P, HALF], U8, f"h_sc{b}{u}")
         w2_w = kept([P, R_PASSES, N], U32, "w2_w")
         wgo_sb = keep.tile([P, S], F32, name="wgo_sb")
@@ -113,8 +122,8 @@ def tile_list_wall_model_adjoint_kernel(
         def half_of(offsets, u):
             return offsets[:, HALF_COLS * u : HALF_COLS * (u + 1)]
 
-        def gather_scales(offset):
-            v_sc[0] = placed([P, S], U8, "v_sc0", offset)
+        def gather_scales():
+            v_sc[0] = kept([P, S], U8, "v_sc0")
             nc.vector.tensor_copy(out=v_sc[0][:], in_=tab_sc[:].indirect(idx[:]))
             for a in range(1, K_PASSES):
                 nc.scalar.dma_start(
@@ -133,11 +142,11 @@ def tile_list_wall_model_adjoint_kernel(
                     out=v_words[a][:, HALF * u : HALF * (u + 1)], in_=window[:].indirect(half_of(idx, u))
                 )
 
-        def weight_piece(a, b, copy):
+        def weight_piece(a, b, copy, offset):
             raw = placed([P, PACK, PASS], F32, f"w{a}{b}", at[f"w{a}{b}"])
             piece = w1[PASS * a : PASS * (a + 1), PASS * b : PASS * (b + 1)]
             nc.sync.dma_start(out=raw[:], in_=piece.rearrange("(p i) c -> p i c", i=PACK))
-            rounded = ring.tile([P, PACK * PASS], BF16, name="rounded", align_bytes=64, bufs=3)
+            rounded = placed([P, PACK * PASS], BF16, f"rounded{a}{b}", offset)
             copy(
                 out=rounded[:].rearrange("p (t m i) -> p m i t", t=PACK, i=PACK),
                 in_=raw[:].rearrange("p i (m t) -> p m i t", t=PACK),
@@ -159,37 +168,6 @@ def tile_list_wall_model_adjoint_kernel(
             nc.scalar.activation(out=scratch, in_=scratch, func=ACT.Abs_reciprocal_sqrt, bias=1.0)
             nc.scalar.activation(out=shear, in_=scratch, func=ACT.Square)
 
-        def shear_both_halves(t):
-            shear_tile(0, t)
-            for u in range(HALVES):
-                damping(damp[0, u][:, t, :], damp[0, u][:, t, :])
-
-        def shear_first_half(t):
-            shear_tile(1, t)
-            parts = [damp[1, 0][:, t, HALF // 2 * c : HALF // 2 * (c + 1)] for c in range(2)]
-            for part in parts:
-                nc.scalar.activation(out=part, in_=part, func=ACT.Square)
-            for part in parts:
-                nc.scalar.activation(out=part, in_=part, func=ACT.Abs_reciprocal_sqrt, bias=1.0)
-            for part in parts:
-                nc.scalar.activation(out=part, in_=part, func=ACT.Square)
-
-        def hidden_rows(b, u):
-            cols = slice(HALF * u, HALF * (u + 1))
-            for t in range(PACK):
-                acc = psum.tile([P, HALF], F32, name="acc", tag="bank")
-                for a in range(K_PASSES):
-                    nc.tensor.matmul_mx(
-                        out=acc[:],
-                        lhsT=w1_words[a, b][:, P * t : P * (t + 1)].bitcast(E4M3),
-                        lhsT_scale=w1_sc[a, b][:, P * t : P * (t + 1)],
-                        rhs=v_words[a][:, cols].bitcast(E5M2),
-                        rhs_scale=v_sc[a][:, cols],
-                        start=(a == 0),
-                        stop=(a == K_PASSES - 1),
-                    )
-                nc.vector.tensor_tensor(out=h_rows[b, u][:, t, :], in0=acc[:], in1=damp[b, u][:, t, :], op=ALU.mult)
-
         def hidden_codes(b, u, copy, woven, words):
             h_words[b, u] = words
             copy(
@@ -208,17 +186,9 @@ def tile_list_wall_model_adjoint_kernel(
                 out=src_sb[u][:], in_=src[:, HALF * u : HALF * (u + 1)].rearrange("(m p) j -> p m j", p=P)
             )
 
-        def scatter(m, u, diff):
-            nc.vector.tensor_tensor(
-                out=pages[m][:].indirect(half_of(idx2, u)),
-                in0=diff,
-                in1=wgo_sb[:, HALF * u : HALF * (u + 1)],
-                op=ALU.mult,
-            )
-
-        def result(m, u, diff):
+        def product(m, u, number):
             rows = slice(P * m, P * (m + 1))
-            y = psum.tile([P, HALF], F32, name="y", tag="bank")
+            y = bank(f"y{m}{u}", number)
             for b in range(R_PASSES):
                 nc.tensor.matmul_mx(
                     out=y[:],
@@ -229,81 +199,118 @@ def tile_list_wall_model_adjoint_kernel(
                     start=(b == 0),
                     stop=(b == R_PASSES - 1),
                 )
+            return y
+
+        def weigh_and_scatter(m, u, diff):
+            nc.gpsimd.tensor_tensor(out=diff, in0=diff, in1=wgo_sb[:, HALF * u : HALF * (u + 1)], op=ALU.mult)
+            nc.vector.tensor_copy(out=pages[m][:].indirect(half_of(idx2, u)), in_=diff)
+
+        def first_result(m, u, diff):
+            y = product(m, u, m)
             nc.vector.tensor_tensor(out=diff, in0=y[:], in1=src_sb[u][:, m, :], op=ALU.subtract)
-            scatter(m, u, diff)
+            weigh_and_scatter(m, u, diff)
 
-        def result_on_tensor(m, u, diff):
-            rows = slice(P * m, P * (m + 1))
-            chunks = [slice(P * c, P * (c + 1)) for c in range(HALF // P)]
-            src_t = psum.tile([P, HALF], F32, name="src_t", tag="bank")
-            for cols in chunks:
-                nc.tensor.transpose(src_t[:, cols], src_sb[u][:, m, cols], identity[:])
-            minus_src_t = src_sb[u][:, m, :]
-            nc.scalar.activation(out=minus_src_t, in_=src_t[:], func=ACT.Copy, scale=-1.0)
-            y_t = psum.tile([P, HALF], F32, name="y_t", tag="bank")
-            for cols in chunks:
-                for b in range(R_PASSES):
-                    nc.tensor.matmul_mx(
-                        out=y_t[:, cols],
-                        lhsT=h_words[b, u][:, cols].bitcast(E4M3),
-                        lhsT_scale=h_sc[b, u][:, cols],
-                        rhs=w2_w[:, b, rows].bitcast(E4M3),
-                        rhs_scale=w2_sc[4 * b : P, rows],
-                        start=(b == 0),
-                        stop=(b == R_PASSES - 1),
-                    )
-            y_t_sb = ring.tile([P, HALF], F32, name="y_t_sb")
-            nc.scalar.copy(out=y_t_sb[:], in_=y_t[:])
-            total = psum.tile([P, HALF], F32, name="total", tag="bank")
-            for cols in chunks:
-                nc.tensor.matmul(
-                    total[:, cols], minus_src_t[:, cols], identity[:], start=True, stop=False, is_transpose=True
-                )
-                nc.tensor.matmul(
-                    total[:, cols], y_t_sb[:, cols], identity[:], start=False, stop=True, is_transpose=True
-                )
-            nc.scalar.copy(out=diff, in_=total[:])
-            scatter(m, u, diff)
+        def result(m, u, diff):
+            y = product(m, u, m)
+            nc.scalar.copy(out=diff, in_=y[:])
+            nc.gpsimd.tensor_tensor(out=diff, in0=diff, in1=src_sb[u][:, m, :], op=ALU.subtract)
+            weigh_and_scatter(m, u, diff)
 
-        shear_both_halves(0)
-        weight_piece(0, 0, nc.vector.tensor_copy)
-        weight_codes(0, 0, kept([P, PASS], U32, "w1_words00"))
-        shear_both_halves(1)
-        gather_scales(at["shear01"] + ROWS_BYTES)
+        def gpsimd_copy(out, in_):
+            nc.gpsimd.tensor_scalar(out=out, in0=in_, scalar1=1.0, scalar2=0.0, op0=ALU.mult, op1=ALU.add)
+
+        def hidden_row(b, u, t):
+            cols = slice(HALF * u, HALF * (u + 1))
+            acc = bank(f"acc{b}{u}{t}", PACK * u + t)
+            for a in range(K_PASSES):
+                nc.tensor.matmul_mx(
+                    out=acc[:],
+                    lhsT=w1_words[a, b][:, P * t : P * (t + 1)].bitcast(E4M3),
+                    lhsT_scale=w1_sc[a, b][:, P * t : P * (t + 1)],
+                    rhs=v_words[a][:, cols].bitcast(E5M2),
+                    rhs_scale=v_sc[a][:, cols],
+                    start=(a == 0),
+                    stop=(a == K_PASSES - 1),
+                )
+            nc.vector.tensor_tensor(out=h_rows[b, u][:, t, :], in0=acc[:], in1=damp[b, u][:, t, :], op=ALU.mult)
+
+        def damp_row(b, u, t, square_on_gpsimd=False):
+            row = damp[b, u][:, t, :]
+            if square_on_gpsimd:
+                nc.gpsimd.tensor_tensor(out=row, in0=row, in1=row, op=ALU.mult)
+            else:
+                nc.scalar.activation(out=row, in_=row, func=ACT.Square)
+            nc.scalar.activation(out=row, in_=row, func=ACT.Abs_reciprocal_sqrt, bias=1.0)
+            nc.scalar.activation(out=row, in_=row, func=ACT.Square)
+
+        def weave(b, u, woven):
+            gpsimd_copy(
+                out=woven.rearrange("p (j t) -> p j t", t=PACK),
+                in_=h_rows[b, u][:].rearrange("p t j -> p j t"),
+            )
+
+        def codes_tile(a, b):
+            return kept([P, PASS], U32, f"w1_words{a}{b}")
+
+        first, second = at["staging"], at["staging"] + ROWS_BYTES
+
+        def quantise_hidden(b, u, woven, offset):
+            h_words[b, u] = placed([P, HALF], U32, f"h_words{b}{u}", offset)
+            nc.vector.quantize_mx(out=h_words[b, u][:].bitcast(E4M3), scales=h_sc[b, u][:], in_=woven[:])
+
+        def diff_tile(m, u):
+            return placed([P, HALF], F32, f"diff{m}{u}", at[f"damp0{u}"] + WORDS_BYTES * m)
+
+        shear_tile(0, 0)
+        gather_scales()
+        pages[3] = placed([P, T2], F32, "page3", at["page3"])
+        nc.gpsimd.memset(pages[3][:], 0.0)
+        for u in range(HALVES):
+            damp_row(0, u, 0)
         table_pass(0)
-        weight_piece(1, 0, nc.scalar.copy)
-        shear_both_halves(2)
+        weight_piece(0, 0, nc.vector.tensor_copy, first)
+        weight_codes(0, 0, codes_tile(0, 0))
+        shear_tile(0, 1)
+        for u in range(HALVES):
+            damp_row(0, u, 1)
         table_pass(1)
-        weight_codes(1, 0, placed([P, PASS], U32, "w1_words10", at["tab1"]))
-        weight_piece(2, 0, nc.scalar.copy)
-        shear_both_halves(3)
-        weight_codes(2, 0, placed([P, PASS], U32, "w1_words20", at["shear03"]))
+        weight_piece(1, 0, nc.vector.tensor_copy, second)
+        weight_codes(1, 0, codes_tile(1, 0))
         table_pass(2)
-        for m in range(PAGES // 2, PAGES):
-            pages[m] = placed([P, T2], F32, f"page{m}", at["tab2"] - SLOT // 2 + SLOT * (m - PAGES // 2))
-            nc.gpsimd.memset(pages[m][:], 0.0)
+        weight_piece(2, 0, nc.scalar.copy, first)
+        weight_codes(2, 0, codes_tile(2, 0))
         for u in range(HALVES):
-            h_rows[0, u] = placed([P, PACK, HALF], BF16, f"h_rows0{u}", at["shear00"] + ROWS_BYTES * u)
-        h_rows[1, 1] = placed([P, PACK, HALF], BF16, "h_rows11", at["shear01"])
-
-        weight_piece(0, 1, nc.scalar.copy)
+            h_rows[0, u] = kept([P, PACK, HALF], BF16, f"h_rows0{u}")
+        for t in range(2):
+            for u in range(HALVES):
+                hidden_row(0, u, t)
+        shear_tile(0, 2)
         for u in range(HALVES):
-            hidden_rows(0, u)
-        weight_codes(0, 1, kept([P, PASS], U32, "w1_words01"))
-        weight_piece(1, 1, nc.scalar.copy)
-        weight_piece(2, 1, nc.scalar.copy)
-        shear_first_half(0)
-        shear_first_half(1)
-        for a in range(1, K_PASSES):
-            weight_codes(a, 1, placed([P, PASS], U32, f"w1_words{a}1", at["shear11"] + WORDS_BYTES * (a - 1)))
-        shear_first_half(2)
-        shear_first_half(3)
-        hidden_codes(
-            0, 0, nc.scalar.copy,
-            placed([P, HALF * PACK], BF16, "woven00", at["w21"])[:],
-            placed([P, HALF], U32, "h_words00", at["shear13"]),
-        )
-        h_rows[1, 0] = placed([P, PACK, HALF], BF16, "h_rows10", at["shear13"] + WORDS_BYTES)
+            damp_row(0, u, 2, False)
+            hidden_row(0, u, 2)
+        weight_piece(0, 1, nc.scalar.copy, second)
+        shear_tile(0, 3)
+        for u in range(HALVES):
+            damp_row(0, u, 3, False)
+            hidden_row(0, u, 3)
+        weight_codes(0, 1, placed([P, PASS], U32, "w1_words01", at["shear03"]))
+        shear_tile(1, 0)
+        weight_piece(1, 1, nc.scalar.copy, first)
+        woven00 = placed([P, HALF * PACK], BF16, "woven00", second)
+        weave(0, 0, woven00[:])
+        damp_row(1, 0, 0)
+        shear_tile(1, 1)
+        weight_codes(1, 1, placed([P, PASS], U32, "w1_words11", at["shear11"]))
+        quantise_hidden(0, 0, woven00, at["shear11"] + WORDS_BYTES)
+        woven01 = placed([P, HALF * PACK], BF16, "woven01", first + ROWS_BYTES // 2)
+        weave(0, 1, woven01[:])
+        weight_piece(2, 1, nc.scalar.copy, at["staging2"])
+        damp_row(1, 0, 1)
+        shear_tile(1, 2)
+        weight_codes(2, 1, placed([P, PASS], U32, "w1_words21", at["shear12"]))
+        damp_row(1, 0, 2)
+        shear_tile(1, 3)
+        damp_row(1, 0, 3)
 
         nc.sync.dma_start(out=w2_w[:].bitcast(I32), in_=w2_words.rearrange("b p c i -> p b (c i)").bitcast(I32))
         for q in range(P // QUADRANT):
@@ -316,24 +323,22 @@ def tile_list_wall_model_adjoint_kernel(
         nc.sync.dma_start(out=wgo_sb[:], in_=wgo)
         load_src(1)
 
-        hidden_rows(1, 0)
+        for u in range(HALVES):
+            h_rows[1, u] = placed([P, PACK, HALF], BF16, f"h_rows1{u}", at["shear13"] + ROWS_BYTES * u)
+        for t in range(PACK):
+            hidden_row(1, 0, t)
+        quantise_hidden(0, 1, woven01, at["damp10"])
         hidden_codes(1, 0, nc.vector.tensor_copy, woven_tile(), kept([P, HALF], U32, "h_words10"))
-        result(0, 0, damp[0, 0][:, 0, :])
-        result(1, 0, damp[0, 0][:, 1, :])
-
-        spent = damp[1, 0]
-        damping(damp[1, 1][:], spent[:])
-        spent_as_woven = spent[:, 0:2, :].rearrange("p t j -> p (t j)").bitcast(BF16)
-        hidden_codes(0, 1, nc.scalar.copy, spent_as_woven, kept([P, HALF], U32, "h_words01"))
-        hidden_rows(1, 1)
-        last_woven = woven_tile()
-        hidden_codes(1, 1, nc.scalar.copy, last_woven, kept([P, HALF], U32, "h_words11"))
-        result(2, 0, damp[1, 1][:, 2, :])
-        result(3, 0, last_woven.bitcast(F32)[:, 0:HALF])
-
+        first_result(0, 0, diff_tile(0, 0)[:])
+        for t in range(PACK):
+            damp_row(1, 1, t)
+            hidden_row(1, 1, t)
+        result(1, 0, diff_tile(1, 0)[:])
+        result(2, 0, diff_tile(2, 0)[:])
+        hidden_codes(
+            1, 1, nc.scalar.copy, woven_tile(), placed([P, HALF], U32, "h_words11", at["damp00"])
+        )
+        result(3, 0, diff_tile(3, 0)[:])
         for m in range(PAGES):
-            if m == 0:
-                result(m, 1, damp[0, 1][:, m, :])
-            else:
-                result_on_tensor(m, 1, damp[0, 1][:, m, :])
+            result(m, 1, diff_tile(m, 1)[:])
             nc.sync.dma_start(out=out[P * m : P * (m + 1), :], in_=pages[m][:])

@@ -34,22 +34,25 @@ ROWS_BYTES = PACK * HALF * 2
 WORDS_BYTES = PASS * 4
 
 SLOTS = (
-    ("shear00", "page3"),
-    ("tab0", "shear03"),
+    ("shear00", "page1"),
+    ("shear01", "page2"),
+    ("shear02", "v_sc0"),
+    ("rounded10", "page3"),
+    ("tab0", "tab2", "shear12"),
     ("w00", "shear10"),
-    ("shear01", "w11"),
-    ("tab1", "shear11"),
-    ("w10", "w21"),
-    ("tab2", "shear12"),
-    ("w20", "shear13"),
-    ("shear02", "src0"),
-    ("w01", "src1"),
-    ("damp00",),
-    ("damp01",),
-    ("damp10",),
-    ("damp11",),
+    ("tab1", "w11"),
+    ("w10", "shear11"),
+    ("shear13",),
+    ("w20", "w21"),
+    ("shear03", "src1"),
+    ("w01", "src0"),
+    ("damp0",),
+    ("damp0_end",),
+    ("damp1",),
+    ("damp1_end",),
     ("staging",),
     ("staging2",),
+    ("tail",),
 )
 BANK = 2048
 
@@ -95,9 +98,8 @@ def tile_list_wall_model_adjoint_kernel(
             nc.vector.memset(v_sc[a][:].bitcast(I32), 0)
 
         pages = {}
-        for m in range(PAGES - 1):
-            pages[m] = keep.tile([P, T2], F32, name=f"page{m}")
-            nc.vector.memset(pages[m][:], 0.0)
+        pages[0] = keep.tile([P, T2], F32, name="page0")
+        nc.vector.memset(pages[0][:], 0.0)
 
         v_words = [kept([P, S], U32, f"v_words{a}") for a in range(K_PASSES)]
         w1_rounded = {}
@@ -111,8 +113,8 @@ def tile_list_wall_model_adjoint_kernel(
         h_words = {}
         h_sc = {}
         for b in range(R_PASSES):
+            damp[b] = placed([P, PACK, S], F32, f"damp{b}", at[f"damp{b}"])
             for u in range(HALVES):
-                damp[b, u] = placed([P, PACK, HALF], F32, f"damp{b}{u}", at[f"damp{b}{u}"])
                 h_sc[b, u] = kept([P, HALF], U8, f"h_sc{b}{u}")
         w2_w = kept([P, R_PASSES, N], U32, "w2_w")
         wgo_sb = keep.tile([P, S], F32, name="wgo_sb")
@@ -122,11 +124,14 @@ def tile_list_wall_model_adjoint_kernel(
         def half_of(offsets, u):
             return offsets[:, HALF_COLS * u : HALF_COLS * (u + 1)]
 
+        def damp_half(b, u, t):
+            return damp[b][:, t, HALF * u : HALF * (u + 1)]
+
         def gather_scales():
-            v_sc[0] = kept([P, S], U8, "v_sc0")
+            v_sc[0] = placed([P, S], U8, "v_sc0", at["v_sc0"])
             nc.vector.tensor_copy(out=v_sc[0][:], in_=tab_sc[:].indirect(idx[:]))
             for a in range(1, K_PASSES):
-                nc.scalar.dma_start(
+                nc.gpsimd.dma_start(
                     out=v_sc[a][0:MOVED_ROWS, :].bitcast(I32),
                     in_=v_sc[0][4 * a : 4 * a + MOVED_ROWS, :].bitcast(I32),
                 )
@@ -137,19 +142,16 @@ def tile_list_wall_model_adjoint_kernel(
                 out=window[:].bitcast(I32),
                 in_=tab_words[a].rearrange("p t i -> p (t i)").bitcast(I32),
             )
-            for u in range(HALVES):
-                nc.vector.tensor_copy(
-                    out=v_words[a][:, HALF * u : HALF * (u + 1)], in_=window[:].indirect(half_of(idx, u))
-                )
+            nc.vector.tensor_copy(out=v_words[a][:], in_=window[:].indirect(idx[:]))
 
-        def weight_piece(a, b, copy, offset):
+        def weight_piece(a, b, copy, offset, walk="p m i t"):
             raw = placed([P, PACK, PASS], F32, f"w{a}{b}", at[f"w{a}{b}"])
             piece = w1[PASS * a : PASS * (a + 1), PASS * b : PASS * (b + 1)]
             nc.sync.dma_start(out=raw[:], in_=piece.rearrange("(p i) c -> p i c", i=PACK))
             rounded = placed([P, PACK * PASS], BF16, f"rounded{a}{b}", offset)
             copy(
-                out=rounded[:].rearrange("p (t m i) -> p m i t", t=PACK, i=PACK),
-                in_=raw[:].rearrange("p i (m t) -> p m i t", t=PACK),
+                out=rounded[:].rearrange("p (t m i) -> " + walk, t=PACK, i=PACK),
+                in_=raw[:].rearrange("p i (m t) -> " + walk, t=PACK),
             )
             w1_rounded[a, b] = rounded
 
@@ -157,16 +159,14 @@ def tile_list_wall_model_adjoint_kernel(
             w1_words[a, b] = words
             nc.vector.quantize_mx(out=words[:].bitcast(E4M3), scales=w1_sc[a, b][:], in_=w1_rounded[a, b][:])
 
-        def shear_tile(b, t):
+        def shear_tile(b, t, by_halves=False):
             window = placed([P, T], F32, f"shear{b}{t}", at[f"shear{b}{t}"])
             nc.sync.dma_start(out=window[:], in_=shear_rows[b, t])
-            for u in range(HALVES):
-                nc.vector.tensor_copy(out=damp[b, u][:, t, :], in_=window[:].indirect(half_of(idx, u)))
-
-        def damping(shear, scratch):
-            nc.scalar.activation(out=scratch, in_=shear, func=ACT.Square)
-            nc.scalar.activation(out=scratch, in_=scratch, func=ACT.Abs_reciprocal_sqrt, bias=1.0)
-            nc.scalar.activation(out=shear, in_=scratch, func=ACT.Square)
+            if by_halves:
+                for u in range(HALVES):
+                    nc.vector.tensor_copy(out=damp_half(b, u, t), in_=window[:].indirect(half_of(idx, u)))
+            else:
+                nc.vector.tensor_copy(out=damp[b][:, t, :], in_=window[:].indirect(idx[:]))
 
         def hidden_codes(b, u, copy, woven, words):
             h_words[b, u] = words
@@ -201,20 +201,19 @@ def tile_list_wall_model_adjoint_kernel(
                 )
             return y
 
-        def weigh_and_scatter(m, u, diff):
-            nc.gpsimd.tensor_tensor(out=diff, in0=diff, in1=wgo_sb[:, HALF * u : HALF * (u + 1)], op=ALU.mult)
-            nc.vector.tensor_copy(out=pages[m][:].indirect(half_of(idx2, u)), in_=diff)
+        def weigh_and_scatter(m, u, diff, weighted, engine):
+            engine.tensor_tensor(out=weighted, in0=diff, in1=wgo_sb[:, HALF * u : HALF * (u + 1)], op=ALU.mult)
+            nc.vector.tensor_copy(out=pages[m][:].indirect(half_of(idx2, u)), in_=weighted)
 
-        def first_result(m, u, diff):
+        def result(m, u, diff_at, values_at=None):
             y = product(m, u, m)
-            nc.vector.tensor_tensor(out=diff, in0=y[:], in1=src_sb[u][:, m, :], op=ALU.subtract)
-            weigh_and_scatter(m, u, diff)
-
-        def result(m, u, diff):
-            y = product(m, u, m)
-            nc.scalar.copy(out=diff, in_=y[:])
-            nc.gpsimd.tensor_tensor(out=diff, in0=diff, in1=src_sb[u][:, m, :], op=ALU.subtract)
-            weigh_and_scatter(m, u, diff)
+            if values_at is None:
+                values_at = at["damp0"] + WORDS_BYTES * (PAGES * u + m)
+            values = placed([P, HALF], F32, f"values{m}{u}", values_at)
+            nc.scalar.copy(out=values[:], in_=y[:])
+            diff = placed([P, HALF], F32, f"diff{m}{u}", diff_at)
+            nc.gpsimd.tensor_tensor(out=diff[:], in0=values[:], in1=src_sb[u][:, m, :], op=ALU.subtract)
+            weigh_and_scatter(m, u, diff[:], values[:], nc.gpsimd)
 
         def gpsimd_copy(out, in_):
             nc.gpsimd.tensor_scalar(out=out, in0=in_, scalar1=1.0, scalar2=0.0, op0=ALU.mult, op1=ALU.add)
@@ -232,16 +231,16 @@ def tile_list_wall_model_adjoint_kernel(
                     start=(a == 0),
                     stop=(a == K_PASSES - 1),
                 )
-            nc.vector.tensor_tensor(out=h_rows[b, u][:, t, :], in0=acc[:], in1=damp[b, u][:, t, :], op=ALU.mult)
+            nc.vector.tensor_tensor(out=h_rows[b, u][:, t, :], in0=acc[:], in1=damp_half(b, u, t), op=ALU.mult)
 
-        def damp_row(b, u, t, square_on_gpsimd=False):
-            row = damp[b, u][:, t, :]
-            if square_on_gpsimd:
-                nc.gpsimd.tensor_tensor(out=row, in0=row, in1=row, op=ALU.mult)
-            else:
-                nc.scalar.activation(out=row, in_=row, func=ACT.Square)
-            nc.scalar.activation(out=row, in_=row, func=ACT.Abs_reciprocal_sqrt, bias=1.0)
-            nc.scalar.activation(out=row, in_=row, func=ACT.Square)
+        def damp_row(b, u, t, scratch_at=None):
+            row = damp_half(b, u, t)
+            scratch = row
+            if scratch_at is not None:
+                scratch = placed([P, HALF], F32, f"scratch{b}{u}{t}", scratch_at)[:]
+            nc.scalar.activation(out=scratch, in_=row, func=ACT.Square)
+            nc.scalar.activation(out=scratch, in_=scratch, func=ACT.Abs_reciprocal_sqrt, bias=1.0)
+            nc.scalar.activation(out=row, in_=scratch, func=ACT.Square)
 
         def weave(b, u, woven):
             gpsimd_copy(
@@ -258,58 +257,61 @@ def tile_list_wall_model_adjoint_kernel(
             h_words[b, u] = placed([P, HALF], U32, f"h_words{b}{u}", offset)
             nc.vector.quantize_mx(out=h_words[b, u][:].bitcast(E4M3), scales=h_sc[b, u][:], in_=woven[:])
 
-        def diff_tile(m, u):
-            return placed([P, HALF], F32, f"diff{m}{u}", at[f"damp0{u}"] + WORDS_BYTES * m)
+        def clear_page(m):
+            pages[m] = placed([P, T2], F32, f"page{m}", at[f"page{m}"])
+            nc.gpsimd.memset(pages[m][:], 0.0)
 
+        third, fourth = at["staging2"], at["staging2"] + ROWS_BYTES
         shear_tile(0, 0)
-        gather_scales()
-        pages[3] = placed([P, T2], F32, "page3", at["page3"])
-        nc.gpsimd.memset(pages[3][:], 0.0)
+        clear_page(1)
         for u in range(HALVES):
             damp_row(0, u, 0)
-        table_pass(0)
-        weight_piece(0, 0, nc.vector.tensor_copy, first)
-        weight_codes(0, 0, codes_tile(0, 0))
         shear_tile(0, 1)
+        clear_page(2)
         for u in range(HALVES):
             damp_row(0, u, 1)
+        shear_tile(0, 2)
+        gather_scales()
+        table_pass(0)
+        weight_piece(0, 0, nc.scalar.copy, first)
+        weight_codes(0, 0, codes_tile(0, 0))
+        for u in range(HALVES):
+            damp_row(0, u, 2, at["w00"] + WORDS_BYTES * u)
         table_pass(1)
-        weight_piece(1, 0, nc.vector.tensor_copy, second)
-        weight_codes(1, 0, codes_tile(1, 0))
+        weight_piece(1, 0, nc.vector.tensor_copy, at["rounded10"])
         table_pass(2)
+        weight_codes(1, 0, codes_tile(1, 0))
+        clear_page(3)
         weight_piece(2, 0, nc.scalar.copy, first)
         weight_codes(2, 0, codes_tile(2, 0))
         for u in range(HALVES):
             h_rows[0, u] = kept([P, PACK, HALF], BF16, f"h_rows0{u}")
-        for t in range(2):
+        shear_tile(0, 3, True)
+        weight_piece(0, 1, gpsimd_copy, third, "p t m i")
+        for t in range(3):
             for u in range(HALVES):
                 hidden_row(0, u, t)
-        shear_tile(0, 2)
         for u in range(HALVES):
-            damp_row(0, u, 2, False)
-            hidden_row(0, u, 2)
-        weight_piece(0, 1, nc.scalar.copy, second)
-        shear_tile(0, 3)
-        for u in range(HALVES):
-            damp_row(0, u, 3, False)
+            damp_row(0, u, 3)
             hidden_row(0, u, 3)
-        weight_codes(0, 1, placed([P, PASS], U32, "w1_words01", at["shear03"]))
         shear_tile(1, 0)
-        weight_piece(1, 1, nc.scalar.copy, first)
+        weight_codes(0, 1, placed([P, PASS], U32, "w1_words01", at["shear10"]))
         woven00 = placed([P, HALF * PACK], BF16, "woven00", second)
         weave(0, 0, woven00[:])
-        damp_row(1, 0, 0)
+        weight_piece(1, 1, nc.scalar.copy, first)
+        for u in range(HALVES):
+            damp_row(1, u, 0, at["w11"] + WORDS_BYTES * u)
         shear_tile(1, 1)
         weight_codes(1, 1, placed([P, PASS], U32, "w1_words11", at["shear11"]))
         quantise_hidden(0, 0, woven00, at["shear11"] + WORDS_BYTES)
         woven01 = placed([P, HALF * PACK], BF16, "woven01", first + ROWS_BYTES // 2)
         weave(0, 1, woven01[:])
-        weight_piece(2, 1, nc.scalar.copy, at["staging2"])
-        damp_row(1, 0, 1)
+        weight_piece(2, 1, nc.scalar.copy, fourth)
+        damp_row(1, 0, 1, at["w21"])
         shear_tile(1, 2)
         weight_codes(2, 1, placed([P, PASS], U32, "w1_words21", at["shear12"]))
         damp_row(1, 0, 2)
-        shear_tile(1, 3)
+        shear_tile(1, 3, True)
         damp_row(1, 0, 3)
 
         nc.sync.dma_start(out=w2_w[:].bitcast(I32), in_=w2_words.rearrange("b p c i -> p b (c i)").bitcast(I32))
@@ -327,18 +329,24 @@ def tile_list_wall_model_adjoint_kernel(
             h_rows[1, u] = placed([P, PACK, HALF], BF16, f"h_rows1{u}", at["shear13"] + ROWS_BYTES * u)
         for t in range(PACK):
             hidden_row(1, 0, t)
-        quantise_hidden(0, 1, woven01, at["damp10"])
+        quantise_hidden(0, 1, woven01, at["shear12"] + WORDS_BYTES)
         hidden_codes(1, 0, nc.vector.tensor_copy, woven_tile(), kept([P, HALF], U32, "h_words10"))
-        first_result(0, 0, diff_tile(0, 0)[:])
         for t in range(PACK):
-            damp_row(1, 1, t)
+            if t:
+                damp_row(1, 1, t, at["w21"] + WORDS_BYTES * t)
             hidden_row(1, 1, t)
-        result(1, 0, diff_tile(1, 0)[:])
-        result(2, 0, diff_tile(2, 0)[:])
-        hidden_codes(
-            1, 1, nc.scalar.copy, woven_tile(), placed([P, HALF], U32, "h_words11", at["damp00"])
-        )
-        result(3, 0, diff_tile(3, 0)[:])
+        y = product(0, 0, 0)
+        diff_at = at["tail"]
+        diff = placed([P, HALF], F32, "diff00", diff_at)
+        nc.vector.tensor_tensor(out=diff[:], in0=y[:], in1=src_sb[0][:, 0, :], op=ALU.subtract)
+        weighted = placed([P, HALF], F32, "weighted00", at["damp1"])
+        weigh_and_scatter(0, 0, diff[:], weighted[:], nc.vector)
+        result(1, 0, diff_at, at["w21"] + WORDS_BYTES * 3)
+        woven11 = placed([P, HALF * PACK], BF16, "woven11", diff_at + WORDS_BYTES)
+        hidden_codes(1, 1, nc.scalar.copy, woven11[:], placed([P, HALF], U32, "h_words11", at["w21"] + WORDS_BYTES * 3))
+        result(2, 0, diff_at)
+        diff_at += WORDS_BYTES // 2
+        result(3, 0, diff_at, at["shear13"] + ROWS_BYTES)
         for m in range(PAGES):
-            result(m, 1, diff_tile(m, 1)[:])
+            result(m, 1, diff_at)
             nc.sync.dma_start(out=out[P * m : P * (m + 1), :], in_=pages[m][:])

@@ -34,18 +34,19 @@ ROWS_BYTES = PACK * HALF * 2
 WORDS_BYTES = PASS * 4
 
 SLOTS = (
-    ("shear00", "page1"),
-    ("shear01", "page2"),
+    ("pad",),
+    ("shear00",),
+    ("shear01",),
+    ("pad_end",),
     ("shear02", "v_sc0"),
-    ("rounded10", "page3"),
-    ("tab0", "tab2", "shear12"),
-    ("w00", "shear10"),
-    ("tab1", "w11"),
-    ("w10", "shear11"),
-    ("shear13",),
-    ("w20", "w21"),
-    ("shear03", "src1"),
-    ("w01", "src0"),
+    ("shear03", "w11"),
+    ("tab1",),
+    ("shear10", "w10", "w21"),
+    ("tab0", "w20", "shear12"),
+    ("w00", "w01", "src0"),
+    ("tab2", "shear13"),
+    ("shear11",),
+    ("src1",),
     ("damp0",),
     ("damp0_end",),
     ("damp1",),
@@ -109,6 +110,7 @@ def tile_list_wall_model_adjoint_kernel(
             for b in range(R_PASSES):
                 w1_sc[a, b] = kept([P, PASS], U8, f"w1_sc{a}{b}")
         damp = {}
+        factor = {}
         h_rows = {}
         h_words = {}
         h_sc = {}
@@ -136,13 +138,19 @@ def tile_list_wall_model_adjoint_kernel(
                     in_=v_sc[0][4 * a : 4 * a + MOVED_ROWS, :].bitcast(I32),
                 )
 
-        def table_pass(a):
+        def table_pass(a, by_halves=False):
             window = placed([P, T], U32, f"tab{a}", at[f"tab{a}"])
             nc.sync.dma_start(
                 out=window[:].bitcast(I32),
                 in_=tab_words[a].rearrange("p t i -> p (t i)").bitcast(I32),
             )
-            nc.vector.tensor_copy(out=v_words[a][:], in_=window[:].indirect(idx[:]))
+            if by_halves:
+                for u in range(HALVES):
+                    nc.vector.tensor_copy(
+                        out=v_words[a][:, HALF * u : HALF * (u + 1)], in_=window[:].indirect(half_of(idx, u))
+                    )
+            else:
+                nc.vector.tensor_copy(out=v_words[a][:], in_=window[:].indirect(idx[:]))
 
         def weight_piece(a, b, copy, offset, walk="p m i t"):
             raw = placed([P, PACK, PASS], F32, f"w{a}{b}", at[f"w{a}{b}"])
@@ -205,7 +213,7 @@ def tile_list_wall_model_adjoint_kernel(
             engine.tensor_tensor(out=weighted, in0=diff, in1=wgo_sb[:, HALF * u : HALF * (u + 1)], op=ALU.mult)
             nc.vector.tensor_copy(out=pages[m][:].indirect(half_of(idx2, u)), in_=weighted)
 
-        def result(m, u, diff_at, values_at=None):
+        def result(m, u, diff_at, values_at=None, weighted_at=None):
             y = product(m, u, m)
             if values_at is None:
                 values_at = at["damp0"] + WORDS_BYTES * (PAGES * u + m)
@@ -213,7 +221,10 @@ def tile_list_wall_model_adjoint_kernel(
             nc.scalar.copy(out=values[:], in_=y[:])
             diff = placed([P, HALF], F32, f"diff{m}{u}", diff_at)
             nc.gpsimd.tensor_tensor(out=diff[:], in0=values[:], in1=src_sb[u][:, m, :], op=ALU.subtract)
-            weigh_and_scatter(m, u, diff[:], values[:], nc.gpsimd)
+            weighted = values
+            if weighted_at is not None:
+                weighted = placed([P, HALF], F32, f"weighted{m}{u}", weighted_at)
+            weigh_and_scatter(m, u, diff[:], weighted[:], nc.gpsimd)
 
         def gpsimd_copy(out, in_):
             nc.gpsimd.tensor_scalar(out=out, in0=in_, scalar1=1.0, scalar2=0.0, op0=ALU.mult, op1=ALU.add)
@@ -231,18 +242,19 @@ def tile_list_wall_model_adjoint_kernel(
                     start=(a == 0),
                     stop=(a == K_PASSES - 1),
                 )
-            nc.vector.tensor_tensor(out=h_rows[b, u][:, t, :], in0=acc[:], in1=damp_half(b, u, t), op=ALU.mult)
+            nc.vector.tensor_tensor(out=h_rows[b, u][:, t, :], in0=acc[:], in1=factor[b, u, t], op=ALU.mult)
 
-        def damp_row(b, u, t, scratch_at=None):
+        def damp_row(b, u, t, scratch_at=None, stay=False):
             row = damp_half(b, u, t)
             scratch = row
             if scratch_at is not None:
                 scratch = placed([P, HALF], F32, f"scratch{b}{u}{t}", scratch_at)[:]
             nc.scalar.activation(out=scratch, in_=row, func=ACT.Square)
             nc.scalar.activation(out=scratch, in_=scratch, func=ACT.Abs_reciprocal_sqrt, bias=1.0)
-            nc.scalar.activation(out=row, in_=scratch, func=ACT.Square)
+            factor[b, u, t] = scratch if stay else row
+            nc.scalar.activation(out=factor[b, u, t], in_=scratch, func=ACT.Square)
 
-        def weave(b, u, woven):
+        def gpsimd_weave(b, u, woven):
             gpsimd_copy(
                 out=woven.rearrange("p (j t) -> p j t", t=PACK),
                 in_=h_rows[b, u][:].rearrange("p t j -> p j t"),
@@ -258,61 +270,60 @@ def tile_list_wall_model_adjoint_kernel(
             nc.vector.quantize_mx(out=h_words[b, u][:].bitcast(E4M3), scales=h_sc[b, u][:], in_=woven[:])
 
         def clear_page(m):
-            pages[m] = placed([P, T2], F32, f"page{m}", at[f"page{m}"])
+            pages[m] = placed([P, T2], F32, f"page{m}", at["shear00"] - SLOT // 2 + SLOT * (m - 1))
             nc.gpsimd.memset(pages[m][:], 0.0)
 
         third, fourth = at["staging2"], at["staging2"] + ROWS_BYTES
-        shear_tile(0, 0)
-        clear_page(1)
-        for u in range(HALVES):
-            damp_row(0, u, 0)
-        shear_tile(0, 1)
-        clear_page(2)
-        for u in range(HALVES):
-            damp_row(0, u, 1)
-        shear_tile(0, 2)
-        gather_scales()
+        for t in range(PACK):
+            shear_tile(0, t)
+            if t == 0:
+                clear_page(1)
+            if t == 1:
+                clear_page(2)
+                clear_page(3)
+            if t == 2:
+                gather_scales()
+            if t < PACK - 1:
+                for u in range(HALVES):
+                    damp_row(0, u, t)
+        shear_tile(1, 0)
         table_pass(0)
         weight_piece(0, 0, nc.scalar.copy, first)
-        weight_codes(0, 0, codes_tile(0, 0))
         for u in range(HALVES):
-            damp_row(0, u, 2, at["w00"] + WORDS_BYTES * u)
+            damp_row(0, u, PACK - 1, at["w00"] + WORDS_BYTES * u)
+        weight_codes(0, 0, codes_tile(0, 0))
         table_pass(1)
-        weight_piece(1, 0, nc.vector.tensor_copy, at["rounded10"])
-        table_pass(2)
-        weight_codes(1, 0, codes_tile(1, 0))
-        clear_page(3)
-        weight_piece(2, 0, nc.scalar.copy, first)
+        weight_piece(1, 0, nc.scalar.copy, second)
+        for u in range(HALVES):
+            damp_row(1, u, 0, at["w10"] + WORDS_BYTES * u)
+        weight_piece(2, 0, nc.vector.tensor_copy, third)
+        weight_codes(1, 0, placed([P, PASS], U32, "w1_words10", at["w20"]))
         weight_codes(2, 0, codes_tile(2, 0))
+        table_pass(2, True)
         for u in range(HALVES):
             h_rows[0, u] = kept([P, PACK, HALF], BF16, f"h_rows0{u}")
-        shear_tile(0, 3, True)
-        weight_piece(0, 1, gpsimd_copy, third, "p t m i")
-        for t in range(3):
-            for u in range(HALVES):
+            for t in range(PACK):
                 hidden_row(0, u, t)
-        for u in range(HALVES):
-            damp_row(0, u, 3)
-            hidden_row(0, u, 3)
-        shear_tile(1, 0)
-        weight_codes(0, 1, placed([P, PASS], U32, "w1_words01", at["shear10"]))
         woven00 = placed([P, HALF * PACK], BF16, "woven00", second)
-        weave(0, 0, woven00[:])
-        weight_piece(1, 1, nc.scalar.copy, first)
-        for u in range(HALVES):
-            damp_row(1, u, 0, at["w11"] + WORDS_BYTES * u)
+        gpsimd_weave(0, 0, woven00[:])
+        weight_piece(0, 1, nc.scalar.copy, first)
         shear_tile(1, 1)
-        weight_codes(1, 1, placed([P, PASS], U32, "w1_words11", at["shear11"]))
+        weight_codes(0, 1, codes_tile(0, 1))
         quantise_hidden(0, 0, woven00, at["shear11"] + WORDS_BYTES)
-        woven01 = placed([P, HALF * PACK], BF16, "woven01", first + ROWS_BYTES // 2)
-        weave(0, 1, woven01[:])
+        weight_piece(1, 1, nc.scalar.copy, third)
+        weight_codes(1, 1, codes_tile(1, 1))
+        woven01 = placed([P, HALF * PACK], BF16, "woven01", second + ROWS_BYTES // 2)
+        gpsimd_weave(0, 1, woven01[:])
         weight_piece(2, 1, nc.scalar.copy, fourth)
-        damp_row(1, 0, 1, at["w21"])
+        for u in range(HALVES):
+            damp_row(1, u, 1, at["w21"] + WORDS_BYTES * u)
         shear_tile(1, 2)
         weight_codes(2, 1, placed([P, PASS], U32, "w1_words21", at["shear12"]))
         damp_row(1, 0, 2)
         shear_tile(1, 3, True)
-        damp_row(1, 0, 3)
+        damp_row(1, 0, 3, at["w11"], True)
+        damp_row(1, 1, 2, at["w21"])
+        damp_row(1, 1, 3, at["w21"] + WORDS_BYTES)
 
         nc.sync.dma_start(out=w2_w[:].bitcast(I32), in_=w2_words.rearrange("b p c i -> p b (c i)").bitcast(I32))
         for q in range(P // QUADRANT):
@@ -325,28 +336,26 @@ def tile_list_wall_model_adjoint_kernel(
         nc.sync.dma_start(out=wgo_sb[:], in_=wgo)
         load_src(1)
 
-        for u in range(HALVES):
-            h_rows[1, u] = placed([P, PACK, HALF], BF16, f"h_rows1{u}", at["shear13"] + ROWS_BYTES * u)
+        h_rows[1, 0] = placed([P, PACK, HALF], BF16, "h_rows10", at["shear13"])
         for t in range(PACK):
             hidden_row(1, 0, t)
-        quantise_hidden(0, 1, woven01, at["shear12"] + WORDS_BYTES)
-        hidden_codes(1, 0, nc.vector.tensor_copy, woven_tile(), kept([P, HALF], U32, "h_words10"))
+        woven10 = placed([P, HALF * PACK], BF16, "woven10", at["shear13"] + ROWS_BYTES)
+        hidden_codes(1, 0, nc.vector.tensor_copy, woven10[:], kept([P, HALF], U32, "h_words10"))
+        quantise_hidden(0, 1, woven01, at["shear13"] + ROWS_BYTES)
+        for m in range(2):
+            y = product(m, 0, m)
+            diff = placed([P, HALF], F32, f"diff{m}0", at["tail"] + WORDS_BYTES * m)
+            nc.vector.tensor_tensor(out=diff[:], in0=y[:], in1=src_sb[0][:, m, :], op=ALU.subtract)
+            weighted = placed([P, HALF], F32, f"weighted{m}0", at["damp0"] + WORDS_BYTES * m)
+            weigh_and_scatter(m, 0, diff[:], weighted[:], nc.gpsimd)
+        h_rows[1, 1] = placed([P, PACK, HALF], BF16, "h_rows11", at["w11"])
         for t in range(PACK):
-            if t:
-                damp_row(1, 1, t, at["w21"] + WORDS_BYTES * t)
             hidden_row(1, 1, t)
-        y = product(0, 0, 0)
-        diff_at = at["tail"]
-        diff = placed([P, HALF], F32, "diff00", diff_at)
-        nc.vector.tensor_tensor(out=diff[:], in0=y[:], in1=src_sb[0][:, 0, :], op=ALU.subtract)
-        weighted = placed([P, HALF], F32, "weighted00", at["damp1"])
-        weigh_and_scatter(0, 0, diff[:], weighted[:], nc.vector)
-        result(1, 0, diff_at, at["w21"] + WORDS_BYTES * 3)
-        woven11 = placed([P, HALF * PACK], BF16, "woven11", diff_at + WORDS_BYTES)
-        hidden_codes(1, 1, nc.scalar.copy, woven11[:], placed([P, HALF], U32, "h_words11", at["w21"] + WORDS_BYTES * 3))
-        result(2, 0, diff_at)
-        diff_at += WORDS_BYTES // 2
-        result(3, 0, diff_at, at["shear13"] + ROWS_BYTES)
+        ring_at = at["tail"] + WORDS_BYTES
+        woven11 = placed([P, HALF * PACK], BF16, "woven11", at["w11"] + ROWS_BYTES)
+        hidden_codes(1, 1, nc.scalar.copy, woven11[:], placed([P, HALF], U32, "h_words11", at["damp0"] + WORDS_BYTES))
+        result(2, 0, ring_at, at["w21"] + WORDS_BYTES, at["w11"])
+        result(3, 0, ring_at, None, at["w11"] + ROWS_BYTES)
         for m in range(PAGES):
-            result(m, 1, diff_at)
+            result(m, 1, ring_at)
             nc.sync.dma_start(out=out[P * m : P * (m + 1), :], in_=pages[m][:])

@@ -40,19 +40,20 @@ SLOTS = (
     ("pad_end",),
     ("shear02", "v_sc0"),
     ("shear03", "w11"),
-    ("tab1",),
-    ("shear10", "w10", "w21"),
-    ("tab0", "w20", "shear12"),
-    ("w00", "w01", "src0"),
+    ("tab1", "w01"),
+    ("shear10", "shear12"),
+    ("tab0", "shear11"),
+    ("w00", "src0"),
     ("tab2", "shear13"),
-    ("shear11",),
-    ("src1",),
+    ("w10", "w21"),
+    ("w20", "src1"),
     ("damp0",),
     ("damp0_end",),
     ("damp1",),
     ("damp1_end",),
     ("staging",),
     ("staging2",),
+    ("staging3",),
     ("tail",),
 )
 BANK = 2048
@@ -167,14 +168,13 @@ def tile_list_wall_model_adjoint_kernel(
             w1_words[a, b] = words
             nc.vector.quantize_mx(out=words[:].bitcast(E4M3), scales=w1_sc[a, b][:], in_=w1_rounded[a, b][:])
 
-        def shear_tile(b, t, by_halves=False):
+        def shear_window(b, t):
             window = placed([P, T], F32, f"shear{b}{t}", at[f"shear{b}{t}"])
             nc.sync.dma_start(out=window[:], in_=shear_rows[b, t])
-            if by_halves:
-                for u in range(HALVES):
-                    nc.vector.tensor_copy(out=damp_half(b, u, t), in_=window[:].indirect(half_of(idx, u)))
-            else:
-                nc.vector.tensor_copy(out=damp[b][:, t, :], in_=window[:].indirect(idx[:]))
+            return window
+
+        def shear_tile(b, t):
+            nc.vector.tensor_copy(out=damp[b][:, t, :], in_=shear_window(b, t)[:].indirect(idx[:]))
 
         def hidden_codes(b, u, copy, woven, words):
             h_words[b, u] = words
@@ -244,15 +244,23 @@ def tile_list_wall_model_adjoint_kernel(
                 )
             nc.vector.tensor_tensor(out=h_rows[b, u][:, t, :], in0=acc[:], in1=factor[b, u, t], op=ALU.mult)
 
-        def damp_row(b, u, t, scratch_at=None, stay=False):
-            row = damp_half(b, u, t)
+        def damp_row(b, u, t, scratch_at=None, stay_at=None, row=None, squared=False):
+            if row is None:
+                row = damp_half(b, u, t)
             scratch = row
             if scratch_at is not None:
                 scratch = placed([P, HALF], F32, f"scratch{b}{u}{t}", scratch_at)[:]
-            nc.scalar.activation(out=scratch, in_=row, func=ACT.Square)
-            nc.scalar.activation(out=scratch, in_=scratch, func=ACT.Abs_reciprocal_sqrt, bias=1.0)
-            factor[b, u, t] = scratch if stay else row
+            if not squared:
+                nc.scalar.activation(out=scratch, in_=row, func=ACT.Square)
+            nc.scalar.activation(out=scratch, in_=row if squared else scratch, func=ACT.Abs_reciprocal_sqrt, bias=1.0)
+            factor[b, u, t] = row
+            if stay_at is not None:
+                factor[b, u, t] = placed([P, HALF], F32, f"factor{b}{u}{t}", stay_at)[:]
             nc.scalar.activation(out=factor[b, u, t], in_=scratch, func=ACT.Square)
+
+        def square(b, t):
+            row = damp[b][:, t, :]
+            nc.gpsimd.tensor_tensor(out=row, in0=row, in1=row, op=ALU.mult)
 
         def gpsimd_weave(b, u, woven):
             gpsimd_copy(
@@ -273,7 +281,7 @@ def tile_list_wall_model_adjoint_kernel(
             pages[m] = placed([P, T2], F32, f"page{m}", at["shear00"] - SLOT // 2 + SLOT * (m - 1))
             nc.gpsimd.memset(pages[m][:], 0.0)
 
-        third, fourth = at["staging2"], at["staging2"] + ROWS_BYTES
+        third, fourth = at["staging2"], at["staging3"] + WORDS_BYTES
         for t in range(PACK):
             shear_tile(0, t)
             if t == 0:
@@ -286,11 +294,12 @@ def tile_list_wall_model_adjoint_kernel(
             if t < PACK - 1:
                 for u in range(HALVES):
                     damp_row(0, u, t)
+        square(0, PACK - 1)
         shear_tile(1, 0)
         table_pass(0)
         weight_piece(0, 0, nc.scalar.copy, first)
         for u in range(HALVES):
-            damp_row(0, u, PACK - 1, at["w00"] + WORDS_BYTES * u)
+            damp_row(0, u, PACK - 1, at["w00"] + WORDS_BYTES * u, squared=True)
         weight_codes(0, 0, codes_tile(0, 0))
         table_pass(1)
         weight_piece(1, 0, nc.scalar.copy, second)
@@ -300,30 +309,32 @@ def tile_list_wall_model_adjoint_kernel(
         weight_codes(1, 0, placed([P, PASS], U32, "w1_words10", at["w20"]))
         weight_codes(2, 0, codes_tile(2, 0))
         table_pass(2, True)
+        weight_piece(0, 1, nc.scalar.copy, first)
+        shear_tile(1, 1)
+        weight_codes(0, 1, placed([P, PASS], U32, "w1_words01", at["shear11"]))
         for u in range(HALVES):
             h_rows[0, u] = kept([P, PACK, HALF], BF16, f"h_rows0{u}")
             for t in range(PACK):
                 hidden_row(0, u, t)
-        woven00 = placed([P, HALF * PACK], BF16, "woven00", second)
+        woven00 = placed([P, HALF * PACK], BF16, "woven00", third)
         gpsimd_weave(0, 0, woven00[:])
-        weight_piece(0, 1, nc.scalar.copy, first)
-        shear_tile(1, 1)
-        weight_codes(0, 1, codes_tile(0, 1))
+        weight_piece(1, 1, nc.scalar.copy, second)
+        weight_codes(1, 1, placed([P, PASS], U32, "w1_words11", at["shear11"] + 2 * WORDS_BYTES))
         quantise_hidden(0, 0, woven00, at["shear11"] + WORDS_BYTES)
-        weight_piece(1, 1, nc.scalar.copy, third)
-        weight_codes(1, 1, codes_tile(1, 1))
-        woven01 = placed([P, HALF * PACK], BF16, "woven01", second + ROWS_BYTES // 2)
-        gpsimd_weave(0, 1, woven01[:])
         weight_piece(2, 1, nc.scalar.copy, fourth)
-        for u in range(HALVES):
-            damp_row(1, u, 1, at["w21"] + WORDS_BYTES * u)
+        damp_row(1, 0, 1, at["w21"] + WORDS_BYTES * 3)
         shear_tile(1, 2)
         weight_codes(2, 1, placed([P, PASS], U32, "w1_words21", at["shear12"]))
+        woven01 = placed([P, HALF * PACK], BF16, "woven01", fourth)
+        gpsimd_weave(0, 1, woven01[:])
         damp_row(1, 0, 2)
-        shear_tile(1, 3, True)
-        damp_row(1, 0, 3, at["w11"], True)
-        damp_row(1, 1, 2, at["w21"])
-        damp_row(1, 1, 3, at["w21"] + WORDS_BYTES)
+        window = shear_window(1, 3)
+        for u in range(HALVES):
+            nc.vector.tensor_copy(out=damp_half(1, u, 3), in_=window[:].indirect(half_of(idx, u)))
+        damp_row(1, 0, 3, at["w21"] + WORDS_BYTES, at["w11"])
+        damp_row(1, 1, 1, at["w21"] + WORDS_BYTES - WORDS_BYTES // 2)
+        damp_row(1, 1, 2, at["w21"] + WORDS_BYTES + WORDS_BYTES // 2)
+        damp_row(1, 1, 3, at["w21"] + WORDS_BYTES - WORDS_BYTES // 2)
 
         nc.sync.dma_start(out=w2_w[:].bitcast(I32), in_=w2_words.rearrange("b p c i -> p b (c i)").bitcast(I32))
         for q in range(P // QUADRANT):
@@ -355,7 +366,7 @@ def tile_list_wall_model_adjoint_kernel(
         woven11 = placed([P, HALF * PACK], BF16, "woven11", at["w11"] + ROWS_BYTES)
         hidden_codes(1, 1, nc.scalar.copy, woven11[:], placed([P, HALF], U32, "h_words11", at["damp0"] + WORDS_BYTES))
         result(2, 0, ring_at, at["w21"] + WORDS_BYTES, at["w11"])
-        result(3, 0, ring_at, None, at["w11"] + ROWS_BYTES)
+        result(3, 0, ring_at, at["w21"], at["w11"] + ROWS_BYTES)
         for m in range(PAGES):
             result(m, 1, ring_at)
             nc.sync.dma_start(out=out[P * m : P * (m + 1), :], in_=pages[m][:])

@@ -82,6 +82,9 @@ def tile_list_wall_model_adjoint_kernel(
 
         idx = keep.tile([P, S // 16], U16, name="idx")
         idx2 = keep.tile([P, S // 16], U16, name="idx2")
+        shear_rows = sT.rearrange("(b p t) c -> b t p c", b=R_PASSES, t=PACK)
+        first_window = placed([P, T], F32, "shear00", at["shear00"])
+        nc.sync.dma_start(out=first_window[:], in_=shear_rows[0, 0])
         nc.sync.dma_start(idx[:], offs)
 
         tab_sc = kept([P, T], U8, "tab_sc")
@@ -122,7 +125,6 @@ def tile_list_wall_model_adjoint_kernel(
         w2_w = kept([P, R_PASSES, N], U32, "w2_w")
         wgo_sb = keep.tile([P, S], F32, name="wgo_sb")
         src_sb = {}
-        shear_rows = sT.rearrange("(b p t) c -> b t p c", b=R_PASSES, t=PACK)
 
         def half_of(offsets, u):
             return offsets[:, HALF_COLS * u : HALF_COLS * (u + 1)]
@@ -169,6 +171,8 @@ def tile_list_wall_model_adjoint_kernel(
             nc.vector.quantize_mx(out=words[:].bitcast(E4M3), scales=w1_sc[a, b][:], in_=w1_rounded[a, b][:])
 
         def shear_window(b, t):
+            if (b, t) == (0, 0):
+                return first_window
             window = placed([P, T], F32, f"shear{b}{t}", at[f"shear{b}{t}"])
             nc.sync.dma_start(out=window[:], in_=shear_rows[b, t])
             return window

@@ -34,19 +34,18 @@ ROWS_BYTES = PACK * HALF * 2
 WORDS_BYTES = PASS * 4
 
 SLOTS = (
-    ("pad",),
-    ("shear00",),
-    ("shear01",),
-    ("pad_end",),
+    ("shear00", "page1"),
+    ("shear01", "shear13"),
     ("shear02", "v_sc0"),
     ("shear03", "w11"),
     ("tab1", "w01"),
     ("shear10", "shear12"),
     ("tab0", "shear11"),
     ("w00", "src0"),
-    ("tab2", "shear13"),
+    ("tab2", "page3"),
     ("w10", "w21"),
     ("w20", "src1"),
+    ("rounded20", "page2"),
     ("damp0",),
     ("damp0_end",),
     ("damp1",),
@@ -233,18 +232,18 @@ def tile_list_wall_model_adjoint_kernel(
         def gpsimd_copy(out, in_):
             nc.gpsimd.tensor_scalar(out=out, in0=in_, scalar1=1.0, scalar2=0.0, op0=ALU.mult, op1=ALU.add)
 
-        def hidden_row(b, u, t):
+        def hidden_row(b, u, t, passes=(0, 1, 2)):
             cols = slice(HALF * u, HALF * (u + 1))
             acc = bank(f"acc{b}{u}{t}", PACK * u + t)
-            for a in range(K_PASSES):
+            for a in passes:
                 nc.tensor.matmul_mx(
                     out=acc[:],
                     lhsT=w1_words[a, b][:, P * t : P * (t + 1)].bitcast(E4M3),
                     lhsT_scale=w1_sc[a, b][:, P * t : P * (t + 1)],
                     rhs=v_words[a][:, cols].bitcast(E5M2),
                     rhs_scale=v_sc[a][:, cols],
-                    start=(a == 0),
-                    stop=(a == K_PASSES - 1),
+                    start=(a == passes[0]),
+                    stop=(a == passes[-1]),
                 )
             nc.vector.tensor_tensor(out=h_rows[b, u][:, t, :], in0=acc[:], in1=factor[b, u, t], op=ALU.mult)
 
@@ -266,6 +265,12 @@ def tile_list_wall_model_adjoint_kernel(
             row = damp[b][:, t, :]
             nc.gpsimd.tensor_tensor(out=row, in0=row, in1=row, op=ALU.mult)
 
+        def square_half(t, offset):
+            row = damp_half(1, 1, t)
+            squared = placed([P, HALF], F32, f"squared{t}", offset)
+            nc.gpsimd.tensor_tensor(out=squared[:], in0=row, in1=row, op=ALU.mult)
+            return squared[:]
+
         def gpsimd_weave(b, u, woven):
             gpsimd_copy(
                 out=woven.rearrange("p (j t) -> p j t", t=PACK),
@@ -282,37 +287,39 @@ def tile_list_wall_model_adjoint_kernel(
             nc.vector.quantize_mx(out=h_words[b, u][:].bitcast(E4M3), scales=h_sc[b, u][:], in_=woven[:])
 
         def clear_page(m):
-            pages[m] = placed([P, T2], F32, f"page{m}", at["shear00"] - SLOT // 2 + SLOT * (m - 1))
+            pages[m] = placed([P, T2], F32, f"page{m}", at[f"page{m}"])
             nc.gpsimd.memset(pages[m][:], 0.0)
 
         third, fourth = at["staging2"], at["staging3"] + WORDS_BYTES
-        for t in range(PACK):
+        shear_tile(0, 0)
+        clear_page(1)
+        for u in range(HALVES):
+            damp_row(0, u, 0)
+        for t in range(1, PACK):
             shear_tile(0, t)
-            if t == 0:
-                clear_page(1)
-            if t == 1:
-                clear_page(2)
-                clear_page(3)
+            square(0, t)
             if t == 2:
                 gather_scales()
             if t < PACK - 1:
                 for u in range(HALVES):
-                    damp_row(0, u, t)
-        square(0, PACK - 1)
+                    damp_row(0, u, t, squared=True)
         shear_tile(1, 0)
+        square(1, 0)
         table_pass(0)
         weight_piece(0, 0, nc.scalar.copy, first)
-        for u in range(HALVES):
-            damp_row(0, u, PACK - 1, at["w00"] + WORDS_BYTES * u, squared=True)
         weight_codes(0, 0, codes_tile(0, 0))
         table_pass(1)
         weight_piece(1, 0, nc.scalar.copy, second)
         for u in range(HALVES):
-            damp_row(1, u, 0, at["w10"] + WORDS_BYTES * u)
-        weight_piece(2, 0, nc.vector.tensor_copy, third)
+            damp_row(0, u, PACK - 1, at["w10"] + WORDS_BYTES * u, squared=True)
+        for u in range(HALVES):
+            damp_row(1, u, 0, at["w10"] + WORDS_BYTES * (2 + u), squared=True)
+        weight_piece(2, 0, nc.vector.tensor_copy, at["rounded20"])
         weight_codes(1, 0, placed([P, PASS], U32, "w1_words10", at["w20"]))
         weight_codes(2, 0, codes_tile(2, 0))
+        clear_page(2)
         table_pass(2, True)
+        clear_page(3)
         weight_piece(0, 1, nc.scalar.copy, first)
         shear_tile(1, 1)
         weight_codes(0, 1, placed([P, PASS], U32, "w1_words01", at["shear11"]))
@@ -325,19 +332,30 @@ def tile_list_wall_model_adjoint_kernel(
         weight_piece(1, 1, nc.scalar.copy, second)
         weight_codes(1, 1, placed([P, PASS], U32, "w1_words11", at["shear11"] + 2 * WORDS_BYTES))
         quantise_hidden(0, 0, woven00, at["shear11"] + WORDS_BYTES)
+        squares = {1: square_half(1, second)}
         weight_piece(2, 1, nc.scalar.copy, fourth)
         damp_row(1, 0, 1, at["w21"] + WORDS_BYTES * 3)
         shear_tile(1, 2)
         weight_codes(2, 1, placed([P, PASS], U32, "w1_words21", at["shear12"]))
-        woven01 = placed([P, HALF * PACK], BF16, "woven01", fourth)
+        squares[2] = square_half(2, fourth - WORDS_BYTES // 2)
+        woven01 = placed([P, HALF * PACK], BF16, "woven01", fourth + WORDS_BYTES // 2)
         gpsimd_weave(0, 1, woven01[:])
         damp_row(1, 0, 2)
         window = shear_window(1, 3)
         for u in range(HALVES):
             nc.vector.tensor_copy(out=damp_half(1, u, 3), in_=window[:].indirect(half_of(idx, u)))
-        damp_row(1, 0, 3, at["w21"] + WORDS_BYTES, at["w11"])
-        damp_row(1, 1, 1, at["w21"] + WORDS_BYTES - WORDS_BYTES // 2)
-        damp_row(1, 1, 2, at["w21"] + WORDS_BYTES + WORDS_BYTES // 2)
+        row = damp_half(1, 0, 3)
+        scratch = placed([P, HALF], F32, "scratch103", at["w21"] + WORDS_BYTES)
+        factor[1, 0, 3] = placed([P, HALF], F32, "factor103", at["w11"])[:]
+        parts = [slice(HALF // 2 * c, HALF // 2 * (c + 1)) for c in range(2)]
+        for part in parts:
+            nc.scalar.activation(out=scratch[:, part], in_=row[:, part], func=ACT.Square)
+        for part in parts:
+            nc.scalar.activation(out=scratch[:, part], in_=scratch[:, part], func=ACT.Abs_reciprocal_sqrt, bias=1.0)
+        for part in parts:
+            nc.scalar.activation(out=factor[1, 0, 3][:, part], in_=scratch[:, part], func=ACT.Square)
+        damp_row(1, 1, 1, at["w21"] + WORDS_BYTES - WORDS_BYTES // 2, row=squares[1], squared=True)
+        damp_row(1, 1, 2, at["w21"] + WORDS_BYTES + WORDS_BYTES // 2, row=squares[2], squared=True)
         damp_row(1, 1, 3, at["w21"] + WORDS_BYTES - WORDS_BYTES // 2)
 
         nc.sync.dma_start(out=w2_w[:].bitcast(I32), in_=w2_words.rearrange("b p c i -> p b (c i)").bitcast(I32))
@@ -365,7 +383,7 @@ def tile_list_wall_model_adjoint_kernel(
             weigh_and_scatter(m, 0, diff[:], weighted[:], nc.gpsimd)
         h_rows[1, 1] = placed([P, PACK, HALF], BF16, "h_rows11", at["w11"])
         for t in range(PACK):
-            hidden_row(1, 1, t)
+            hidden_row(1, 1, t, (2, 1, 0))
         ring_at = at["tail"] + WORDS_BYTES
         woven11 = placed([P, HALF * PACK], BF16, "woven11", at["w11"] + ROWS_BYTES)
         hidden_codes(1, 1, nc.scalar.copy, woven11[:], placed([P, HALF], U32, "h_words11", at["damp0"] + WORDS_BYTES))

@@ -26,12 +26,14 @@ HALF = 512
 HALVES = S // HALF
 HALF_COLS = HALF // 16
 QUADRANT = 32
-MOVED_ROWS = 112
+MOVED_ROWS = 3 * QUADRANT + 4
+FIRST_RESULTS = 2
 RUN = 4
 
 SLOT = 8192
-ROWS_BYTES = PACK * HALF * 2
-WORDS_BYTES = PASS * 4
+ROWS = PACK * HALF * 2
+ROW = HALF * 4
+BANK = 2048
 
 SLOTS = (
     ("shear00", "page1"),
@@ -47,15 +49,14 @@ SLOTS = (
     ("w20", "src1"),
     ("rounded20", "page2"),
     ("damp0",),
-    ("damp0_end",),
+    ("damp0_second_half",),
     ("damp1",),
-    ("damp1_end",),
-    ("staging",),
-    ("staging2",),
-    ("staging3",),
-    ("tail",),
+    ("damp1_second_half",),
+    ("stage_a",),
+    ("stage_b",),
+    ("stage_c",),
+    ("diffs",),
 )
-BANK = 2048
 
 
 def tile_list_wall_model_adjoint_kernel(
@@ -65,7 +66,6 @@ def tile_list_wall_model_adjoint_kernel(
     with ExitStack() as ctx:
         keep = ctx.enter_context(tc.tile_pool(name="keep", bufs=1))
         arena = ctx.enter_context(tc.tile_pool(name="arena", bufs=1))
-        ring = ctx.enter_context(tc.tile_pool(name="ring", bufs=2))
         psum = ctx.enter_context(tc.psum_pool(name="psum", bufs=1))
 
         at = {name: SLOT * i for i, names in enumerate(SLOTS) for name in names}
@@ -73,17 +73,22 @@ def tile_list_wall_model_adjoint_kernel(
         def placed(shape, dtype, name, offset):
             return arena.tile(shape, dtype, name=name, offset=offset, align_bytes=64)
 
-        def bank(name, number):
-            return psum.tile([P, HALF], F32, name=name, offset=BANK * number)
-
         def kept(shape, dtype, name):
             return keep.tile(shape, dtype, name=name, align_bytes=64)
 
+        def bank(name, number):
+            return psum.tile([P, HALF], F32, name=name, offset=BANK * number)
+
+        shear_rows = sT.rearrange("(b p t) c -> b t p c", b=R_PASSES, t=PACK)
+
+        def shear_window(b, t):
+            window = placed([P, T], F32, f"shear{b}{t}", at[f"shear{b}{t}"])
+            nc.sync.dma_start(out=window[:], in_=shear_rows[b, t])
+            return window
+
         idx = keep.tile([P, S // 16], U16, name="idx")
         idx2 = keep.tile([P, S // 16], U16, name="idx2")
-        shear_rows = sT.rearrange("(b p t) c -> b t p c", b=R_PASSES, t=PACK)
-        first_window = placed([P, T], F32, "shear00", at["shear00"])
-        nc.sync.dma_start(out=first_window[:], in_=shear_rows[0, 0])
+        first_window = shear_window(0, 0)
         nc.sync.dma_start(idx[:], offs)
 
         tab_sc = kept([P, T], U8, "tab_sc")
@@ -101,105 +106,143 @@ def tile_list_wall_model_adjoint_kernel(
             v_sc[a] = kept([P, S], U8, f"v_sc{a}")
             nc.vector.memset(v_sc[a][:].bitcast(I32), 0)
 
-        pages = {}
-        pages[0] = keep.tile([P, T2], F32, name="page0")
+        pages = {0: keep.tile([P, T2], F32, name="page0")}
         nc.vector.memset(pages[0][:], 0.0)
 
         v_words = [kept([P, S], U32, f"v_words{a}") for a in range(K_PASSES)]
-        w1_rounded = {}
-        w1_words = {}
-        w1_sc = {}
-        for a in range(K_PASSES):
-            for b in range(R_PASSES):
-                w1_sc[a, b] = kept([P, PASS], U8, f"w1_sc{a}{b}")
-        damp = {}
-        factor = {}
-        h_rows = {}
-        h_words = {}
+        w1_sc = {(a, b): kept([P, PASS], U8, f"w1_sc{a}{b}") for a in range(K_PASSES) for b in range(R_PASSES)}
+        shears = {}
         h_sc = {}
         for b in range(R_PASSES):
-            damp[b] = placed([P, PACK, S], F32, f"damp{b}", at[f"damp{b}"])
+            shears[b] = placed([P, PACK, S], F32, f"damp{b}", at[f"damp{b}"])
             for u in range(HALVES):
                 h_sc[b, u] = kept([P, HALF], U8, f"h_sc{b}{u}")
         w2_w = kept([P, R_PASSES, N], U32, "w2_w")
         wgo_sb = keep.tile([P, S], F32, name="wgo_sb")
+        w1_rounded = {}
+        w1_words = {}
+        damping = {}
+        h_rows = {}
+        h_words = {}
         src_sb = {}
+
+        def half(u):
+            return slice(HALF * u, HALF * (u + 1))
 
         def half_of(offsets, u):
             return offsets[:, HALF_COLS * u : HALF_COLS * (u + 1)]
 
-        def damp_half(b, u, t):
-            return damp[b][:, t, HALF * u : HALF * (u + 1)]
+        def gather(out, window, offsets):
+            nc.vector.tensor_copy(out=out, in_=window[:].indirect(offsets))
+
+        def clear_page(m):
+            pages[m] = placed([P, T2], F32, f"page{m}", at[f"page{m}"])
+            nc.gpsimd.memset(pages[m][:], 0.0)
 
         def gather_scales():
             v_sc[0] = placed([P, S], U8, "v_sc0", at["v_sc0"])
-            nc.vector.tensor_copy(out=v_sc[0][:], in_=tab_sc[:].indirect(idx[:]))
+            gather(v_sc[0][:], tab_sc, idx[:])
             for a in range(1, K_PASSES):
                 nc.gpsimd.dma_start(
                     out=v_sc[a][0:MOVED_ROWS, :].bitcast(I32),
                     in_=v_sc[0][4 * a : 4 * a + MOVED_ROWS, :].bitcast(I32),
                 )
 
-        def table_pass(a, by_halves=False):
+        def table_window(a):
             window = placed([P, T], U32, f"tab{a}", at[f"tab{a}"])
             nc.sync.dma_start(
                 out=window[:].bitcast(I32),
                 in_=tab_words[a].rearrange("p t i -> p (t i)").bitcast(I32),
             )
-            if by_halves:
-                for u in range(HALVES):
-                    nc.vector.tensor_copy(
-                        out=v_words[a][:, HALF * u : HALF * (u + 1)], in_=window[:].indirect(half_of(idx, u))
-                    )
-            else:
-                nc.vector.tensor_copy(out=v_words[a][:], in_=window[:].indirect(idx[:]))
+            return window
 
-        def weight_piece(a, b, copy, offset, walk="p m i t"):
+        def weight_piece(a, b, copy, offset):
             raw = placed([P, PACK, PASS], F32, f"w{a}{b}", at[f"w{a}{b}"])
             piece = w1[PASS * a : PASS * (a + 1), PASS * b : PASS * (b + 1)]
             nc.sync.dma_start(out=raw[:], in_=piece.rearrange("(p i) c -> p i c", i=PACK))
-            rounded = placed([P, PACK * PASS], BF16, f"rounded{a}{b}", offset)
+            w1_rounded[a, b] = placed([P, PACK * PASS], BF16, f"rounded{a}{b}", offset)
             copy(
-                out=rounded[:].rearrange("p (t m i) -> " + walk, t=PACK, i=PACK),
-                in_=raw[:].rearrange("p i (m t) -> " + walk, t=PACK),
+                out=w1_rounded[a, b][:].rearrange("p (t m i) -> p m i t", t=PACK, i=PACK),
+                in_=raw[:].rearrange("p i (m t) -> p m i t", t=PACK),
             )
-            w1_rounded[a, b] = rounded
 
-        def weight_codes(a, b, words):
-            w1_words[a, b] = words
-            nc.vector.quantize_mx(out=words[:].bitcast(E4M3), scales=w1_sc[a, b][:], in_=w1_rounded[a, b][:])
+        def words_tile(name, offset):
+            if offset is None:
+                return kept([P, HALF], U32, name)
+            return placed([P, HALF], U32, name, offset)
 
-        def shear_window(b, t):
-            if (b, t) == (0, 0):
-                return first_window
-            window = placed([P, T], F32, f"shear{b}{t}", at[f"shear{b}{t}"])
-            nc.sync.dma_start(out=window[:], in_=shear_rows[b, t])
-            return window
+        def weight_codes(a, b, offset=None):
+            w1_words[a, b] = words_tile(f"w1_words{a}{b}", offset)
+            nc.vector.quantize_mx(
+                out=w1_words[a, b][:].bitcast(E4M3), scales=w1_sc[a, b][:], in_=w1_rounded[a, b][:]
+            )
 
-        def shear_tile(b, t):
-            nc.vector.tensor_copy(out=damp[b][:, t, :], in_=shear_window(b, t)[:].indirect(idx[:]))
+        def square(out, row):
+            nc.gpsimd.tensor_tensor(out=out, in0=row, in1=row, op=ALU.mult)
 
-        def hidden_codes(b, u, copy, woven, words):
-            h_words[b, u] = words
+        def damp(b, u, t, scratch_at=None, squares=None, into=None, parts=1):
+            row = shears[b][:, t, half(u)] if squares is None else squares
+            scratch = row if scratch_at is None else placed([P, HALF], F32, f"scratch{b}{u}{t}", scratch_at)[:]
+            damping[b, u, t] = row if into is None else into
+            cuts = [slice(HALF // parts * c, HALF // parts * (c + 1)) for c in range(parts)]
+            if squares is None:
+                for cut in cuts:
+                    nc.scalar.activation(out=scratch[:, cut], in_=row[:, cut], func=ACT.Square)
+                squares = scratch
+            for cut in cuts:
+                nc.scalar.activation(
+                    out=scratch[:, cut], in_=squares[:, cut], func=ACT.Abs_reciprocal_sqrt, bias=1.0
+                )
+            for cut in cuts:
+                nc.scalar.activation(out=damping[b, u, t][:, cut], in_=scratch[:, cut], func=ACT.Square)
+
+        def hidden_rows(b, u):
+            passes = (2, 1, 0) if (b, u) == (1, 1) else (0, 1, 2)
+            for t in range(PACK):
+                acc = bank(f"acc{b}{u}{t}", PACK * u + t)
+                for a in passes:
+                    nc.tensor.matmul_mx(
+                        out=acc[:],
+                        lhsT=w1_words[a, b][:, P * t : P * (t + 1)].bitcast(E4M3),
+                        lhsT_scale=w1_sc[a, b][:, P * t : P * (t + 1)],
+                        rhs=v_words[a][:, half(u)].bitcast(E5M2),
+                        rhs_scale=v_sc[a][:, half(u)],
+                        start=(a == passes[0]),
+                        stop=(a == passes[-1]),
+                    )
+                nc.vector.tensor_tensor(out=h_rows[b, u][:, t, :], in0=acc[:], in1=damping[b, u, t], op=ALU.mult)
+
+        def weave(b, u, offset, copy):
+            woven = placed([P, HALF * PACK], BF16, f"woven{b}{u}", offset)
             copy(
-                out=woven.rearrange("p (c i t) -> p c t i", i=RUN, t=PACK),
+                out=woven[:].rearrange("p (c i t) -> p c t i", i=RUN, t=PACK),
                 in_=h_rows[b, u][:].rearrange("p t (c i) -> p c t i", i=RUN),
             )
-            nc.vector.quantize_mx(out=words[:].bitcast(E4M3), scales=h_sc[b, u][:], in_=woven)
+            return woven
 
-        def woven_tile():
-            woven = ring.tile([P, HALF * PACK], BF16, name="woven", align_bytes=64)
-            return woven[:]
+        def weave_on_gpsimd(b, u, offset):
+            woven = placed([P, HALF * PACK], BF16, f"woven{b}{u}", offset)
+            nc.gpsimd.tensor_scalar(
+                out=woven[:].rearrange("p (j t) -> p j t", t=PACK),
+                in0=h_rows[b, u][:].rearrange("p t j -> p j t"),
+                scalar1=1.0,
+                scalar2=0.0,
+                op0=ALU.mult,
+                op1=ALU.add,
+            )
+            return woven
+
+        def hidden_codes(b, u, woven, offset=None):
+            h_words[b, u] = words_tile(f"h_words{b}{u}", offset)
+            nc.vector.quantize_mx(out=h_words[b, u][:].bitcast(E4M3), scales=h_sc[b, u][:], in_=woven[:])
 
         def load_src(u):
             src_sb[u] = placed([P, PAGES, HALF], F32, f"src{u}", at[f"src{u}"])
-            nc.sync.dma_start(
-                out=src_sb[u][:], in_=src[:, HALF * u : HALF * (u + 1)].rearrange("(m p) j -> p m j", p=P)
-            )
+            nc.sync.dma_start(out=src_sb[u][:], in_=src[:, half(u)].rearrange("(m p) j -> p m j", p=P))
 
-        def product(m, u, number):
+        def product(m, u):
             rows = slice(P * m, P * (m + 1))
-            y = bank(f"y{m}{u}", number)
+            y = bank(f"y{m}{u}", m)
             for b in range(R_PASSES):
                 nc.tensor.matmul_mx(
                     out=y[:],
@@ -212,151 +255,87 @@ def tile_list_wall_model_adjoint_kernel(
                 )
             return y
 
-        def weigh_and_scatter(m, u, diff, weighted, engine):
-            engine.tensor_tensor(out=weighted, in0=diff, in1=wgo_sb[:, HALF * u : HALF * (u + 1)], op=ALU.mult)
-            nc.vector.tensor_copy(out=pages[m][:].indirect(half_of(idx2, u)), in_=weighted)
+        def weigh_and_scatter(m, u, diff, weighted):
+            nc.gpsimd.tensor_tensor(out=weighted[:], in0=diff[:], in1=wgo_sb[:, half(u)], op=ALU.mult)
+            nc.vector.tensor_copy(out=pages[m][:].indirect(half_of(idx2, u)), in_=weighted[:])
 
-        def result(m, u, diff_at, values_at=None, weighted_at=None):
-            y = product(m, u, m)
-            if values_at is None:
-                values_at = at["damp0"] + WORDS_BYTES * (PAGES * u + m)
+        def result_on_vector(m, u, diff_at, weighted_at):
+            y = product(m, u)
+            diff = placed([P, HALF], F32, f"diff{m}{u}", diff_at)
+            nc.vector.tensor_tensor(out=diff[:], in0=y[:], in1=src_sb[u][:, m, :], op=ALU.subtract)
+            weigh_and_scatter(m, u, diff, placed([P, HALF], F32, f"weighted{m}{u}", weighted_at))
+
+        def result(m, u, values_at, diff_at, weighted_at=None):
+            y = product(m, u)
             values = placed([P, HALF], F32, f"values{m}{u}", values_at)
             nc.scalar.copy(out=values[:], in_=y[:])
             diff = placed([P, HALF], F32, f"diff{m}{u}", diff_at)
             nc.gpsimd.tensor_tensor(out=diff[:], in0=values[:], in1=src_sb[u][:, m, :], op=ALU.subtract)
-            weighted = values
-            if weighted_at is not None:
-                weighted = placed([P, HALF], F32, f"weighted{m}{u}", weighted_at)
-            weigh_and_scatter(m, u, diff[:], weighted[:], nc.gpsimd)
+            weighted = values if weighted_at is None else placed([P, HALF], F32, f"weighted{m}{u}", weighted_at)
+            weigh_and_scatter(m, u, diff, weighted)
 
-        def gpsimd_copy(out, in_):
-            nc.gpsimd.tensor_scalar(out=out, in0=in_, scalar1=1.0, scalar2=0.0, op0=ALU.mult, op1=ALU.add)
-
-        def hidden_row(b, u, t, passes=(0, 1, 2)):
-            cols = slice(HALF * u, HALF * (u + 1))
-            acc = bank(f"acc{b}{u}{t}", PACK * u + t)
-            for a in passes:
-                nc.tensor.matmul_mx(
-                    out=acc[:],
-                    lhsT=w1_words[a, b][:, P * t : P * (t + 1)].bitcast(E4M3),
-                    lhsT_scale=w1_sc[a, b][:, P * t : P * (t + 1)],
-                    rhs=v_words[a][:, cols].bitcast(E5M2),
-                    rhs_scale=v_sc[a][:, cols],
-                    start=(a == passes[0]),
-                    stop=(a == passes[-1]),
-                )
-            nc.vector.tensor_tensor(out=h_rows[b, u][:, t, :], in0=acc[:], in1=factor[b, u, t], op=ALU.mult)
-
-        def damp_row(b, u, t, scratch_at=None, stay_at=None, row=None, squared=False):
-            if row is None:
-                row = damp_half(b, u, t)
-            scratch = row
-            if scratch_at is not None:
-                scratch = placed([P, HALF], F32, f"scratch{b}{u}{t}", scratch_at)[:]
-            if not squared:
-                nc.scalar.activation(out=scratch, in_=row, func=ACT.Square)
-            nc.scalar.activation(out=scratch, in_=row if squared else scratch, func=ACT.Abs_reciprocal_sqrt, bias=1.0)
-            factor[b, u, t] = row
-            if stay_at is not None:
-                factor[b, u, t] = placed([P, HALF], F32, f"factor{b}{u}{t}", stay_at)[:]
-            nc.scalar.activation(out=factor[b, u, t], in_=scratch, func=ACT.Square)
-
-        def square(b, t):
-            row = damp[b][:, t, :]
-            nc.gpsimd.tensor_tensor(out=row, in0=row, in1=row, op=ALU.mult)
-
-        def square_half(t, offset):
-            row = damp_half(1, 1, t)
-            squared = placed([P, HALF], F32, f"squared{t}", offset)
-            nc.gpsimd.tensor_tensor(out=squared[:], in0=row, in1=row, op=ALU.mult)
-            return squared[:]
-
-        def gpsimd_weave(b, u, woven):
-            gpsimd_copy(
-                out=woven.rearrange("p (j t) -> p j t", t=PACK),
-                in_=h_rows[b, u][:].rearrange("p t j -> p j t"),
-            )
-
-        def codes_tile(a, b):
-            return kept([P, PASS], U32, f"w1_words{a}{b}")
-
-        first, second = at["staging"], at["staging"] + ROWS_BYTES
-
-        def quantise_hidden(b, u, woven, offset):
-            h_words[b, u] = placed([P, HALF], U32, f"h_words{b}{u}", offset)
-            nc.vector.quantize_mx(out=h_words[b, u][:].bitcast(E4M3), scales=h_sc[b, u][:], in_=woven[:])
-
-        def clear_page(m):
-            pages[m] = placed([P, T2], F32, f"page{m}", at[f"page{m}"])
-            nc.gpsimd.memset(pages[m][:], 0.0)
-
-        third, fourth = at["staging2"], at["staging3"] + WORDS_BYTES
-        shear_tile(0, 0)
+        gather(shears[0][:, 0, :], first_window, idx[:])
         clear_page(1)
         for u in range(HALVES):
-            damp_row(0, u, 0)
+            damp(0, u, 0)
         for t in range(1, PACK):
-            shear_tile(0, t)
-            square(0, t)
-            if t == 2:
+            gather(shears[0][:, t, :], shear_window(0, t), idx[:])
+            square(shears[0][:, t, :], shears[0][:, t, :])
+            if t == PACK - 2:
                 gather_scales()
             if t < PACK - 1:
                 for u in range(HALVES):
-                    damp_row(0, u, t, squared=True)
-        shear_tile(1, 0)
-        square(1, 0)
-        table_pass(0)
-        weight_piece(0, 0, nc.scalar.copy, first)
-        weight_codes(0, 0, codes_tile(0, 0))
-        table_pass(1)
-        weight_piece(1, 0, nc.scalar.copy, second)
-        for u in range(HALVES):
-            damp_row(0, u, PACK - 1, at["w10"] + WORDS_BYTES * u, squared=True)
-        for u in range(HALVES):
-            damp_row(1, u, 0, at["w10"] + WORDS_BYTES * (2 + u), squared=True)
+                    damp(0, u, t, squares=shears[0][:, t, half(u)])
+        gather(shears[1][:, 0, :], shear_window(1, 0), idx[:])
+        square(shears[1][:, 0, :], shears[1][:, 0, :])
+
+        gather(v_words[0][:], table_window(0), idx[:])
+        weight_piece(0, 0, nc.scalar.copy, at["stage_a"])
+        weight_codes(0, 0)
+        gather(v_words[1][:], table_window(1), idx[:])
+        weight_piece(1, 0, nc.scalar.copy, at["stage_a"] + ROWS)
+        for b, t in ((0, PACK - 1), (1, 0)):
+            for u in range(HALVES):
+                damp(b, u, t, at["w10"] + ROW * (HALVES * b + u), shears[b][:, t, half(u)])
         weight_piece(2, 0, nc.vector.tensor_copy, at["rounded20"])
-        weight_codes(1, 0, placed([P, PASS], U32, "w1_words10", at["w20"]))
-        weight_codes(2, 0, codes_tile(2, 0))
+        weight_codes(1, 0, at["w20"])
+        weight_codes(2, 0)
         clear_page(2)
-        table_pass(2, True)
+        window = table_window(2)
+        for u in range(HALVES):
+            gather(v_words[2][:, half(u)], window, half_of(idx, u))
         clear_page(3)
-        weight_piece(0, 1, nc.scalar.copy, first)
-        shear_tile(1, 1)
-        weight_codes(0, 1, placed([P, PASS], U32, "w1_words01", at["shear11"]))
+
+        weight_piece(0, 1, nc.scalar.copy, at["stage_a"])
+        gather(shears[1][:, 1, :], shear_window(1, 1), idx[:])
+        weight_codes(0, 1, at["shear11"])
         for u in range(HALVES):
             h_rows[0, u] = kept([P, PACK, HALF], BF16, f"h_rows0{u}")
-            for t in range(PACK):
-                hidden_row(0, u, t)
-        woven00 = placed([P, HALF * PACK], BF16, "woven00", third)
-        gpsimd_weave(0, 0, woven00[:])
-        weight_piece(1, 1, nc.scalar.copy, second)
-        weight_codes(1, 1, placed([P, PASS], U32, "w1_words11", at["shear11"] + 2 * WORDS_BYTES))
-        quantise_hidden(0, 0, woven00, at["shear11"] + WORDS_BYTES)
-        squares = {1: square_half(1, second)}
-        weight_piece(2, 1, nc.scalar.copy, fourth)
-        damp_row(1, 0, 1, at["w21"] + WORDS_BYTES * 3)
-        shear_tile(1, 2)
-        weight_codes(2, 1, placed([P, PASS], U32, "w1_words21", at["shear12"]))
-        squares[2] = square_half(2, fourth - WORDS_BYTES // 2)
-        woven01 = placed([P, HALF * PACK], BF16, "woven01", fourth + WORDS_BYTES // 2)
-        gpsimd_weave(0, 1, woven01[:])
-        damp_row(1, 0, 2)
+            hidden_rows(0, u)
+        woven00 = weave_on_gpsimd(0, 0, at["stage_b"])
+        weight_piece(1, 1, nc.scalar.copy, at["stage_a"] + ROWS)
+        weight_codes(1, 1, at["shear11"] + 2 * ROW)
+        hidden_codes(0, 0, woven00, at["shear11"] + ROW)
+        squares11 = placed([P, HALF], F32, "squares11", at["stage_a"] + ROWS)
+        square(squares11[:], shears[1][:, 1, half(1)])
+        rounded21_at = at["stage_c"] + ROW
+        weight_piece(2, 1, nc.scalar.copy, rounded21_at)
+        damp(1, 0, 1, at["w21"] + 3 * ROW)
+        gather(shears[1][:, 2, :], shear_window(1, 2), idx[:])
+        weight_codes(2, 1, at["shear12"])
+        squares12 = placed([P, HALF], F32, "squares12", rounded21_at - ROW // 2)
+        square(squares12[:], shears[1][:, 2, half(1)])
+        woven01 = weave_on_gpsimd(0, 1, rounded21_at + ROW // 2)
+        damp(1, 0, 2)
+
         window = shear_window(1, 3)
         for u in range(HALVES):
-            nc.vector.tensor_copy(out=damp_half(1, u, 3), in_=window[:].indirect(half_of(idx, u)))
-        row = damp_half(1, 0, 3)
-        scratch = placed([P, HALF], F32, "scratch103", at["w21"] + WORDS_BYTES)
-        factor[1, 0, 3] = placed([P, HALF], F32, "factor103", at["w11"])[:]
-        parts = [slice(HALF // 2 * c, HALF // 2 * (c + 1)) for c in range(2)]
-        for part in parts:
-            nc.scalar.activation(out=scratch[:, part], in_=row[:, part], func=ACT.Square)
-        for part in parts:
-            nc.scalar.activation(out=scratch[:, part], in_=scratch[:, part], func=ACT.Abs_reciprocal_sqrt, bias=1.0)
-        for part in parts:
-            nc.scalar.activation(out=factor[1, 0, 3][:, part], in_=scratch[:, part], func=ACT.Square)
-        damp_row(1, 1, 1, at["w21"] + WORDS_BYTES - WORDS_BYTES // 2, row=squares[1], squared=True)
-        damp_row(1, 1, 2, at["w21"] + WORDS_BYTES + WORDS_BYTES // 2, row=squares[2], squared=True)
-        damp_row(1, 1, 3, at["w21"] + WORDS_BYTES - WORDS_BYTES // 2)
+            gather(shears[1][:, 3, half(u)], window, half_of(idx, u))
+        last_at = at["w21"] + ROW
+        damp(1, 0, 3, last_at, into=placed([P, HALF], F32, "damping103", at["w11"])[:], parts=2)
+        damp(1, 1, 1, last_at - ROW // 2, squares11[:])
+        damp(1, 1, 2, last_at + ROW // 2, squares12[:])
+        damp(1, 1, 3, last_at - ROW // 2)
 
         nc.sync.dma_start(out=w2_w[:].bitcast(I32), in_=w2_words.rearrange("b p c i -> p b (c i)").bitcast(I32))
         for q in range(P // QUADRANT):
@@ -370,25 +349,18 @@ def tile_list_wall_model_adjoint_kernel(
         load_src(1)
 
         h_rows[1, 0] = placed([P, PACK, HALF], BF16, "h_rows10", at["shear13"])
-        for t in range(PACK):
-            hidden_row(1, 0, t)
-        woven10 = placed([P, HALF * PACK], BF16, "woven10", at["shear13"] + ROWS_BYTES)
-        hidden_codes(1, 0, nc.vector.tensor_copy, woven10[:], kept([P, HALF], U32, "h_words10"))
-        quantise_hidden(0, 1, woven01, at["shear13"] + ROWS_BYTES)
-        for m in range(2):
-            y = product(m, 0, m)
-            diff = placed([P, HALF], F32, f"diff{m}0", at["tail"] + WORDS_BYTES * m)
-            nc.vector.tensor_tensor(out=diff[:], in0=y[:], in1=src_sb[0][:, m, :], op=ALU.subtract)
-            weighted = placed([P, HALF], F32, f"weighted{m}0", at["damp0"] + WORDS_BYTES * m)
-            weigh_and_scatter(m, 0, diff[:], weighted[:], nc.gpsimd)
+        hidden_rows(1, 0)
+        hidden_codes(1, 0, weave(1, 0, at["shear13"] + ROWS, nc.vector.tensor_copy))
+        hidden_codes(0, 1, woven01, at["shear13"] + ROWS)
+        for m in range(FIRST_RESULTS):
+            result_on_vector(m, 0, at["diffs"] + ROW * m, at["damp0"] + ROW * m)
         h_rows[1, 1] = placed([P, PACK, HALF], BF16, "h_rows11", at["w11"])
-        for t in range(PACK):
-            hidden_row(1, 1, t, (2, 1, 0))
-        ring_at = at["tail"] + WORDS_BYTES
-        woven11 = placed([P, HALF * PACK], BF16, "woven11", at["w11"] + ROWS_BYTES)
-        hidden_codes(1, 1, nc.scalar.copy, woven11[:], placed([P, HALF], U32, "h_words11", at["damp0"] + WORDS_BYTES))
-        result(2, 0, ring_at, at["w21"] + WORDS_BYTES, at["w11"])
-        result(3, 0, ring_at, at["w21"], at["w11"] + ROWS_BYTES)
+        hidden_rows(1, 1)
+
+        hidden_codes(1, 1, weave(1, 1, at["w11"] + ROWS, nc.scalar.copy), at["damp0"] + ROW)
+        diff_at = at["diffs"] + ROW
+        result(2, 0, last_at, diff_at, at["w11"])
+        result(3, 0, last_at - ROW, diff_at, at["w11"] + ROWS)
         for m in range(PAGES):
-            result(m, 1, ring_at)
+            result(m, 1, at["damp0"] + ROW * (PAGES + m), diff_at)
             nc.sync.dma_start(out=out[P * m : P * (m + 1), :], in_=pages[m][:])

@@ -22,41 +22,39 @@ PASS = P * PACK
 K_PASSES = K // PASS
 R_PASSES = H // PASS
 PAGES = N // P
-HALF = 512
-HALVES = S // HALF
-HALF_COLS = HALF // 16
+CHUNK = 128
+CHUNKS = S // CHUNK
+HALF = S // 2
+QUARTER = S // 4
 QUADRANT = 32
 MOVED_ROWS = 3 * QUADRANT + 4
-FIRST_RESULTS = 2
-RUN = 4
+RUN = 2
 
-SLOT = 8192
-ROWS = PACK * HALF * 2
-ROW = HALF * 4
-BANK = 2048
+KIB = 1024
+SLOT = 8 * KIB
+BANK = 2 * KIB
 
 SLOTS = (
-    ("shear00", "page1"),
-    ("shear01", "shear13"),
+    ("shear00", "page2"),
+    ("shear01", "shear11"),
     ("shear02", "v_sc0"),
-    ("shear03", "w11"),
-    ("tab1", "w01"),
-    ("shear10", "shear12"),
-    ("tab0", "shear11"),
-    ("w00", "src0"),
-    ("tab2", "page3"),
-    ("w10", "w21"),
-    ("w20", "src1"),
-    ("rounded20", "page2"),
+    ("shear03", "page3"),
+    ("shear10", "tab2"),
+    ("tab0", "shear12"),
+    ("w00", "shear13"),
+    ("tab1", "src0"),
+    ("w10", "src1"),
+    ("w20", "w11"),
+    ("w21",),
+    ("w01",),
     ("damp0",),
-    ("damp0_second_half",),
+    ("damp0_rest",),
     ("damp1",),
-    ("damp1_second_half",),
-    ("stage_a",),
-    ("stage_b",),
-    ("stage_c",),
-    ("diffs",),
+    ("damp1_rest",),
+    ("stage",),
+    ("stage_rest",),
 )
+GROUPS = ((0, QUARTER), (QUARTER, QUARTER), (HALF, HALF))
 
 
 def tile_list_wall_model_adjoint_kernel(
@@ -76,8 +74,11 @@ def tile_list_wall_model_adjoint_kernel(
         def kept(shape, dtype, name):
             return keep.tile(shape, dtype, name=name, align_bytes=64)
 
-        def bank(name, number):
-            return psum.tile([P, HALF], F32, name=name, offset=BANK * number)
+        def span(first, count):
+            return slice(first, first + count)
+
+        def entries(offsets, first, count):
+            return offsets[:, first // 16 : (first + count) // 16]
 
         shear_rows = sT.rearrange("(b p t) c -> b t p c", b=R_PASSES, t=PACK)
 
@@ -98,39 +99,29 @@ def tile_list_wall_model_adjoint_kernel(
                 out=tab_sc[QUADRANT * q : QUADRANT * q + 4 * K_PASSES, :].bitcast(I32),
                 in_=tab_scales[:, 4 * q : 4 * q + 4, :].bitcast(I32),
             )
-
         w2_sc = kept([P, N], U8, "w2_sc")
         nc.vector.memset(w2_sc[:].bitcast(I32), 0)
-        v_sc = {}
-        for a in range(1, K_PASSES):
-            v_sc[a] = kept([P, S], U8, f"v_sc{a}")
-            nc.vector.memset(v_sc[a][:].bitcast(I32), 0)
-
-        pages = {0: keep.tile([P, T2], F32, name="page0")}
-        nc.vector.memset(pages[0][:], 0.0)
+        moved_sc = kept([P, (K_PASSES - 1) * S], U8, "moved_sc")
+        nc.vector.memset(moved_sc[:].bitcast(I32), 0)
+        pages = {}
+        for m in range(2):
+            pages[m] = keep.tile([P, T2], F32, name=f"page{m}")
+            nc.vector.memset(pages[m][:], 0.0)
 
         v_words = [kept([P, S], U32, f"v_words{a}") for a in range(K_PASSES)]
+        v_sc = {}
         w1_sc = {(a, b): kept([P, PASS], U8, f"w1_sc{a}{b}") for a in range(K_PASSES) for b in range(R_PASSES)}
-        shears = {}
-        h_sc = {}
-        for b in range(R_PASSES):
-            shears[b] = placed([P, PACK, S], F32, f"damp{b}", at[f"damp{b}"])
-            for u in range(HALVES):
-                h_sc[b, u] = kept([P, HALF], U8, f"h_sc{b}{u}")
+        h_sc = [kept([P, S], U8, f"h_sc{b}") for b in range(R_PASSES)]
         w2_w = kept([P, R_PASSES, N], U32, "w2_w")
         wgo_sb = keep.tile([P, S], F32, name="wgo_sb")
+        damp0 = placed([P, PACK, S], F32, "damp0", at["damp0"])
+        damp1 = [
+            placed([P, PACK, count], F32, f"damp1_{g}", at["damp1"] + PACK * 4 * first)
+            for g, (first, count) in enumerate(GROUPS)
+        ]
         w1_rounded = {}
         w1_words = {}
-        damping = {}
-        h_rows = {}
-        h_words = {}
         src_sb = {}
-
-        def half(u):
-            return slice(HALF * u, HALF * (u + 1))
-
-        def half_of(offsets, u):
-            return offsets[:, HALF_COLS * u : HALF_COLS * (u + 1)]
 
         def gather(out, window, offsets):
             nc.vector.tensor_copy(out=out, in_=window[:].indirect(offsets))
@@ -140,12 +131,14 @@ def tile_list_wall_model_adjoint_kernel(
             nc.gpsimd.memset(pages[m][:], 0.0)
 
         def gather_scales():
-            v_sc[0] = placed([P, S], U8, "v_sc0", at["v_sc0"])
-            gather(v_sc[0][:], tab_sc, idx[:])
+            picked = placed([P, S], U8, "v_sc0", at["v_sc0"])
+            gather(picked[:], tab_sc, idx[:])
+            v_sc[0] = picked[:]
             for a in range(1, K_PASSES):
+                v_sc[a] = moved_sc[:, span(S * (a - 1), S)]
                 nc.gpsimd.dma_start(
-                    out=v_sc[a][0:MOVED_ROWS, :].bitcast(I32),
-                    in_=v_sc[0][4 * a : 4 * a + MOVED_ROWS, :].bitcast(I32),
+                    out=moved_sc[0:MOVED_ROWS, span(S * (a - 1), S)].bitcast(I32),
+                    in_=picked[4 * a : 4 * a + MOVED_ROWS, :].bitcast(I32),
                 )
 
         def table_window(a):
@@ -156,186 +149,154 @@ def tile_list_wall_model_adjoint_kernel(
             )
             return window
 
-        def weight_piece(a, b, copy, offset):
+        def weight_piece(a, b, copy):
             raw = placed([P, PACK, PASS], F32, f"w{a}{b}", at[f"w{a}{b}"])
             piece = w1[PASS * a : PASS * (a + 1), PASS * b : PASS * (b + 1)]
             nc.sync.dma_start(out=raw[:], in_=piece.rearrange("(p i) c -> p i c", i=PACK))
-            w1_rounded[a, b] = placed([P, PACK * PASS], BF16, f"rounded{a}{b}", offset)
+            w1_rounded[a, b] = placed([P, PACK * PASS], BF16, f"rounded{a}{b}", at["stage"] + 4 * KIB * a)
             copy(
                 out=w1_rounded[a, b][:].rearrange("p (t m i) -> p m i t", t=PACK, i=PACK),
                 in_=raw[:].rearrange("p i (m t) -> p m i t", t=PACK),
             )
 
-        def words_tile(name, offset):
-            if offset is None:
-                return kept([P, HALF], U32, name)
-            return placed([P, HALF], U32, name, offset)
+        def quantise(words, scales, values):
+            nc.vector.quantize_mx(out=words.bitcast(E4M3), scales=scales, in_=values)
 
         def weight_codes(a, b, offset=None):
-            w1_words[a, b] = words_tile(f"w1_words{a}{b}", offset)
-            nc.vector.quantize_mx(
-                out=w1_words[a, b][:].bitcast(E4M3), scales=w1_sc[a, b][:], in_=w1_rounded[a, b][:]
-            )
+            name = f"w1_words{a}{b}"
+            w1_words[a, b] = kept([P, PASS], U32, name) if offset is None else placed([P, PASS], U32, name, offset)
+            quantise(w1_words[a, b][:], w1_sc[a, b][:], w1_rounded[a, b][:])
 
         def square(out, row):
             nc.gpsimd.tensor_tensor(out=out, in0=row, in1=row, op=ALU.mult)
 
-        def damp(b, u, t, scratch_at=None, squares=None, into=None, parts=1):
-            row = shears[b][:, t, half(u)] if squares is None else squares
-            scratch = row if scratch_at is None else placed([P, HALF], F32, f"scratch{b}{u}{t}", scratch_at)[:]
-            damping[b, u, t] = row if into is None else into
-            cuts = [slice(HALF // parts * c, HALF // parts * (c + 1)) for c in range(parts)]
-            if squares is None:
-                for cut in cuts:
-                    nc.scalar.activation(out=scratch[:, cut], in_=row[:, cut], func=ACT.Square)
-                squares = scratch
-            for cut in cuts:
-                nc.scalar.activation(
-                    out=scratch[:, cut], in_=squares[:, cut], func=ACT.Abs_reciprocal_sqrt, bias=1.0
-                )
-            for cut in cuts:
-                nc.scalar.activation(out=damping[b, u, t][:, cut], in_=scratch[:, cut], func=ACT.Square)
+        def square_on_scalar(out, row):
+            nc.scalar.activation(out=out, in_=row, func=ACT.Square)
 
-        def hidden_rows(b, u):
-            passes = (2, 1, 0) if (b, u) == (1, 1) else (0, 1, 2)
-            for t in range(PACK):
-                acc = bank(f"acc{b}{u}{t}", PACK * u + t)
-                for a in passes:
+        def inverse_root(out, squares):
+            nc.scalar.activation(out=out, in_=squares, func=ACT.Abs_reciprocal_sqrt, bias=1.0)
+
+        def finish_damping(t, roots, first, count):
+            for g, (start, width) in enumerate(GROUPS):
+                if first <= start < first + count:
+                    square_on_scalar(damp1[g][:, t, :], roots[:, span(start - first, width)])
+
+        def sums(b, c):
+            acc = psum.tile([P, PACK, CHUNK], F32, name=f"acc{b}{c}", offset=BANK * c)
+            passes = (0, 2, 1) if b == 0 and c >= CHUNKS // 2 else (0, 1, 2)
+            for a in passes:
+                for t in range(PACK):
                     nc.tensor.matmul_mx(
-                        out=acc[:],
-                        lhsT=w1_words[a, b][:, P * t : P * (t + 1)].bitcast(E4M3),
-                        lhsT_scale=w1_sc[a, b][:, P * t : P * (t + 1)],
-                        rhs=v_words[a][:, half(u)].bitcast(E5M2),
-                        rhs_scale=v_sc[a][:, half(u)],
-                        start=(a == passes[0]),
-                        stop=(a == passes[-1]),
+                        out=acc[:, t, :],
+                        lhsT=w1_words[a, b][:, span(P * t, P)].bitcast(E4M3),
+                        lhsT_scale=w1_sc[a, b][:, span(P * t, P)],
+                        rhs=v_words[a][:, span(CHUNK * c, CHUNK)].bitcast(E5M2),
+                        rhs_scale=v_sc[a][:, span(CHUNK * c, CHUNK)],
+                        start=(a == passes[0] and t == 0),
+                        stop=(a == passes[-1] and t == PACK - 1),
                     )
-                nc.vector.tensor_tensor(out=h_rows[b, u][:, t, :], in0=acc[:], in1=damping[b, u, t], op=ALU.mult)
+            return acc
 
-        def weave(b, u, offset, copy):
-            woven = placed([P, HALF * PACK], BF16, f"woven{b}{u}", offset)
-            copy(
-                out=woven[:].rearrange("p (c i t) -> p c t i", i=RUN, t=PACK),
-                in_=h_rows[b, u][:].rearrange("p t (c i) -> p c t i", i=RUN),
+        def damped(acc, damping, woven):
+            nc.vector.tensor_tensor(
+                out=woven.rearrange("p (c i t) -> p c t i", i=RUN, t=PACK),
+                in0=acc[:].rearrange("p t (c i) -> p c t i", i=RUN),
+                in1=damping.rearrange("p t (c i) -> p c t i", i=RUN),
+                op=ALU.mult,
             )
-            return woven
-
-        def weave_on_gpsimd(b, u, offset):
-            woven = placed([P, HALF * PACK], BF16, f"woven{b}{u}", offset)
-            nc.gpsimd.tensor_scalar(
-                out=woven[:].rearrange("p (j t) -> p j t", t=PACK),
-                in0=h_rows[b, u][:].rearrange("p t j -> p j t"),
-                scalar1=1.0,
-                scalar2=0.0,
-                op0=ALU.mult,
-                op1=ALU.add,
-            )
-            return woven
-
-        def hidden_codes(b, u, woven, offset=None):
-            h_words[b, u] = words_tile(f"h_words{b}{u}", offset)
-            nc.vector.quantize_mx(out=h_words[b, u][:].bitcast(E4M3), scales=h_sc[b, u][:], in_=woven[:])
 
         def load_src(u):
             src_sb[u] = placed([P, PAGES, HALF], F32, f"src{u}", at[f"src{u}"])
-            nc.sync.dma_start(out=src_sb[u][:], in_=src[:, half(u)].rearrange("(m p) j -> p m j", p=P))
+            nc.sync.dma_start(out=src_sb[u][:], in_=src[:, span(HALF * u, HALF)].rearrange("(m p) j -> p m j", p=P))
 
-        def product(m, u):
-            rows = slice(P * m, P * (m + 1))
-            y = bank(f"y{m}{u}", m)
-            for b in range(R_PASSES):
-                nc.tensor.matmul_mx(
-                    out=y[:],
-                    lhsT=w2_w[:, b, rows].bitcast(E4M3),
-                    lhsT_scale=w2_sc[4 * b : P, rows],
-                    rhs=h_words[b, u][:].bitcast(E4M3),
-                    rhs_scale=h_sc[b, u][:],
-                    start=(b == 0),
-                    stop=(b == R_PASSES - 1),
-                )
-            return y
-
-        def weigh_and_scatter(m, u, diff, weighted):
-            nc.gpsimd.tensor_tensor(out=weighted[:], in0=diff[:], in1=wgo_sb[:, half(u)], op=ALU.mult)
-            nc.vector.tensor_copy(out=pages[m][:].indirect(half_of(idx2, u)), in_=weighted[:])
-
-        def result_on_vector(m, u, diff_at, weighted_at):
-            y = product(m, u)
-            diff = placed([P, HALF], F32, f"diff{m}{u}", diff_at)
-            nc.vector.tensor_tensor(out=diff[:], in0=y[:], in1=src_sb[u][:, m, :], op=ALU.subtract)
-            weigh_and_scatter(m, u, diff, placed([P, HALF], F32, f"weighted{m}{u}", weighted_at))
-
-        def result(m, u, values_at, diff_at, weighted_at=None):
-            y = product(m, u)
-            values = placed([P, HALF], F32, f"values{m}{u}", values_at)
-            nc.scalar.copy(out=values[:], in_=y[:])
-            diff = placed([P, HALF], F32, f"diff{m}{u}", diff_at)
-            nc.gpsimd.tensor_tensor(out=diff[:], in0=values[:], in1=src_sb[u][:, m, :], op=ALU.subtract)
-            weighted = values if weighted_at is None else placed([P, HALF], F32, f"weighted{m}{u}", weighted_at)
-            weigh_and_scatter(m, u, diff, weighted)
-
-        gather(shears[0][:, 0, :], first_window, idx[:])
-        clear_page(1)
-        for u in range(HALVES):
-            damp(0, u, 0)
+        gather(damp0[:, 0, :], first_window, idx[:])
+        clear_page(2)
+        for step in (square_on_scalar, inverse_root, square_on_scalar):
+            for u in range(2):
+                step(damp0[:, 0, span(HALF * u, HALF)], damp0[:, 0, span(HALF * u, HALF)])
         for t in range(1, PACK):
-            gather(shears[0][:, t, :], shear_window(0, t), idx[:])
-            square(shears[0][:, t, :], shears[0][:, t, :])
+            gather(damp0[:, t, :], shear_window(0, t), idx[:])
+            square(damp0[:, t, :], damp0[:, t, :])
             if t == PACK - 2:
                 gather_scales()
             if t < PACK - 1:
-                for u in range(HALVES):
-                    damp(0, u, t, squares=shears[0][:, t, half(u)])
-        gather(shears[1][:, 0, :], shear_window(1, 0), idx[:])
-        square(shears[1][:, 0, :], shears[1][:, 0, :])
-
-        gather(v_words[0][:], table_window(0), idx[:])
-        weight_piece(0, 0, nc.scalar.copy, at["stage_a"])
-        weight_codes(0, 0)
-        gather(v_words[1][:], table_window(1), idx[:])
-        weight_piece(1, 0, nc.scalar.copy, at["stage_a"] + ROWS)
-        for b, t in ((0, PACK - 1), (1, 0)):
-            for u in range(HALVES):
-                damp(b, u, t, at["w10"] + ROW * (HALVES * b + u), shears[b][:, t, half(u)])
-        weight_piece(2, 0, nc.vector.tensor_copy, at["rounded20"])
-        weight_codes(1, 0, at["w20"])
-        weight_codes(2, 0)
-        clear_page(2)
-        window = table_window(2)
-        for u in range(HALVES):
-            gather(v_words[2][:, half(u)], window, half_of(idx, u))
+                for step in (inverse_root, square_on_scalar):
+                    for u in range(2):
+                        step(damp0[:, t, span(HALF * u, HALF)], damp0[:, t, span(HALF * u, HALF)])
+        row10 = placed([P, S], F32, "row10", at["v_sc0"] + KIB)
+        gather(row10[:], shear_window(1, 0), idx[:])
+        square(row10[:], row10[:])
         clear_page(3)
 
-        weight_piece(0, 1, nc.scalar.copy, at["stage_a"])
-        gather(shears[1][:, 1, :], shear_window(1, 1), idx[:])
+        weight_piece(0, 0, nc.scalar.copy)
+        gather(v_words[0][:], table_window(0), idx[:])
+        weight_codes(0, 0)
+        gather(v_words[1][:], table_window(1), idx[:])
+        weight_piece(1, 0, nc.scalar.copy)
+        roots03 = placed([P, S], F32, "roots03", at["w10"])
+        roots10 = placed([P, S], F32, "roots10", at["w10"] + 4 * KIB)
+        inverse_root(roots03[:], damp0[:, PACK - 1, :])
+        inverse_root(roots10[:], row10[:])
+        square_on_scalar(damp0[:, PACK - 1, :], roots03[:])
+        finish_damping(0, roots10, 0, S)
+        weight_piece(2, 0, nc.vector.tensor_copy)
+        weight_codes(1, 0)
+        weight_codes(2, 0)
+        window = table_window(2)
+        for u in range(2):
+            gather(v_words[2][:, span(HALF * u, HALF)], window, entries(idx, HALF * u, HALF))
+
+        weight_piece(0, 1, nc.scalar.copy)
+        row11 = placed([P, S], F32, "row11", at["tab2"])
+        gather(row11[:], shear_window(1, 1), idx[:])
         weight_codes(0, 1, at["shear11"])
-        for u in range(HALVES):
-            h_rows[0, u] = kept([P, PACK, HALF], BF16, f"h_rows0{u}")
-            hidden_rows(0, u)
-        woven00 = weave_on_gpsimd(0, 0, at["stage_b"])
-        weight_piece(1, 1, nc.scalar.copy, at["stage_a"] + ROWS)
-        weight_codes(1, 1, at["shear11"] + 2 * ROW)
-        hidden_codes(0, 0, woven00, at["shear11"] + ROW)
-        squares11 = placed([P, HALF], F32, "squares11", at["stage_a"] + ROWS)
-        square(squares11[:], shears[1][:, 1, half(1)])
-        rounded21_at = at["stage_c"] + ROW
-        weight_piece(2, 1, nc.scalar.copy, rounded21_at)
-        damp(1, 0, 1, at["w21"] + 3 * ROW)
-        gather(shears[1][:, 2, :], shear_window(1, 2), idx[:])
+        squares11 = placed([P, S], F32, "squares11", at["stage"])
+        square(squares11[:], row11[:])
+        woven0 = [
+            placed([P, PACK * HALF], BF16, "woven00", at["stage"] + 12 * KIB),
+            placed([P, PACK * HALF], BF16, "woven01", at["shear11"] + 2 * KIB),
+        ]
+        for c in range(CHUNKS):
+            u, part = divmod(c, CHUNKS // 2)
+            damped(sums(0, c), damp0[:, :, span(CHUNK * c, CHUNK)], woven0[u][:, span(PACK * CHUNK * part, PACK * CHUNK)])
+        weight_piece(1, 1, nc.scalar.copy)
+        weight_codes(1, 1)
+        weight_piece(2, 1, nc.scalar.copy)
+        roots11 = placed([P, S], F32, "roots11", at["w21"])
+        inverse_root(roots11[:], squares11[:])
+        finish_damping(1, roots11, 0, S)
+        row12 = placed([P, S], F32, "row12", at["tab2"] + 4 * KIB)
+        gather(row12[:], shear_window(1, 2), idx[:])
         weight_codes(2, 1, at["shear12"])
-        squares12 = placed([P, HALF], F32, "squares12", rounded21_at - ROW // 2)
-        square(squares12[:], shears[1][:, 2, half(1)])
-        woven01 = weave_on_gpsimd(0, 1, rounded21_at + ROW // 2)
-        damp(1, 0, 2)
+        late_at = at["stage"] + 8 * KIB
+        squares12 = placed([P, HALF], F32, "squares12", late_at)
+        square(squares12[:], row12[:, span(HALF, HALF)])
+        for step in (square_on_scalar, inverse_root):
+            for first, count in GROUPS[:2]:
+                step(row12[:, span(first, count)], row12[:, span(first, count)])
+        finish_damping(2, row12, 0, HALF)
 
         window = shear_window(1, 3)
-        for u in range(HALVES):
-            gather(shears[1][:, 3, half(u)], window, half_of(idx, u))
-        last_at = at["w21"] + ROW
-        damp(1, 0, 3, last_at, into=placed([P, HALF], F32, "damping103", at["w11"])[:], parts=2)
-        damp(1, 1, 1, last_at - ROW // 2, squares11[:])
-        damp(1, 1, 2, last_at + ROW // 2, squares12[:])
-        damp(1, 1, 3, last_at - ROW // 2)
+        row13 = placed([P, S], F32, "row13", at["w01"])
+        for first, count in GROUPS:
+            gather(row13[:, span(first, count)], window, entries(idx, first, count))
+        h_words0 = placed([P, S], U32, "h_words0", at["shear13"])
+        for u in range(2):
+            quantise(h_words0[:, span(HALF * u, HALF)], h_sc[0][:, span(HALF * u, HALF)], woven0[u][:])
+        squares13 = placed([P, HALF], F32, "squares13", at["shear11"] + 2 * KIB)
+        square(squares13[:], row13[:, span(HALF, HALF)])
+        roots_at = at["w21"] + 4 * KIB
+        roots13 = placed([P, HALF], F32, "roots13", roots_at)
+        for first, count in GROUPS[:2]:
+            square_on_scalar(roots13[:, span(first, count)], row13[:, span(first, count)])
+            inverse_root(roots13[:, span(first, count)], roots13[:, span(first, count)])
+            finish_damping(3, roots13[:, span(first, count)], first, count)
+        roots12_late = placed([P, HALF], F32, "roots12_late", roots_at + KIB)
+        inverse_root(roots12_late[:], squares12[:])
+        finish_damping(2, roots12_late, HALF, HALF)
+        roots13_late = placed([P, HALF], F32, "roots13_late", late_at)
+        inverse_root(roots13_late[:], squares13[:])
+        finish_damping(3, roots13_late, HALF, HALF)
 
         nc.sync.dma_start(out=w2_w[:].bitcast(I32), in_=w2_words.rearrange("b p c i -> p b (c i)").bitcast(I32))
         for q in range(P // QUADRANT):
@@ -348,19 +309,61 @@ def tile_list_wall_model_adjoint_kernel(
         nc.sync.dma_start(out=wgo_sb[:], in_=wgo)
         load_src(1)
 
-        h_rows[1, 0] = placed([P, PACK, HALF], BF16, "h_rows10", at["shear13"])
-        hidden_rows(1, 0)
-        hidden_codes(1, 0, weave(1, 0, at["shear13"] + ROWS, nc.vector.tensor_copy))
-        hidden_codes(0, 1, woven01, at["shear13"] + ROWS)
-        for m in range(FIRST_RESULTS):
-            result_on_vector(m, 0, at["diffs"] + ROW * m, at["damp0"] + ROW * m)
-        h_rows[1, 1] = placed([P, PACK, HALF], BF16, "h_rows11", at["w11"])
-        hidden_rows(1, 1)
+        woven1 = [
+            placed([P, PACK * count], BF16, f"woven1{g}", at["w11"] + PACK * 2 * first)
+            for g, (first, count) in enumerate(GROUPS)
+        ]
+        h_words1 = {0: kept([P, HALF], U32, "h_words10")}
+        for g, (first, count) in enumerate(GROUPS):
+            for part in range(count // CHUNK):
+                damped(
+                    sums(1, first // CHUNK + part),
+                    damp1[g][:, :, span(CHUNK * part, CHUNK)],
+                    woven1[g][:, span(PACK * CHUNK * part, PACK * CHUNK)],
+                )
+            if first < HALF:
+                quantise(h_words1[0][:, span(first, count)], h_sc[1][:, span(first, count)], woven1[g][:])
 
-        hidden_codes(1, 1, weave(1, 1, at["w11"] + ROWS, nc.scalar.copy), at["damp0"] + ROW)
-        diff_at = at["diffs"] + ROW
-        result(2, 0, last_at, diff_at, at["w11"])
-        result(3, 0, last_at - ROW, diff_at, at["w11"] + ROWS)
-        for m in range(PAGES):
-            result(m, 1, at["damp0"] + ROW * (PAGES + m), diff_at)
-            nc.sync.dma_start(out=out[P * m : P * (m + 1), :], in_=pages[m][:])
+        diff_at = at["damp0"]
+
+        def result(number, m, first, count, values_at, weighted_at):
+            u, inside = divmod(first, HALF)
+            y = psum.tile([P, count], F32, name=f"y{number}", offset=BANK * (number % CHUNKS))
+            words = (h_words0[:, span(first, count)], h_words1[u][:, span(inside, count)])
+            for b in range(R_PASSES):
+                nc.tensor.matmul_mx(
+                    out=y[:],
+                    lhsT=w2_w[:, b, span(P * m, P)].bitcast(E4M3),
+                    lhsT_scale=w2_sc[4 * b : P, span(P * m, P)],
+                    rhs=words[b].bitcast(E4M3),
+                    rhs_scale=h_sc[b][:, span(first, count)],
+                    start=(b == 0),
+                    stop=(b == R_PASSES - 1),
+                )
+            values = placed([P, count], F32, f"values{number}", values_at)
+            nc.scalar.copy(out=values[:], in_=y[:])
+            diff = placed([P, count], F32, f"diff{number}", diff_at)
+            nc.gpsimd.tensor_tensor(
+                out=diff[:], in0=values[:], in1=src_sb[u][:, m, span(inside, count)], op=ALU.subtract
+            )
+            weighted = placed([P, count], F32, f"weighted{number}", weighted_at)
+            nc.gpsimd.tensor_tensor(out=weighted[:], in0=diff[:], in1=wgo_sb[:, span(first, count)], op=ALU.mult)
+            nc.vector.tensor_copy(out=pages[m][:].indirect(entries(idx2, first, count)), in_=weighted[:])
+
+        ring_at = at["damp0"] + 2 * KIB
+        result(0, 0, 0, QUARTER, late_at, ring_at)
+        h_words1[1] = placed([P, HALF], U32, "h_words11", ring_at)
+        quantise(h_words1[1][:], h_sc[1][:, span(HALF, HALF)], woven1[2][:])
+        result(1, 0, QUARTER, QUARTER, late_at + KIB, ring_at + 2 * KIB)
+        result(2, 1, 0, HALF, roots_at + KIB, at["w11"] + 4 * KIB)
+        number = 3
+        for u in range(2):
+            for m in range(PAGES):
+                if u == 1 or m >= 2:
+                    result(
+                        number, m, HALF * u, HALF,
+                        ring_at + 2 * KIB * (2 + number % 2), ring_at + 2 * KIB * (4 + number % 3),
+                    )
+                    number = number + 1
+                if u == 1:
+                    nc.sync.dma_start(out=out[span(P * m, P), :], in_=pages[m][:])

@@ -28,7 +28,7 @@ HALF = S // 2
 QUARTER = S // 4
 QUADRANT = 32
 MOVED_ROWS = 3 * QUADRANT + 4
-RUN = 2
+PAIR = 2
 
 KIB = 1024
 SLOT = 8 * KIB
@@ -36,23 +36,24 @@ BANK = 2 * KIB
 
 SLOTS = (
     ("shear00", "page2"),
-    ("shear01", "shear11"),
+    ("shear01", "tab1", "w21"),
     ("shear02", "v_sc0"),
-    ("shear03", "page3"),
-    ("shear10", "tab2"),
-    ("tab0", "shear12"),
-    ("w00", "shear13"),
-    ("tab1", "src0"),
-    ("w10", "src1"),
-    ("w20", "w11"),
-    ("w21",),
-    ("w01",),
+    ("shear03", "w11", "src0"),
+    ("shear11", "tab2", "page3"),
+    ("shear12", "w01", "src1"),
+    ("w00", "early_roots", "woven1"),
+    ("tab0", "shear13"),
+    ("before_w10",),
+    ("w10",),
+    ("behind_w10",),
+    ("shear10", "w20"),
+    ("rows_a",),
+    ("rows_b",),
     ("damp0",),
     ("damp0_rest",),
-    ("damp1",),
-    ("damp1_rest",),
     ("stage",),
     ("stage_rest",),
+    ("woven0",),
 )
 GROUPS = ((0, QUARTER), (QUARTER, QUARTER), (HALF, HALF))
 
@@ -114,9 +115,9 @@ def tile_list_wall_model_adjoint_kernel(
         h_sc = [kept([P, S], U8, f"h_sc{b}") for b in range(R_PASSES)]
         w2_w = kept([P, R_PASSES, N], U32, "w2_w")
         wgo_sb = keep.tile([P, S], F32, name="wgo_sb")
-        damp0 = placed([P, PACK, S], F32, "damp0", at["damp0"])
+        damp0 = placed([P, PAIR, S, PAIR], F32, "damp0", at["damp0"])
         damp1 = [
-            placed([P, PACK, count], F32, f"damp1_{g}", at["damp1"] + PACK * 4 * first)
+            placed([P, PAIR, count, PAIR], F32, f"damp1_{g}", at["w10"] + KIB * (2, 6, -6)[g])
             for g, (first, count) in enumerate(GROUPS)
         ]
         w1_rounded = {}
@@ -176,10 +177,8 @@ def tile_list_wall_model_adjoint_kernel(
         def inverse_root(out, squares):
             nc.scalar.activation(out=out, in_=squares, func=ACT.Abs_reciprocal_sqrt, bias=1.0)
 
-        def finish_damping(t, roots, first, count):
-            for g, (start, width) in enumerate(GROUPS):
-                if first <= start < first + count:
-                    square_on_scalar(damp1[g][:, t, :], roots[:, span(start - first, width)])
+        def square_pair(out, roots):
+            square_on_scalar(out, roots.rearrange("p e j -> p j e"))
 
         def sums(b, c):
             acc = psum.tile([P, PACK, CHUNK], F32, name=f"acc{b}{c}", offset=BANK * c)
@@ -199,9 +198,9 @@ def tile_list_wall_model_adjoint_kernel(
 
         def damped(acc, damping, woven):
             nc.vector.tensor_tensor(
-                out=woven.rearrange("p (c i t) -> p c t i", i=RUN, t=PACK),
-                in0=acc[:].rearrange("p t (c i) -> p c t i", i=RUN),
-                in1=damping.rearrange("p t (c i) -> p c t i", i=RUN),
+                out=woven.rearrange("p (j u e) -> p j u e", u=PAIR, e=PAIR),
+                in0=acc[:].rearrange("p (u e) j -> p j u e", e=PAIR),
+                in1=damping.rearrange("p u j e -> p j u e"),
                 op=ALU.mult,
             )
 
@@ -209,94 +208,78 @@ def tile_list_wall_model_adjoint_kernel(
             src_sb[u] = placed([P, PAGES, HALF], F32, f"src{u}", at[f"src{u}"])
             nc.sync.dma_start(out=src_sb[u][:], in_=src[:, span(HALF * u, HALF)].rearrange("(m p) j -> p m j", p=P))
 
-        gather(damp0[:, 0, :], first_window, idx[:])
-        clear_page(2)
-        for step in (square_on_scalar, inverse_root, square_on_scalar):
-            for u in range(2):
-                step(damp0[:, 0, span(HALF * u, HALF)], damp0[:, 0, span(HALF * u, HALF)])
-        for t in range(1, PACK):
-            gather(damp0[:, t, :], shear_window(0, t), idx[:])
-            square(damp0[:, t, :], damp0[:, t, :])
-            if t == PACK - 2:
-                gather_scales()
-            if t < PACK - 1:
-                for step in (inverse_root, square_on_scalar):
-                    for u in range(2):
-                        step(damp0[:, t, span(HALF * u, HALF)], damp0[:, t, span(HALF * u, HALF)])
-        row10 = placed([P, S], F32, "row10", at["v_sc0"] + KIB)
-        gather(row10[:], shear_window(1, 0), idx[:])
-        square(row10[:], row10[:])
-        clear_page(3)
+        halves = [span(0, HALF), span(HALF, HALF)]
+        for u in range(PAIR):
+            rows0 = placed([P, PAIR, S], F32, f"rows0{u}", at[("rows_a", "rows_b")[u]])
+            for e in range(PAIR):
+                t = PAIR * u + e
+                gather(rows0[:, e, :], first_window if t == 0 else shear_window(0, t), idx[:])
+                if t == 0:
+                    clear_page(2)
+                if u == 0:
+                    for cut in halves:
+                        square_on_scalar(rows0[:, e, cut], rows0[:, e, cut])
+                else:
+                    square(rows0[:, e, :], rows0[:, e, :])
+                if t == PACK - 2:
+                    gather_scales()
+                for cut in halves:
+                    inverse_root(rows0[:, e, cut], rows0[:, e, cut])
+            for cut in halves:
+                square_pair(damp0[:, u, cut, :], rows0[:, :, cut])
+        rows = {}
+        for t, offset in enumerate((at["rows_a"], at["rows_a"] + 4 * KIB, at["v_sc0"] + KIB)):
+            rows[t] = placed([P, S], F32, f"row1{t}", offset)
+            gather(rows[t][:], shear_window(1, t), idx[:])
+            square(rows[t][:], rows[t][:])
 
         weight_piece(0, 0, nc.scalar.copy)
         gather(v_words[0][:], table_window(0), idx[:])
         weight_codes(0, 0)
+        early_roots = placed([P, PAIR, S], F32, "early_roots", at["early_roots"])
+        for e in range(PAIR):
+            inverse_root(early_roots[:, e, :], rows[e][:])
         gather(v_words[1][:], table_window(1), idx[:])
         weight_piece(1, 0, nc.scalar.copy)
-        roots03 = placed([P, S], F32, "roots03", at["w10"])
-        roots10 = placed([P, S], F32, "roots10", at["w10"] + 4 * KIB)
-        inverse_root(roots03[:], damp0[:, PACK - 1, :])
-        inverse_root(roots10[:], row10[:])
-        square_on_scalar(damp0[:, PACK - 1, :], roots03[:])
-        finish_damping(0, roots10, 0, S)
+        for g, (first, count) in enumerate(GROUPS):
+            square_pair(damp1[g][:, 0], early_roots[:, :, span(first, count)])
         weight_piece(2, 0, nc.vector.tensor_copy)
-        weight_codes(1, 0)
+        late_roots = [
+            placed([P, PAIR, count], F32, f"late_roots{g}", at["w20"] + KIB * (2, 4, -2)[g])
+            for g, (first, count) in enumerate(GROUPS)
+        ]
+        for g, (first, count) in enumerate(GROUPS):
+            inverse_root(late_roots[g][:, 0, :], rows[2][:, span(first, count)])
+        weight_codes(1, 0, at["w20"] + 6 * KIB)
         weight_codes(2, 0)
         window = table_window(2)
         for u in range(2):
             gather(v_words[2][:, span(HALF * u, HALF)], window, entries(idx, HALF * u, HALF))
+        clear_page(3)
 
         weight_piece(0, 1, nc.scalar.copy)
-        row11 = placed([P, S], F32, "row11", at["tab2"])
-        gather(row11[:], shear_window(1, 1), idx[:])
-        weight_codes(0, 1, at["shear11"])
-        squares11 = placed([P, S], F32, "squares11", at["stage"])
-        square(squares11[:], row11[:])
-        woven0 = [
-            placed([P, PACK * HALF], BF16, "woven00", at["stage"] + 12 * KIB),
-            placed([P, PACK * HALF], BF16, "woven01", at["shear11"] + 2 * KIB),
-        ]
+        weight_codes(0, 1)
+        woven0 = [placed([P, PACK * HALF], BF16, f"woven0{u}", at["woven0"] + 4 * KIB * u) for u in range(2)]
         for c in range(CHUNKS):
             u, part = divmod(c, CHUNKS // 2)
-            damped(sums(0, c), damp0[:, :, span(CHUNK * c, CHUNK)], woven0[u][:, span(PACK * CHUNK * part, PACK * CHUNK)])
+            damped(sums(0, c), damp0[:, :, span(CHUNK * c, CHUNK), :], woven0[u][:, span(PACK * CHUNK * part, PACK * CHUNK)])
         weight_piece(1, 1, nc.scalar.copy)
         weight_codes(1, 1)
         weight_piece(2, 1, nc.scalar.copy)
-        roots11 = placed([P, S], F32, "roots11", at["w21"])
-        inverse_root(roots11[:], squares11[:])
-        finish_damping(1, roots11, 0, S)
-        row12 = placed([P, S], F32, "row12", at["tab2"] + 4 * KIB)
-        gather(row12[:], shear_window(1, 2), idx[:])
-        weight_codes(2, 1, at["shear12"])
-        late_at = at["stage"] + 8 * KIB
-        squares12 = placed([P, HALF], F32, "squares12", late_at)
-        square(squares12[:], row12[:, span(HALF, HALF)])
-        for step in (square_on_scalar, inverse_root):
-            for first, count in GROUPS[:2]:
-                step(row12[:, span(first, count)], row12[:, span(first, count)])
-        finish_damping(2, row12, 0, HALF)
 
         window = shear_window(1, 3)
-        row13 = placed([P, S], F32, "row13", at["w01"])
+        row13 = placed([P, S], F32, "row13", at["rows_b"])
         for first, count in GROUPS:
             gather(row13[:, span(first, count)], window, entries(idx, first, count))
+        weight_codes(2, 1, at["shear13"] + 4 * KIB)
         h_words0 = placed([P, S], U32, "h_words0", at["shear13"])
         for u in range(2):
             quantise(h_words0[:, span(HALF * u, HALF)], h_sc[0][:, span(HALF * u, HALF)], woven0[u][:])
-        squares13 = placed([P, HALF], F32, "squares13", at["shear11"] + 2 * KIB)
-        square(squares13[:], row13[:, span(HALF, HALF)])
-        roots_at = at["w21"] + 4 * KIB
-        roots13 = placed([P, HALF], F32, "roots13", roots_at)
-        for first, count in GROUPS[:2]:
-            square_on_scalar(roots13[:, span(first, count)], row13[:, span(first, count)])
-            inverse_root(roots13[:, span(first, count)], roots13[:, span(first, count)])
-            finish_damping(3, roots13[:, span(first, count)], first, count)
-        roots12_late = placed([P, HALF], F32, "roots12_late", roots_at + KIB)
-        inverse_root(roots12_late[:], squares12[:])
-        finish_damping(2, roots12_late, HALF, HALF)
-        roots13_late = placed([P, HALF], F32, "roots13_late", late_at)
-        inverse_root(roots13_late[:], squares13[:])
-        finish_damping(3, roots13_late, HALF, HALF)
+        for g, (first, count) in enumerate(GROUPS):
+            square_on_scalar(late_roots[g][:, 1, :], row13[:, span(first, count)])
+            inverse_root(late_roots[g][:, 1, :], late_roots[g][:, 1, :])
+            square_pair(damp1[g][:, 1], late_roots[g][:])
+        late_at = at["w20"] - 2 * KIB
 
         nc.sync.dma_start(out=w2_w[:].bitcast(I32), in_=w2_words.rearrange("b p c i -> p b (c i)").bitcast(I32))
         for q in range(P // QUADRANT):
@@ -310,7 +293,7 @@ def tile_list_wall_model_adjoint_kernel(
         load_src(1)
 
         woven1 = [
-            placed([P, PACK * count], BF16, f"woven1{g}", at["w11"] + PACK * 2 * first)
+            placed([P, PACK * count], BF16, f"woven1{g}", at["woven1"] + PACK * 2 * first)
             for g, (first, count) in enumerate(GROUPS)
         ]
         h_words1 = {0: kept([P, HALF], U32, "h_words10")}
@@ -318,7 +301,7 @@ def tile_list_wall_model_adjoint_kernel(
             for part in range(count // CHUNK):
                 damped(
                     sums(1, first // CHUNK + part),
-                    damp1[g][:, :, span(CHUNK * part, CHUNK)],
+                    damp1[g][:, :, span(CHUNK * part, CHUNK), :],
                     woven1[g][:, span(PACK * CHUNK * part, PACK * CHUNK)],
                 )
             if first < HALF:
@@ -355,7 +338,7 @@ def tile_list_wall_model_adjoint_kernel(
         h_words1[1] = placed([P, HALF], U32, "h_words11", ring_at)
         quantise(h_words1[1][:], h_sc[1][:, span(HALF, HALF)], woven1[2][:])
         result(1, 0, QUARTER, QUARTER, late_at + KIB, ring_at + 2 * KIB)
-        result(2, 1, 0, HALF, roots_at + KIB, at["w11"] + 4 * KIB)
+        result(2, 1, 0, HALF, late_at + 2 * KIB, at["woven1"] + 4 * KIB)
         number = 3
         for u in range(2):
             for m in range(PAGES):

@@ -31,31 +31,18 @@ MOVED_ROWS = 3 * QUADRANT + 4
 PAIR = 2
 
 KIB = 1024
-SLOT = 8 * KIB
 BANK = 2 * KIB
 
-SLOTS = (
-    ("shear00", "page2"),
-    ("shear01", "tab1", "w21"),
-    ("shear02", "v_sc0"),
-    ("shear03", "w11", "src0"),
-    ("shear11", "tab2", "page3"),
-    ("shear12", "w01", "src1"),
-    ("w00", "early_roots", "woven1"),
-    ("tab0", "shear13"),
-    ("before_w10",),
-    ("w10",),
-    ("behind_w10",),
-    ("shear10", "w20"),
-    ("rows_a",),
-    ("rows_b",),
-    ("damp0",),
-    ("damp0_rest",),
-    ("stage",),
-    ("stage_rest",),
-    ("woven0",),
-)
-GROUPS = ((0, QUARTER), (QUARTER, QUARTER), (HALF, HALF))
+PLACES = {
+    "values": 0, "shear00": 4, "shear10": 8, "tab0": 8, "codes00": 8, "tab2": 10, "w2": 10, "wgo": 14,
+    "shear01": 18, "shear11": 18, "tab1": 18, "w01": 18, "src0": 22,
+    "shear02": 30, "shear12": 30, "w10": 30, "w11": 30, "src1": 30,
+    "shear03": 38, "shear13": 38, "w20": 38, "w21": 38,
+    "w00": 54, "woven": 54,
+    "rows": 62, "page2": 62, "weighted": 70, "tab_sc": 78, "roots": 138,
+    "damp0": 94, "damp1": 110,
+    "rounded00": 66, "rounded10": 130, "rounded20": 154, "page3": 154, "rounded01": 146, "rounded11": 126, "rounded21": 130,
+}
 
 
 def tile_list_wall_model_adjoint_kernel(
@@ -67,7 +54,7 @@ def tile_list_wall_model_adjoint_kernel(
         arena = ctx.enter_context(tc.tile_pool(name="arena", bufs=1))
         psum = ctx.enter_context(tc.psum_pool(name="psum", bufs=1))
 
-        at = {name: SLOT * i for i, names in enumerate(SLOTS) for name in names}
+        at = {name: KIB * place for name, place in PLACES.items()}
 
         def placed(shape, dtype, name, offset):
             return arena.tile(shape, dtype, name=name, offset=offset, align_bytes=64)
@@ -93,7 +80,7 @@ def tile_list_wall_model_adjoint_kernel(
         first_window = shear_window(0, 0)
         nc.sync.dma_start(idx[:], offs)
 
-        tab_sc = kept([P, T], U8, "tab_sc")
+        tab_sc = placed([P, T], U8, "tab_sc", at["tab_sc"])
         nc.vector.memset(tab_sc[:].bitcast(I32), 0)
         for q in range(P // QUADRANT):
             nc.scalar.dma_start(
@@ -113,15 +100,10 @@ def tile_list_wall_model_adjoint_kernel(
         v_sc = {}
         w1_sc = {(a, b): kept([P, PASS], U8, f"w1_sc{a}{b}") for a in range(K_PASSES) for b in range(R_PASSES)}
         h_sc = [kept([P, S], U8, f"h_sc{b}") for b in range(R_PASSES)]
-        w2_w = kept([P, R_PASSES, N], U32, "w2_w")
-        wgo_sb = keep.tile([P, S], F32, name="wgo_sb")
-        damp0 = placed([P, PAIR, S, PAIR], F32, "damp0", at["damp0"])
-        damp1 = [
-            placed([P, PAIR, count, PAIR], F32, f"damp1_{g}", at["w10"] + KIB * (2, 6, -6)[g])
-            for g, (first, count) in enumerate(GROUPS)
-        ]
+        damp = [placed([P, PAIR, S, PAIR], F32, f"damp{b}", at[f"damp{b}"]) for b in range(R_PASSES)]
         w1_rounded = {}
         w1_words = {}
+        h_words = {}
         src_sb = {}
 
         def gather(out, window, offsets):
@@ -132,7 +114,7 @@ def tile_list_wall_model_adjoint_kernel(
             nc.gpsimd.memset(pages[m][:], 0.0)
 
         def gather_scales():
-            picked = placed([P, S], U8, "v_sc0", at["v_sc0"])
+            picked = kept([P, S], U8, "v_sc0")
             gather(picked[:], tab_sc, idx[:])
             v_sc[0] = picked[:]
             for a in range(1, K_PASSES):
@@ -150,15 +132,16 @@ def tile_list_wall_model_adjoint_kernel(
             )
             return window
 
-        def weight_piece(a, b, copy):
+        def weight_piece(a, b, copies):
             raw = placed([P, PACK, PASS], F32, f"w{a}{b}", at[f"w{a}{b}"])
             piece = w1[PASS * a : PASS * (a + 1), PASS * b : PASS * (b + 1)]
             nc.sync.dma_start(out=raw[:], in_=piece.rearrange("(p i) c -> p i c", i=PACK))
-            w1_rounded[a, b] = placed([P, PACK * PASS], BF16, f"rounded{a}{b}", at["stage"] + 4 * KIB * a)
-            copy(
-                out=w1_rounded[a, b][:].rearrange("p (t m i) -> p m i t", t=PACK, i=PACK),
-                in_=raw[:].rearrange("p i (m t) -> p m i t", t=PACK),
-            )
+            w1_rounded[a, b] = placed([P, PACK * PASS], BF16, f"rounded{a}{b}", at[f"rounded{a}{b}"])
+            dealt = w1_rounded[a, b][:].rearrange("p (t m i) -> p m i t", t=PACK, i=PACK)
+            given = raw[:].rearrange("p i (m t) -> p m i t", t=PACK)
+            share = PACK // len(copies)
+            for n, copy in enumerate(copies):
+                copy(out=dealt[:, :, :, span(share * n, share)], in_=given[:, :, :, span(share * n, share)])
 
         def quantise(words, scales, values):
             nc.vector.quantize_mx(out=words.bitcast(E4M3), scales=scales, in_=values)
@@ -168,21 +151,20 @@ def tile_list_wall_model_adjoint_kernel(
             w1_words[a, b] = kept([P, PASS], U32, name) if offset is None else placed([P, PASS], U32, name, offset)
             quantise(w1_words[a, b][:], w1_sc[a, b][:], w1_rounded[a, b][:])
 
-        def square(out, row):
-            nc.gpsimd.tensor_tensor(out=out, in0=row, in1=row, op=ALU.mult)
-
-        def square_on_scalar(out, row):
-            nc.scalar.activation(out=out, in_=row, func=ACT.Square)
-
-        def inverse_root(out, squares):
-            nc.scalar.activation(out=out, in_=squares, func=ACT.Abs_reciprocal_sqrt, bias=1.0)
-
-        def square_pair(out, roots):
-            square_on_scalar(out, roots.rearrange("p e j -> p j e"))
+        def damping_pair(b, u, between):
+            roots = placed([P, PAIR, S], F32, f"roots{b}{u}", at["roots"] + 8 * KIB * u)
+            for e in range(PAIR):
+                t = PAIR * u + e
+                row = placed([P, S], F32, f"row{b}{t}", at["rows"] + 4 * KIB * (PACK * b + t))
+                gather(row[:], first_window if (b, t) == (0, 0) else shear_window(b, t), idx[:])
+                nc.gpsimd.tensor_tensor(out=row[:], in0=row[:], in1=row[:], op=ALU.mult)
+                nc.scalar.activation(out=roots[:, e, :], in_=row[:], func=ACT.Abs_reciprocal_sqrt, bias=1.0)
+                between[e]()
+            nc.scalar.activation(out=damp[b][:, u], in_=roots[:].rearrange("p e j -> p j e"), func=ACT.Square)
 
         def sums(b, c):
             acc = psum.tile([P, PACK, CHUNK], F32, name=f"acc{b}{c}", offset=BANK * c)
-            passes = (0, 2, 1) if b == 0 and c >= CHUNKS // 2 else (0, 1, 2)
+            passes = (0, 2, 1) if c >= CHUNKS // 2 else (0, 1, 2)
             for a in passes:
                 for t in range(PACK):
                     nc.tensor.matmul_mx(
@@ -196,157 +178,121 @@ def tile_list_wall_model_adjoint_kernel(
                     )
             return acc
 
-        def damped(acc, damping, woven):
+        def damped(b, c, woven, part):
             nc.vector.tensor_tensor(
-                out=woven.rearrange("p (j u e) -> p j u e", u=PAIR, e=PAIR),
-                in0=acc[:].rearrange("p (u e) j -> p j u e", e=PAIR),
-                in1=damping.rearrange("p u j e -> p j u e"),
+                out=woven[:, span(PACK * CHUNK * part, PACK * CHUNK)].rearrange("p (j u e) -> p j u e", u=PAIR, e=PAIR),
+                in0=sums(b, c)[:].rearrange("p (u e) j -> p j u e", e=PAIR),
+                in1=damp[b][:, :, span(CHUNK * c, CHUNK), :].rearrange("p u j e -> p j u e"),
                 op=ALU.mult,
             )
 
-        def load_src(u):
-            src_sb[u] = placed([P, PAGES, HALF], F32, f"src{u}", at[f"src{u}"])
-            nc.sync.dma_start(out=src_sb[u][:], in_=src[:, span(HALF * u, HALF)].rearrange("(m p) j -> p m j", p=P))
+        def nothing():
+            return None
 
-        halves = [span(0, HALF), span(HALF, HALF)]
-        for u in range(PAIR):
-            rows0 = placed([P, PAIR, S], F32, f"rows0{u}", at[("rows_a", "rows_b")[u]])
-            for e in range(PAIR):
-                t = PAIR * u + e
-                gather(rows0[:, e, :], first_window if t == 0 else shear_window(0, t), idx[:])
-                if t == 0:
-                    clear_page(2)
-                if u == 0:
-                    for cut in halves:
-                        square_on_scalar(rows0[:, e, cut], rows0[:, e, cut])
-                else:
-                    square(rows0[:, e, :], rows0[:, e, :])
-                if t == PACK - 2:
-                    gather_scales()
-                for cut in halves:
-                    inverse_root(rows0[:, e, cut], rows0[:, e, cut])
-            for cut in halves:
-                square_pair(damp0[:, u, cut, :], rows0[:, :, cut])
-        rows = {}
-        for t, offset in enumerate((at["rows_a"], at["rows_a"] + 4 * KIB, at["v_sc0"] + KIB)):
-            rows[t] = placed([P, S], F32, f"row1{t}", offset)
-            gather(rows[t][:], shear_window(1, t), idx[:])
-            square(rows[t][:], rows[t][:])
+        def scales_and_first_weights():
+            gather_scales()
+            weight_piece(0, 0, [nc.scalar.copy])
 
-        weight_piece(0, 0, nc.scalar.copy)
+        damping_pair(0, 0, (nothing, nothing))
+        damping_pair(0, 1, (nothing, scales_and_first_weights))
+        damping_pair(1, 0, (nothing, nothing))
+        damping_pair(1, 1, (nothing, nothing))
+
         gather(v_words[0][:], table_window(0), idx[:])
-        weight_codes(0, 0)
-        early_roots = placed([P, PAIR, S], F32, "early_roots", at["early_roots"])
-        for e in range(PAIR):
-            inverse_root(early_roots[:, e, :], rows[e][:])
+        weight_codes(0, 0, at["codes00"])
+        clear_page(2)
         gather(v_words[1][:], table_window(1), idx[:])
-        weight_piece(1, 0, nc.scalar.copy)
-        for g, (first, count) in enumerate(GROUPS):
-            square_pair(damp1[g][:, 0], early_roots[:, :, span(first, count)])
-        weight_piece(2, 0, nc.vector.tensor_copy)
-        late_roots = [
-            placed([P, PAIR, count], F32, f"late_roots{g}", at["w20"] + KIB * (2, 4, -2)[g])
-            for g, (first, count) in enumerate(GROUPS)
-        ]
-        for g, (first, count) in enumerate(GROUPS):
-            inverse_root(late_roots[g][:, 0, :], rows[2][:, span(first, count)])
-        weight_codes(1, 0, at["w20"] + 6 * KIB)
+        weight_piece(1, 0, [nc.vector.tensor_copy])
+        weight_codes(1, 0)
+        weight_piece(2, 0, [nc.vector.tensor_copy])
         weight_codes(2, 0)
+        clear_page(3)
         window = table_window(2)
         for u in range(2):
             gather(v_words[2][:, span(HALF * u, HALF)], window, entries(idx, HALF * u, HALF))
-        clear_page(3)
 
-        weight_piece(0, 1, nc.scalar.copy)
+        woven = placed([P, PACK * HALF], BF16, "woven00", at["woven"])
+        for c in range(CHUNKS // 2):
+            damped(0, c, woven, c)
+        h_words[0, 0] = kept([P, HALF], U32, "h_words00")
+        quantise(h_words[0, 0][:], h_sc[0][:, span(0, HALF)], woven[:])
+        weight_piece(0, 1, [nc.scalar.copy])
         weight_codes(0, 1)
-        woven0 = [placed([P, PACK * HALF], BF16, f"woven0{u}", at["woven0"] + 4 * KIB * u) for u in range(2)]
-        for c in range(CHUNKS):
-            u, part = divmod(c, CHUNKS // 2)
-            damped(sums(0, c), damp0[:, :, span(CHUNK * c, CHUNK), :], woven0[u][:, span(PACK * CHUNK * part, PACK * CHUNK)])
-        weight_piece(1, 1, nc.scalar.copy)
+        woven = placed([P, PACK * HALF], BF16, "woven01", at["w01"])
+        for c in range(CHUNKS // 2):
+            damped(0, CHUNKS // 2 + c, woven, c)
+        weight_piece(1, 1, [nc.scalar.copy])
         weight_codes(1, 1)
-        weight_piece(2, 1, nc.scalar.copy)
+        weight_piece(2, 1, [nc.vector.tensor_copy, nc.scalar.copy])
+        weight_codes(2, 1)
+        h_words[0, 1] = placed([P, HALF], U32, "h_words01", at["w21"])
+        quantise(h_words[0, 1][:], h_sc[0][:, span(HALF, HALF)], woven[:])
 
-        window = shear_window(1, 3)
-        row13 = placed([P, S], F32, "row13", at["rows_b"])
-        for first, count in GROUPS:
-            gather(row13[:, span(first, count)], window, entries(idx, first, count))
-        weight_codes(2, 1, at["shear13"] + 4 * KIB)
-        h_words0 = placed([P, S], U32, "h_words0", at["shear13"])
-        for u in range(2):
-            quantise(h_words0[:, span(HALF * u, HALF)], h_sc[0][:, span(HALF * u, HALF)], woven0[u][:])
-        for g, (first, count) in enumerate(GROUPS):
-            square_on_scalar(late_roots[g][:, 1, :], row13[:, span(first, count)])
-            inverse_root(late_roots[g][:, 1, :], late_roots[g][:, 1, :])
-            square_pair(damp1[g][:, 1], late_roots[g][:])
-        late_at = at["w20"] - 2 * KIB
-
-        nc.sync.dma_start(out=w2_w[:].bitcast(I32), in_=w2_words.rearrange("b p c i -> p b (c i)").bitcast(I32))
         for q in range(P // QUADRANT):
             nc.sync.dma_start(
                 out=w2_sc[QUADRANT * q : QUADRANT * q + 4 * R_PASSES, :].bitcast(I32),
                 in_=w2_scales[:, 4 * q : 4 * q + 4, :].bitcast(I32),
             )
         nc.sync.dma_start(idx2[:], offs2)
-        load_src(0)
+        w2_w = placed([P, R_PASSES, N], U32, "w2_w", at["w2"])
+        nc.sync.dma_start(out=w2_w[:].bitcast(I32), in_=w2_words.rearrange("b p c i -> p b (c i)").bitcast(I32))
+        wgo_sb = placed([P, S], F32, "wgo_sb", at["wgo"])
         nc.sync.dma_start(out=wgo_sb[:], in_=wgo)
-        load_src(1)
+        for u in range(2):
+            src_sb[u] = placed([P, PAGES, HALF], F32, f"src{u}", at[f"src{u}"])
+            nc.sync.dma_start(out=src_sb[u][:], in_=src[:, span(HALF * u, HALF)].rearrange("(m p) j -> p m j", p=P))
 
-        woven1 = [
-            placed([P, PACK * count], BF16, f"woven1{g}", at["woven1"] + PACK * 2 * first)
-            for g, (first, count) in enumerate(GROUPS)
-        ]
-        h_words1 = {0: kept([P, HALF], U32, "h_words10")}
-        for g, (first, count) in enumerate(GROUPS):
-            for part in range(count // CHUNK):
-                damped(
-                    sums(1, first // CHUNK + part),
-                    damp1[g][:, :, span(CHUNK * part, CHUNK), :],
-                    woven1[g][:, span(PACK * CHUNK * part, PACK * CHUNK)],
-                )
-            if first < HALF:
-                quantise(h_words1[0][:, span(first, count)], h_sc[1][:, span(first, count)], woven1[g][:])
+        quarters = [placed([P, PACK * QUARTER], BF16, f"woven1{g}", at["woven"] + KIB * (4 + 2 * g)) for g in range(2)]
+        last_half = placed([P, PACK * HALF], BF16, "woven12", at["damp0"] + 3 * KIB)
+        h_words[1, 0] = kept([P, HALF], U32, "h_words10")
 
-        diff_at = at["damp0"]
+        def quarter_codes(g):
+            cut = span(QUARTER * g, QUARTER)
+            quantise(h_words[1, 0][:, cut], h_sc[1][:, cut], quarters[g][:])
 
-        def result(number, m, first, count, values_at, weighted_at):
+        damped(1, 0, quarters[0], 0)
+        damped(1, 1, quarters[0], 1)
+        damped(1, 2, quarters[1], 0)
+        quarter_codes(0)
+        damped(1, 3, quarters[1], 1)
+        damped(1, 4, last_half, 0)
+        quarter_codes(1)
+        for part in range(1, CHUNKS // 2):
+            damped(1, CHUNKS // 2 + part, last_half, part)
+
+        def result(number, m, first, count, before_scatter=nothing):
             u, inside = divmod(first, HALF)
             y = psum.tile([P, count], F32, name=f"y{number}", offset=BANK * (number % CHUNKS))
-            words = (h_words0[:, span(first, count)], h_words1[u][:, span(inside, count)])
             for b in range(R_PASSES):
                 nc.tensor.matmul_mx(
                     out=y[:],
                     lhsT=w2_w[:, b, span(P * m, P)].bitcast(E4M3),
                     lhsT_scale=w2_sc[4 * b : P, span(P * m, P)],
-                    rhs=words[b].bitcast(E4M3),
+                    rhs=h_words[b, u][:, span(inside, count)].bitcast(E4M3),
                     rhs_scale=h_sc[b][:, span(first, count)],
                     start=(b == 0),
                     stop=(b == R_PASSES - 1),
                 )
-            values = placed([P, count], F32, f"values{number}", values_at)
+            values = placed([P, count], F32, f"values{number}", at["values"] + 2 * KIB * (number % 3))
             nc.scalar.copy(out=values[:], in_=y[:])
-            diff = placed([P, count], F32, f"diff{number}", diff_at)
+            diff = placed([P, count], F32, f"diff{number}", at["damp0"] + KIB * (1 if number <= 4 else 2))
             nc.gpsimd.tensor_tensor(
                 out=diff[:], in0=values[:], in1=src_sb[u][:, m, span(inside, count)], op=ALU.subtract
             )
-            weighted = placed([P, count], F32, f"weighted{number}", weighted_at)
+            weighted = placed([P, count], F32, f"weighted{number}", at["weighted"] + 2 * KIB * (number % 3))
             nc.gpsimd.tensor_tensor(out=weighted[:], in0=diff[:], in1=wgo_sb[:, span(first, count)], op=ALU.mult)
+            before_scatter()
             nc.vector.tensor_copy(out=pages[m][:].indirect(entries(idx2, first, count)), in_=weighted[:])
 
-        ring_at = at["damp0"] + 2 * KIB
-        result(0, 0, 0, QUARTER, late_at, ring_at)
-        h_words1[1] = placed([P, HALF], U32, "h_words11", ring_at)
-        quantise(h_words1[1][:], h_sc[1][:, span(HALF, HALF)], woven1[2][:])
-        result(1, 0, QUARTER, QUARTER, late_at + KIB, ring_at + 2 * KIB)
-        result(2, 1, 0, HALF, late_at + 2 * KIB, at["woven1"] + 4 * KIB)
-        number = 3
-        for u in range(2):
-            for m in range(PAGES):
-                if u == 1 or m >= 2:
-                    result(
-                        number, m, HALF * u, HALF,
-                        ring_at + 2 * KIB * (2 + number % 2), ring_at + 2 * KIB * (4 + number % 3),
-                    )
-                    number = number + 1
-                if u == 1:
-                    nc.sync.dma_start(out=out[span(P * m, P), :], in_=pages[m][:])
+        def last_codes():
+            h_words[1, 1] = placed([P, HALF], U32, "h_words11", at["damp0"])
+            quantise(h_words[1, 1][:], h_sc[1][:, span(HALF, HALF)], last_half[:])
+
+        for g in range(2):
+            for m in range(2):
+                result(2 * g + m, m, QUARTER * g, QUARTER)
+        result(4, 2, 0, HALF, last_codes)
+        result(5, 3, 0, HALF)
+        for m in range(PAGES):
+            result(6 + m, m, HALF, HALF)
+            nc.sync.dma_start(out=out[span(P * m, P), :], in_=pages[m][:])

@@ -34,15 +34,21 @@ KIB = 1024
 BANK = 2 * KIB
 
 PLACES = {
-    "values": 0, "shear00": 4, "shear10": 8, "tab0": 8, "codes00": 8, "tab2": 10, "w2": 10, "wgo": 14,
-    "shear01": 18, "shear11": 18, "tab1": 18, "w01": 18, "src0": 22,
-    "shear02": 30, "shear12": 30, "w10": 30, "w11": 30, "src1": 30,
-    "shear03": 38, "shear13": 38, "w20": 38, "w21": 38,
-    "w00": 54, "woven": 54,
-    "rows": 62, "page2": 62, "weighted": 70, "tab_sc": 78, "roots": 138,
-    "damp0": 94, "damp1": 110,
-    "rounded00": 66, "rounded10": 130, "rounded20": 154, "page3": 154, "rounded01": 146, "rounded11": 126, "rounded21": 130,
+    "shear00": 0, "w00": 0, "roots10": 0, "rounded01": 0,
+    "shear01": 8, "tab0": 8, "codes00": 8, "woven": 10,
+    "shear02": 21, "picked": 28, "tab1": 20, "w11": 20, "src1": 20,
+    "shear11": 37, "tab2": 37, "w2": 38, "wgo": 42,
+    "shear03": 46, "w10": 46, "w21": 46,
+    "shear12": 54, "w01": 54, "src0": 56,
+    "rows": 64, "codes21": 64, "row13_0": 65.5, "row13_2": 66, "row13_1": 68, "late_squares": 69.5, "tab_sc": 76, "weighted": 72, "values": 140,
+    "roots00": 92, "rounded11": 92, "roots01": 100, "rounded21": 100,
+    "damp0": 108,
+    "damp1_2": 124, "shear10": 130, "w20": 130, "damp1_0": 132, "damp1_1": 136,
+    "late_roots": 80,
+    "rounded00": 148, "page2": 148, "rounded20": 156, "page3": 156,
+    "rounded10": 164, "shear13": 164,
 }
+GROUPS = ((0, QUARTER), (QUARTER, QUARTER), (HALF, HALF))
 
 
 def tile_list_wall_model_adjoint_kernel(
@@ -54,7 +60,7 @@ def tile_list_wall_model_adjoint_kernel(
         arena = ctx.enter_context(tc.tile_pool(name="arena", bufs=1))
         psum = ctx.enter_context(tc.psum_pool(name="psum", bufs=1))
 
-        at = {name: KIB * place for name, place in PLACES.items()}
+        at = {name: int(KIB * place) for name, place in PLACES.items()}
 
         def placed(shape, dtype, name, offset):
             return arena.tile(shape, dtype, name=name, offset=offset, align_bytes=64)
@@ -77,13 +83,14 @@ def tile_list_wall_model_adjoint_kernel(
 
         idx = keep.tile([P, S // 16], U16, name="idx")
         idx2 = keep.tile([P, S // 16], U16, name="idx2")
-        first_window = shear_window(0, 0)
+        windows = {(0, 0): shear_window(0, 0)}
         nc.sync.dma_start(idx[:], offs)
 
         tab_sc = placed([P, T], U8, "tab_sc", at["tab_sc"])
         nc.vector.memset(tab_sc[:].bitcast(I32), 0)
+        windows[0, 1] = shear_window(0, 1)
         for q in range(P // QUADRANT):
-            nc.scalar.dma_start(
+            nc.sync.dma_start(
                 out=tab_sc[QUADRANT * q : QUADRANT * q + 4 * K_PASSES, :].bitcast(I32),
                 in_=tab_scales[:, 4 * q : 4 * q + 4, :].bitcast(I32),
             )
@@ -100,7 +107,11 @@ def tile_list_wall_model_adjoint_kernel(
         v_sc = {}
         w1_sc = {(a, b): kept([P, PASS], U8, f"w1_sc{a}{b}") for a in range(K_PASSES) for b in range(R_PASSES)}
         h_sc = [kept([P, S], U8, f"h_sc{b}") for b in range(R_PASSES)]
-        damp = [placed([P, PAIR, S, PAIR], F32, f"damp{b}", at[f"damp{b}"]) for b in range(R_PASSES)]
+        damp0 = placed([P, PAIR, S, PAIR], F32, "damp0", at["damp0"])
+        damp1 = [
+            placed([P, PAIR, count, PAIR], F32, f"damp1_{g}", at[f"damp1_{g}"])
+            for g, (first, count) in enumerate(GROUPS)
+        ]
         w1_rounded = {}
         w1_words = {}
         h_words = {}
@@ -109,12 +120,8 @@ def tile_list_wall_model_adjoint_kernel(
         def gather(out, window, offsets):
             nc.vector.tensor_copy(out=out, in_=window[:].indirect(offsets))
 
-        def clear_page(m):
-            pages[m] = placed([P, T2], F32, f"page{m}", at[f"page{m}"])
-            nc.gpsimd.memset(pages[m][:], 0.0)
-
         def gather_scales():
-            picked = kept([P, S], U8, "v_sc0")
+            picked = placed([P, S], U8, "picked", at["picked"])
             gather(picked[:], tab_sc, idx[:])
             v_sc[0] = picked[:]
             for a in range(1, K_PASSES):
@@ -151,20 +158,38 @@ def tile_list_wall_model_adjoint_kernel(
             w1_words[a, b] = kept([P, PASS], U32, name) if offset is None else placed([P, PASS], U32, name, offset)
             quantise(w1_words[a, b][:], w1_sc[a, b][:], w1_rounded[a, b][:])
 
-        def damping_pair(b, u, between):
-            roots = placed([P, PAIR, S], F32, f"roots{b}{u}", at["roots"] + 8 * KIB * u)
+        def clear_page(m):
+            pages[m] = placed([P, T2], F32, f"page{m}", at[f"page{m}"])
+            nc.gpsimd.memset(pages[m][:], 0.0)
+
+        def square_on_gpsimd(out, row):
+            nc.gpsimd.tensor_tensor(out=out, in0=row, in1=row, op=ALU.mult)
+
+        def square_on_scalar(out, row):
+            nc.scalar.activation(out=out, in_=row, func=ACT.Square)
+
+        def inverse_root(out, squares):
+            nc.scalar.activation(out=out, in_=squares, func=ACT.Abs_reciprocal_sqrt, bias=1.0)
+
+        def square_pair(out, roots):
+            square_on_scalar(out, roots.rearrange("p e j -> p j e"))
+
+        def squared_row(b, t):
+            row = placed([P, S], F32, f"row{b}{t}", at["rows"] + 4 * KIB * (PACK * b + t))
+            gather(row[:], windows[b, t] if (b, t) in windows else shear_window(b, t), idx[:])
+            square_on_gpsimd(row[:], row[:])
+            return row
+
+        def pair_roots(b, u, between):
+            roots = placed([P, PAIR, S], F32, f"roots{b}{u}", at[f"roots{b}{u}"])
             for e in range(PAIR):
-                t = PAIR * u + e
-                row = placed([P, S], F32, f"row{b}{t}", at["rows"] + 4 * KIB * (PACK * b + t))
-                gather(row[:], first_window if (b, t) == (0, 0) else shear_window(b, t), idx[:])
-                nc.gpsimd.tensor_tensor(out=row[:], in0=row[:], in1=row[:], op=ALU.mult)
-                nc.scalar.activation(out=roots[:, e, :], in_=row[:], func=ACT.Abs_reciprocal_sqrt, bias=1.0)
+                inverse_root(roots[:, e, :], squared_row(b, PAIR * u + e)[:])
                 between[e]()
-            nc.scalar.activation(out=damp[b][:, u], in_=roots[:].rearrange("p e j -> p j e"), func=ACT.Square)
+            return roots
 
         def sums(b, c):
             acc = psum.tile([P, PACK, CHUNK], F32, name=f"acc{b}{c}", offset=BANK * c)
-            passes = (0, 2, 1) if c >= CHUNKS // 2 else (0, 1, 2)
+            passes = (0, 2, 1) if b == 0 and c >= CHUNKS // 2 else (0, 1, 2)
             for a in passes:
                 for t in range(PACK):
                     nc.tensor.matmul_mx(
@@ -178,55 +203,82 @@ def tile_list_wall_model_adjoint_kernel(
                     )
             return acc
 
-        def damped(b, c, woven, part):
+        def damped(b, c, damping, woven, part):
             nc.vector.tensor_tensor(
                 out=woven[:, span(PACK * CHUNK * part, PACK * CHUNK)].rearrange("p (j u e) -> p j u e", u=PAIR, e=PAIR),
                 in0=sums(b, c)[:].rearrange("p (u e) j -> p j u e", e=PAIR),
-                in1=damp[b][:, :, span(CHUNK * c, CHUNK), :].rearrange("p u j e -> p j u e"),
+                in1=damping.rearrange("p u j e -> p j u e"),
                 op=ALU.mult,
             )
 
         def nothing():
             return None
 
-        def scales_and_first_weights():
-            gather_scales()
-            weight_piece(0, 0, [nc.scalar.copy])
-
-        damping_pair(0, 0, (nothing, nothing))
-        damping_pair(0, 1, (nothing, scales_and_first_weights))
-        damping_pair(1, 0, (nothing, nothing))
-        damping_pair(1, 1, (nothing, nothing))
+        square_pair(damp0[:, 0], pair_roots(0, 0, (nothing, nothing))[:])
+        square_pair(damp0[:, 1], pair_roots(0, 1, (gather_scales, nothing))[:])
+        rows = [squared_row(1, t) for t in range(PACK - 1)]
+        weight_piece(0, 0, [nc.scalar.copy])
+        roots = placed([P, PAIR, S], F32, "roots10", at["roots10"])
+        for e in range(PAIR):
+            inverse_root(roots[:, e, :], rows[e][:])
+        late_roots = [
+            placed([P, PAIR, count], F32, f"late_roots{g}", at["late_roots"] + 8 * first)
+            for g, (first, count) in enumerate(GROUPS)
+        ]
+        for g, (first, count) in enumerate(GROUPS):
+            inverse_root(late_roots[g][:, 0, :], rows[2][:, span(first, count)])
 
         gather(v_words[0][:], table_window(0), idx[:])
         weight_codes(0, 0, at["codes00"])
         clear_page(2)
         gather(v_words[1][:], table_window(1), idx[:])
-        weight_piece(1, 0, [nc.vector.tensor_copy])
-        weight_codes(1, 0)
-        weight_piece(2, 0, [nc.vector.tensor_copy])
-        weight_codes(2, 0)
+        for a in range(1, K_PASSES):
+            weight_piece(a, 0, [nc.vector.tensor_copy, nc.scalar.copy])
+            weight_codes(a, 0)
         clear_page(3)
+        for g, (first, count) in enumerate(GROUPS):
+            square_pair(damp1[g][:, 0], roots[:, :, span(first, count)])
         window = table_window(2)
         for u in range(2):
             gather(v_words[2][:, span(HALF * u, HALF)], window, entries(idx, HALF * u, HALF))
 
-        woven = placed([P, PACK * HALF], BF16, "woven00", at["woven"])
-        for c in range(CHUNKS // 2):
-            damped(0, c, woven, c)
-        h_words[0, 0] = kept([P, HALF], U32, "h_words00")
-        quantise(h_words[0, 0][:], h_sc[0][:, span(0, HALF)], woven[:])
+        def products(first, count, offset):
+            woven = placed([P, PACK * count], BF16, f"woven0_{first}", offset)
+            for part in range(count // CHUNK):
+                c = first // CHUNK + part
+                damped(0, c, damp0[:, :, span(CHUNK * c, CHUNK), :], woven, part)
+            return woven
+
+        def codes(first, count, woven):
+            u, inside = divmod(first, HALF)
+            quantise(h_words[0, u][:, span(inside, count)], h_sc[0][:, span(first, count)], woven[:])
+
+        for u in range(2):
+            h_words[0, u] = kept([P, HALF], U32, f"h_words0{u}")
+        first_half = products(0, HALF, at["woven"])
+        third_quarter = products(HALF, QUARTER, at["woven"] + 8 * KIB)
+        codes(0, HALF, first_half)
         weight_piece(0, 1, [nc.scalar.copy])
         weight_codes(0, 1)
-        woven = placed([P, PACK * HALF], BF16, "woven01", at["w01"])
-        for c in range(CHUNKS // 2):
-            damped(0, CHUNKS // 2 + c, woven, c)
+        last_quarter = products(HALF + QUARTER, QUARTER, at["w01"])
+        codes(HALF, QUARTER, third_quarter)
         weight_piece(1, 1, [nc.scalar.copy])
         weight_codes(1, 1)
-        weight_piece(2, 1, [nc.vector.tensor_copy, nc.scalar.copy])
-        weight_codes(2, 1)
-        h_words[0, 1] = placed([P, HALF], U32, "h_words01", at["w21"])
-        quantise(h_words[0, 1][:], h_sc[0][:, span(HALF, HALF)], woven[:])
+        codes(HALF + QUARTER, QUARTER, last_quarter)
+        weight_piece(2, 1, [nc.scalar.copy])
+
+        window = shear_window(1, 3)
+        for g, (first, count) in enumerate(GROUPS):
+            if g == len(GROUPS) - 1:
+                weight_codes(2, 1, at["codes21"])
+            row = placed([P, count], F32, f"row13_{g}", at[f"row13_{g}"])
+            gather(row[:], window, entries(idx, first, count))
+            for part in range(0, count, QUARTER):
+                cut = span(part, QUARTER)
+                squares = placed([P, QUARTER], F32, f"late_squares{first + part}", at["late_squares"] + (0, 0, -KIB // 2, KIB // 2)[(first + part) // QUARTER])[:]
+                (square_on_scalar if g == 0 else square_on_gpsimd)(squares, row[:, cut])
+                inverse_root(late_roots[g][:, 1, cut], squares)
+                square_pair(damp1[g][:, 1, cut, :], late_roots[g][:, :, cut])
 
         for q in range(P // QUADRANT):
             nc.sync.dma_start(
@@ -250,15 +302,15 @@ def tile_list_wall_model_adjoint_kernel(
             cut = span(QUARTER * g, QUARTER)
             quantise(h_words[1, 0][:, cut], h_sc[1][:, cut], quarters[g][:])
 
-        damped(1, 0, quarters[0], 0)
-        damped(1, 1, quarters[0], 1)
-        damped(1, 2, quarters[1], 0)
-        quarter_codes(0)
-        damped(1, 3, quarters[1], 1)
-        damped(1, 4, last_half, 0)
-        quarter_codes(1)
-        for part in range(1, CHUNKS // 2):
-            damped(1, CHUNKS // 2 + part, last_half, part)
+        def product(c):
+            g = min(c // 2, 2)
+            part = c - GROUPS[g][0] // CHUNK
+            damped(1, c, damp1[g][:, :, span(CHUNK * part, CHUNK), :], (quarters + [last_half])[g], part)
+
+        for c in range(CHUNKS):
+            product(c)
+            if c in (2, 4):
+                quarter_codes(c // 2 - 1)
 
         def result(number, m, first, count, before_scatter=nothing):
             u, inside = divmod(first, HALF)
@@ -275,7 +327,7 @@ def tile_list_wall_model_adjoint_kernel(
                 )
             values = placed([P, count], F32, f"values{number}", at["values"] + 2 * KIB * (number % 3))
             nc.scalar.copy(out=values[:], in_=y[:])
-            diff = placed([P, count], F32, f"diff{number}", at["damp0"] + KIB * (1 if number <= 4 else 2))
+            diff = placed([P, count], F32, f"diff{number}", at["damp0"] + KIB * ((1, 2, 1, 2, 1)[number] if number <= 4 else (8, 2)[number % 2]))
             nc.gpsimd.tensor_tensor(
                 out=diff[:], in0=values[:], in1=src_sb[u][:, m, span(inside, count)], op=ALU.subtract
             )

@@ -37,7 +37,7 @@ PLACES = {
     "shear00": 0, "w00": 0, "roots10": 0, "rounded01": 0,
     "shear01": 8, "tab0": 8, "codes00": 8, "woven": 10,
     "shear02": 21, "picked": 28, "tab1": 20, "w11": 20, "src1": 20,
-    "shear11": 37, "tab2": 37, "w2": 38, "wgo": 42,
+    "shear11": 37, "tab2": 37, "w2_sc": 37, "w2": 38, "wgo": 42,
     "shear03": 46, "w10": 46, "w21": 46,
     "shear12": 54, "w01": 54, "src0": 56,
     "rows": 64, "codes21": 64, "row13_0": 65.5, "row13_2": 66, "row13_1": 68, "late_squares": 69.5, "tab_sc": 76, "weighted": 72, "values": 140,
@@ -88,14 +88,11 @@ def tile_list_wall_model_adjoint_kernel(
 
         tab_sc = placed([P, T], U8, "tab_sc", at["tab_sc"])
         nc.vector.memset(tab_sc[:].bitcast(I32), 0)
-        windows[0, 1] = shear_window(0, 1)
         for q in range(P // QUADRANT):
-            nc.sync.dma_start(
+            nc.gpsimd.dma_start(
                 out=tab_sc[QUADRANT * q : QUADRANT * q + 4 * K_PASSES, :].bitcast(I32),
                 in_=tab_scales[:, 4 * q : 4 * q + 4, :].bitcast(I32),
             )
-        w2_sc = kept([P, N], U8, "w2_sc")
-        nc.vector.memset(w2_sc[:].bitcast(I32), 0)
         moved_sc = kept([P, (K_PASSES - 1) * S], U8, "moved_sc")
         nc.vector.memset(moved_sc[:].bitcast(I32), 0)
         pages = {}
@@ -280,6 +277,8 @@ def tile_list_wall_model_adjoint_kernel(
                 inverse_root(late_roots[g][:, 1, cut], squares)
                 square_pair(damp1[g][:, 1, cut, :], late_roots[g][:, :, cut])
 
+        w2_sc = placed([P, N], U8, "w2_sc", at["w2_sc"])
+        nc.gpsimd.memset(w2_sc[:].bitcast(I32), 0)
         for q in range(P // QUADRANT):
             nc.sync.dma_start(
                 out=w2_sc[QUADRANT * q : QUADRANT * q + 4 * R_PASSES, :].bitcast(I32),

from contextlib import ExitStack

import concourse.mybir as mybir

K, H, N, T, S, T2 = 1536, 1024, 512, 2048, 1024, 2048
FLOPS = 2 * K * H * S + 2 * H * N * S

F32 = mybir.dt.float32
BF16 = mybir.dt.bfloat16
I32 = mybir.dt.int32
U32 = mybir.dt.uint32
U16 = mybir.dt.uint16
U8 = mybir.dt.uint8
E4M3 = mybir.dt.float8_e4m3fn_x4
E5M2 = mybir.dt.float8_e5m2_x4
ACT = mybir.ActivationFunctionType
ALU = mybir.AluOpType

P = 128
PACK = 4
PASS = P * PACK
K_PASSES = K // PASS
R_PASSES = H // PASS
PAGES = N // P
CHUNK = 128
CHUNKS = S // CHUNK
HALF = S // 2
QUARTER = S // 4
QUADRANT = 32
MOVED_ROWS = 3 * QUADRANT + 4
PAIR = 2

KIB = 1024
BANK = 2 * KIB

PLACES = {
    "shear00": 0, "w00": 0, "roots10": 0, "rounded01": 0,
    "shear01": 8, "tab0": 8, "codes00": 8, "woven": 10,
    "shear02": 21, "picked": 28, "tab1": 20, "w11": 20, "src1": 20,
    "shear11": 37, "tab2": 37, "w2_sc": 37, "w2": 38, "wgo": 42,
    "shear03": 46, "w10": 46, "w21": 46,
    "shear12": 54, "w01": 54, "src0": 56,
    "rows": 64, "codes21": 64, "row13_0": 65.5, "row13_2": 66, "row13_1": 68, "late_squares": 69.5, "tab_sc": 76, "weighted": 72, "values": 140,
    "roots00": 92, "rounded11": 92, "roots01": 100, "rounded21": 100,
    "damp0": 108,
    "damp1_2": 124, "shear10": 130, "w20": 130, "damp1_0": 132, "damp1_1": 136,
    "late_roots": 80,
    "rounded00": 148, "page2": 148, "rounded20": 156, "page3": 156,
    "rounded10": 164, "shear13": 164,
}
GROUPS = ((0, QUARTER), (QUARTER, QUARTER), (HALF, HALF))


def tile_list_wall_model_adjoint_kernel(
    tc, tab_words, tab_scales, offs, offs2, w1, w2_words, w2_scales, sT, src, wgo, out
):
    nc = tc.nc
    with ExitStack() as ctx:
        keep = ctx.enter_context(tc.tile_pool(name="keep", bufs=1))
        arena = ctx.enter_context(tc.tile_pool(name="arena", bufs=1))
        psum = ctx.enter_context(tc.psum_pool(name="psum", bufs=1))

        at = {name: int(KIB * place) for name, place in PLACES.items()}

        def placed(shape, dtype, name, offset):
            return arena.tile(shape, dtype, name=name, offset=offset, align_bytes=64)

        def kept(shape, dtype, name):
            return keep.tile(shape, dtype, name=name, align_bytes=64)

        def span(first, count):
            return slice(first, first + count)

        def entries(offsets, first, count):
            return offsets[:, first // 16 : (first + count) // 16]

        shear_rows = sT.rearrange("(b p t) c -> b t p c", b=R_PASSES, t=PACK)

        def shear_window(b, t):
            window = placed([P, T], F32, f"shear{b}{t}", at[f"shear{b}{t}"])
            nc.sync.dma_start(out=window[:], in_=shear_rows[b, t])
            return window

        idx = keep.tile([P, S // 16], U16, name="idx")
        idx2 = keep.tile([P, S // 16], U16, name="idx2")
        windows = {(0, 0): shear_window(0, 0)}
        nc.sync.dma_start(idx[:], offs)

        tab_sc = placed([P, T], U8, "tab_sc", at["tab_sc"])
        nc.vector.memset(tab_sc[:].bitcast(I32), 0)
        for q in range(P // QUADRANT):
            nc.gpsimd.dma_start(
                out=tab_sc[QUADRANT * q : QUADRANT * q + 4 * K_PASSES, :].bitcast(I32),
                in_=tab_scales[:, 4 * q : 4 * q + 4, :].bitcast(I32),
            )
        moved_sc = kept([P, (K_PASSES - 1) * S], U8, "moved_sc")
        nc.vector.memset(moved_sc[:].bitcast(I32), 0)
        pages = {}
        for m in range(2):
            pages[m] = keep.tile([P, T2], F32, name=f"page{m}")
            nc.vector.memset(pages[m][:], 0.0)

        v_words = [kept([P, S], U32, f"v_words{a}") for a in range(K_PASSES)]
        v_sc = {}
        w1_sc = {(a, b): kept([P, PASS], U8, f"w1_sc{a}{b}") for a in range(K_PASSES) for b in range(R_PASSES)}
        h_sc = [kept([P, S], U8, f"h_sc{b}") for b in range(R_PASSES)]
        damp0 = placed([P, PAIR, S, PAIR], F32, "damp0", at["damp0"])
        damp1 = [
            placed([P, PAIR, count, PAIR], F32, f"damp1_{g}", at[f"damp1_{g}"])
            for g, (first, count) in enumerate(GROUPS)
        ]
        w1_rounded = {}
        w1_words = {}
        h_words = {}
        src_sb = {}

        def gather(out, window, offsets):
            nc.vector.tensor_copy(out=out, in_=window[:].indirect(offsets))

        def gather_scales():
            picked = placed([P, S], U8, "picked", at["picked"])
            gather(picked[:], tab_sc, idx[:])
            v_sc[0] = picked[:]
            for a in range(1, K_PASSES):
                v_sc[a] = moved_sc[:, span(S * (a - 1), S)]
                nc.gpsimd.dma_start(
                    out=moved_sc[0:MOVED_ROWS, span(S * (a - 1), S)].bitcast(I32),
                    in_=picked[4 * a : 4 * a + MOVED_ROWS, :].bitcast(I32),
                )

        def table_window(a):
            window = placed([P, T], U32, f"tab{a}", at[f"tab{a}"])
            nc.sync.dma_start(
                out=window[:].bitcast(I32),
                in_=tab_words[a].rearrange("p t i -> p (t i)").bitcast(I32),
            )
            return window

        def weight_piece(a, b, copies):
            raw = placed([P, PACK, PASS], F32, f"w{a}{b}", at[f"w{a}{b}"])
            piece = w1[PASS * a : PASS * (a + 1), PASS * b : PASS * (b + 1)]
            nc.sync.dma_start(out=raw[:], in_=piece.rearrange("(p i) c -> p i c", i=PACK))
            w1_rounded[a, b] = placed([P, PACK * PASS], BF16, f"rounded{a}{b}", at[f"rounded{a}{b}"])
            dealt = w1_rounded[a, b][:].rearrange("p (t m i) -> p m i t", t=PACK, i=PACK)
            given = raw[:].rearrange("p i (m t) -> p m i t", t=PACK)
            share = PACK // len(copies)
            for n, copy in enumerate(copies):
                copy(out=dealt[:, :, :, span(share * n, share)], in_=given[:, :, :, span(share * n, share)])

        def quantise(words, scales, values):
            nc.vector.quantize_mx(out=words.bitcast(E4M3), scales=scales, in_=values)

        def weight_codes(a, b, offset=None):
            name = f"w1_words{a}{b}"
            w1_words[a, b] = kept([P, PASS], U32, name) if offset is None else placed([P, PASS], U32, name, offset)
            quantise(w1_words[a, b][:], w1_sc[a, b][:], w1_rounded[a, b][:])

        def clear_page(m):
            pages[m] = placed([P, T2], F32, f"page{m}", at[f"page{m}"])
            nc.gpsimd.memset(pages[m][:], 0.0)

        def square_on_gpsimd(out, row):
            nc.gpsimd.tensor_tensor(out=out, in0=row, in1=row, op=ALU.mult)

        def square_on_scalar(out, row):
            nc.scalar.activation(out=out, in_=row, func=ACT.Square)

        def inverse_root(out, squares):
            nc.scalar.activation(out=out, in_=squares, func=ACT.Abs_reciprocal_sqrt, bias=1.0)

        def square_pair(out, roots):
            square_on_scalar(out, roots.rearrange("p e j -> p j e"))

        def squared_row(b, t):
            row = placed([P, S], F32, f"row{b}{t}", at["rows"] + 4 * KIB * (PACK * b + t))
            gather(row[:], windows[b, t] if (b, t) in windows else shear_window(b, t), idx[:])
            square_on_gpsimd(row[:], row[:])
            return row

        def pair_roots(b, u, between):
            roots = placed([P, PAIR, S], F32, f"roots{b}{u}", at[f"roots{b}{u}"])
            for e in range(PAIR):
                inverse_root(roots[:, e, :], squared_row(b, PAIR * u + e)[:])
                between[e]()
            return roots

        def sums(b, c):
            acc = psum.tile([P, PACK, CHUNK], F32, name=f"acc{b}{c}", offset=BANK * c)
            passes = (0, 2, 1) if b == 0 and c >= CHUNKS // 2 else (0, 1, 2)
            for a in passes:
                for t in range(PACK):
                    nc.tensor.matmul_mx(
                        out=acc[:, t, :],
                        lhsT=w1_words[a, b][:, span(P * t, P)].bitcast(E4M3),
                        lhsT_scale=w1_sc[a, b][:, span(P * t, P)],
                        rhs=v_words[a][:, span(CHUNK * c, CHUNK)].bitcast(E5M2),
                        rhs_scale=v_sc[a][:, span(CHUNK * c, CHUNK)],
                        start=(a == passes[0] and t == 0),
                        stop=(a == passes[-1] and t == PACK - 1),
                    )
            return acc

        def damped(b, c, damping, woven, part):
            nc.vector.tensor_tensor(
                out=woven[:, span(PACK * CHUNK * part, PACK * CHUNK)].rearrange("p (j u e) -> p j u e", u=PAIR, e=PAIR),
                in0=sums(b, c)[:].rearrange("p (u e) j -> p j u e", e=PAIR),
                in1=damping.rearrange("p u j e -> p j u e"),
                op=ALU.mult,
            )

        def nothing():
            return None

        square_pair(damp0[:, 0], pair_roots(0, 0, (nothing, nothing))[:])
        square_pair(damp0[:, 1], pair_roots(0, 1, (gather_scales, nothing))[:])
        rows = [squared_row(1, t) for t in range(PACK - 1)]
        weight_piece(0, 0, [nc.scalar.copy])
        roots = placed([P, PAIR, S], F32, "roots10", at["roots10"])
        for e in range(PAIR):
            inverse_root(roots[:, e, :], rows[e][:])
        late_roots = [
            placed([P, PAIR, count], F32, f"late_roots{g}", at["late_roots"] + 8 * first)
            for g, (first, count) in enumerate(GROUPS)
        ]
        for g, (first, count) in enumerate(GROUPS):
            inverse_root(late_roots[g][:, 0, :], rows[2][:, span(first, count)])

        gather(v_words[0][:], table_window(0), idx[:])
        weight_codes(0, 0, at["codes00"])
        clear_page(2)
        gather(v_words[1][:], table_window(1), idx[:])
        for a in range(1, K_PASSES):
            weight_piece(a, 0, [nc.vector.tensor_copy, nc.scalar.copy])
            weight_codes(a, 0)
        clear_page(3)
        for g, (first, count) in enumerate(GROUPS):
            square_pair(damp1[g][:, 0], roots[:, :, span(first, count)])
        window = table_window(2)
        for u in range(2):
            gather(v_words[2][:, span(HALF * u, HALF)], window, entries(idx, HALF * u, HALF))

        def products(first, count, offset):
            woven = placed([P, PACK * count], BF16, f"woven0_{first}", offset)
            for part in range(count // CHUNK):
                c = first // CHUNK + part
                damped(0, c, damp0[:, :, span(CHUNK * c, CHUNK), :], woven, part)
            return woven

        def codes(first, count, woven):
            u, inside = divmod(first, HALF)
            quantise(h_words[0, u][:, span(inside, count)], h_sc[0][:, span(first, count)], woven[:])

        for u in range(2):
            h_words[0, u] = kept([P, HALF], U32, f"h_words0{u}")
        first_half = products(0, HALF, at["woven"])
        third_quarter = products(HALF, QUARTER, at["woven"] + 8 * KIB)
        codes(0, HALF, first_half)
        weight_piece(0, 1, [nc.scalar.copy])
        weight_codes(0, 1)
        last_quarter = products(HALF + QUARTER, QUARTER, at["w01"])
        codes(HALF, QUARTER, third_quarter)
        weight_piece(1, 1, [nc.scalar.copy])
        weight_codes(1, 1)
        codes(HALF + QUARTER, QUARTER, last_quarter)
        weight_piece(2, 1, [nc.scalar.copy])

        window = shear_window(1, 3)
        for g, (first, count) in enumerate(GROUPS):
            if g == len(GROUPS) - 1:
                weight_codes(2, 1, at["codes21"])
            row = placed([P, count], F32, f"row13_{g}", at[f"row13_{g}"])
            gather(row[:], window, entries(idx, first, count))
            for part in range(0, count, QUARTER):
                cut = span(part, QUARTER)
                squares = placed([P, QUARTER], F32, f"late_squares{first + part}", at["late_squares"] + (0, 0, -KIB // 2, KIB // 2)[(first + part) // QUARTER])[:]
                (square_on_scalar if g == 0 else square_on_gpsimd)(squares, row[:, cut])
                inverse_root(late_roots[g][:, 1, cut], squares)
                square_pair(damp1[g][:, 1, cut, :], late_roots[g][:, :, cut])

        w2_sc = placed([P, N], U8, "w2_sc", at["w2_sc"])
        nc.gpsimd.memset(w2_sc[:].bitcast(I32), 0)
        for q in range(P // QUADRANT):
            nc.sync.dma_start(
                out=w2_sc[QUADRANT * q : QUADRANT * q + 4 * R_PASSES, :].bitcast(I32),
                in_=w2_scales[:, 4 * q : 4 * q + 4, :].bitcast(I32),
            )
        nc.sync.dma_start(idx2[:], offs2)
        w2_w = placed([P, R_PASSES, N], U32, "w2_w", at["w2"])
        nc.sync.dma_start(out=w2_w[:].bitcast(I32), in_=w2_words.rearrange("b p c i -> p b (c i)").bitcast(I32))
        wgo_sb = placed([P, S], F32, "wgo_sb", at["wgo"])
        nc.sync.dma_start(out=wgo_sb[:], in_=wgo)
        for u in range(2):
            src_sb[u] = placed([P, PAGES, HALF], F32, f"src{u}", at[f"src{u}"])
            nc.sync.dma_start(out=src_sb[u][:], in_=src[:, span(HALF * u, HALF)].rearrange("(m p) j -> p m j", p=P))

        quarters = [placed([P, PACK * QUARTER], BF16, f"woven1{g}", at["woven"] + KIB * (4 + 2 * g)) for g in range(2)]
        last_half = placed([P, PACK * HALF], BF16, "woven12", at["damp0"] + 3 * KIB)
        h_words[1, 0] = kept([P, HALF], U32, "h_words10")

        def quarter_codes(g):
            cut = span(QUARTER * g, QUARTER)
            quantise(h_words[1, 0][:, cut], h_sc[1][:, cut], quarters[g][:])

        def product(c):
            g = min(c // 2, 2)
            part = c - GROUPS[g][0] // CHUNK
            damped(1, c, damp1[g][:, :, span(CHUNK * part, CHUNK), :], (quarters + [last_half])[g], part)

        for c in range(CHUNKS):
            product(c)
            if c in (2, 4):
                quarter_codes(c // 2 - 1)

        def result(number, m, first, count, before_scatter=nothing):
            u, inside = divmod(first, HALF)
            y = psum.tile([P, count], F32, name=f"y{number}", offset=BANK * (number % CHUNKS))
            for b in range(R_PASSES):
                nc.tensor.matmul_mx(
                    out=y[:],
                    lhsT=w2_w[:, b, span(P * m, P)].bitcast(E4M3),
                    lhsT_scale=w2_sc[4 * b : P, span(P * m, P)],
                    rhs=h_words[b, u][:, span(inside, count)].bitcast(E4M3),
                    rhs_scale=h_sc[b][:, span(first, count)],
                    start=(b == 0),
                    stop=(b == R_PASSES - 1),
                )
            values = placed([P, count], F32, f"values{number}", at["values"] + 2 * KIB * (number % 3))
            nc.scalar.copy(out=values[:], in_=y[:])
            diff = placed([P, count], F32, f"diff{number}", at["damp0"] + KIB * ((1, 2, 1, 2, 1)[number] if number <= 4 else (8, 2)[number % 2]))
            nc.gpsimd.tensor_tensor(
                out=diff[:], in0=values[:], in1=src_sb[u][:, m, span(inside, count)], op=ALU.subtract
            )
            weighted = placed([P, count], F32, f"weighted{number}", at["weighted"] + 2 * KIB * (number % 3))
            nc.gpsimd.tensor_tensor(out=weighted[:], in0=diff[:], in1=wgo_sb[:, span(first, count)], op=ALU.mult)
            before_scatter()
            nc.vector.tensor_copy(out=pages[m][:].indirect(entries(idx2, first, count)), in_=weighted[:])

        def last_codes():
            h_words[1, 1] = placed([P, HALF], U32, "h_words11", at["damp0"])
            quantise(h_words[1, 1][:], h_sc[1][:, span(HALF, HALF)], last_half[:])

        for g in range(2):
            for m in range(2):
                result(2 * g + m, m, QUARTER * g, QUARTER)
        result(4, 2, 0, HALF, last_codes)
        result(5, 3, 0, HALF)
        for m in range(PAGES):
            result(6 + m, m, HALF, HALF)
            nc.sync.dma_start(out=out[span(P * m, P), :], in_=pages[m][:])
